import numpy as np, ml_dtypes
CORES = [2,3,42,43,82,83,122,123]
N = 8
BF = ml_dtypes.bfloat16
W, L, CAP, EQ, CNT, RO = 4096, 256, 32, 12, 10, 4
TAU = [96, 700, 24, 2496]
WA = np.array([7, 113, 51, 229, 87, 19, 161, 203, 35, 149, 71, 247, 93, 181, 125, 11])
WB = np.array([1, 3, 2, 7, 5, 1, 6, 3, 7, 2, 5, 4, 1, 6, 3, 5])
KP = np.array([3, 18, 45, 71, 102, 125, 150, 187, 208, 233, 260, 291, 318, 345, 382, 407])
KZ = np.array([0, 0, 0, 0, 0, 0, 25, 0, 0, 0, 1, 0, 0, 0, 0, 0])
TOP = 130560
def home(k):
    return (k @ WB) & (N - 1)
def look(k, n):
    u = (k @ WA) & (W - 1)
    return ((u * (2 * n + 1) >> 5)[..., None] + KP * u[..., None]) & (W - 1)
def whole8(x):
    return np.minimum(np.rint(np.asarray(x, np.float32)), TOP).astype(BF).astype(np.float32)
def pool(rng, keys):
    keys = keys[np.any(keys > 0, axis=1)]; z = home(keys); out = []
    for r in range(N):
        a = np.nonzero(z == r)[0]
        if len(a) == 0: a = np.arange(len(keys))
        out.append(keys[np.resize(rng.permutation(a), 4)])
    return np.stack(out)
def bend(rng, k, c, flip):
    n = len(k); i = (np.arange(16) * (2 * rng.integers(0, 8, (n, 1)) + 1) + rng.integers(0, 16, (n, 1))) & 15
    new = 255 - k if flip else (k + rng.integers(1, 256, k.shape)) & 255
    return np.where(i < np.asarray(c)[:, None], new, k)
def cut(rng, a, ln):
    col = np.arange(16)[None, :]; ln = np.asarray(ln)[:, None]
    a = np.where(col == ln, 0, a)
    return np.where((col > ln) & (rng.random((len(a), 1)) < 0.6), 0, a)
def thin(rng, k):
    i = np.where(rng.random(k) < 0.5, 15, rng.integers(0, 16, k))
    x = np.where(rng.random(k) < 0.5, rng.choice(np.array([1, 255]), k), rng.integers(1, 256, k))
    return np.where(np.arange(16)[None, :] == i[:, None], x[:, None], 0)
def nought(cand):
    at = np.nonzero((((cand @ WA) & (W - 1)) == 0) & ((home(cand) & 1) == 1))[0]
    return cand[at[0]] if len(at) else KZ
def keys_plain(rng):
    return rng.integers(0, 256, (512, 16))
def name_plain(rng, shape):
    return rng.integers(1, 256, shape)
def vt_plain(rng, k):
    x = np.exp2(8 + 9 * rng.random((k, 1))) * (0.25 + 0.75 * rng.random((k, 16)))
    x = np.where(rng.random((k, 16)) < 0.15, np.exp2(8 * rng.random((k, 16))) - 1, x)
    return whole8(np.where(rng.random((k, 1)) < 0.25, TOP, x))
def vl_plain(rng, k):
    x = np.exp2(11 + 6 * rng.random((k, 1))) * (0.25 + 0.75 * rng.random((k, 16)))
    return whole8(np.where(rng.random((k, 16)) < 0.1, np.exp2(8 * rng.random((k, 16))) - 1, x))
def make(rng, keys, flip, vt, vl, name, fill, lens):
    P = np.stack([pool(rng, keys(rng)) for g in range(8)]); few = [name(rng, 24) for g in range(8)]
    F = np.zeros((N, 8, W, 16), np.int64); G = np.zeros((N, 8, W, 16), np.int64); V = np.zeros((N, 8, W, 16), np.float32)
    f = np.zeros((N, 8, L, 16), np.int64); v = np.zeros((N, 8, L, 16), np.float32); nm = np.zeros((N, 8, L, 16), np.int64)
    for r in range(N):
        for g in range(8):
            Q = P[g].reshape(-1, 16)
            F[r, g] = bend(rng, P[g, r][rng.integers(0, 4, W)], rng.integers(0, 18 - EQ, W), flip) * (rng.random((W, 1)) < fill[g])
            G[r, g] = bend(rng, Q[rng.integers(0, len(Q), W)], rng.integers(0, 3, W) * (rng.random(W) < 0.2), flip)
            G[r, g] *= (rng.random((W, 1)) >= 0.04)
            V[r, g] = vt(rng, W)
            k = np.where(rng.random((L, 1)) < 0.7, P[g, r][rng.integers(0, 4, L)], Q[rng.integers(0, len(Q), L)])
            f[r, g] = bend(rng, k, rng.integers(0, 3, L) * (rng.random(L) < 0.2), flip) * (rng.random((L, 1)) >= 0.05)
            v[r, g] = vl(rng, L)
            a = np.where(rng.random((L, 16)) < 0.5, few[g][rng.integers(0, 24, (L, 16))], name(rng, (L, 16)))
            nm[r, g] = cut(rng, a, rng.choice(np.array(lens), L))
    return P, F, G, V, f, v, nm
def pack(F, G, V, f, v, nm):
    on = np.any(F > 0, axis=3, keepdims=True); d = {}
    for k, a in (("rf", F), ("rg", np.where(on, G, 0)), ("rv", np.where(on, V, 0)), ("wf", f), ("wv", v), ("nm", nm)):
        a = np.ascontiguousarray(np.swapaxes(a, 2, 3).reshape(N, 128, -1))
        d[k] = a.astype(np.int32) if k == "nm" else a.astype(np.float32).astype(BF)
    return d
def setup_inputs(rng):
    m = make(rng, keys_plain, False, vt_plain, vl_plain, name_plain, rng.uniform(0.4, 0.6, 8), [0, 1, 1, 2, 2, 3, 4, 6, 9, 16])
    return pack(*m[1:])
def setup_inputs_spread(rng):
    def keys(rng): return np.exp2(8 * rng.random((512, 16))).astype(np.int64) - 1
    def vt(rng, k): return whole8(np.exp2(17 * rng.random((k, 1))) * np.exp2(-3 * rng.random((k, 16))) * (rng.random((k, 16)) > 0.0625))
    def vl(rng, k): return whole8(np.exp2(9 + 8 * rng.random((k, 1))) * np.exp2(-3 * rng.random((k, 16))))
    def name(rng, shape): return np.exp2(8 * rng.random(shape)).astype(np.int64)
    m = make(rng, keys, False, vt, vl, name, rng.permutation(np.linspace(0.1, 0.95, 8)), [0, 1, 2, 3, 5, 8, 12, 15, 16])
    return pack(*m[1:])
def setup_inputs_near(rng):
    def keys(rng):
        b = np.repeat(rng.integers(0, 256, (1, 16)), 512, axis=0); return bend(rng, b, rng.integers(0, 19 - EQ, 512), False)
    def vt(rng, k):
        o = np.argsort(rng.random((k, 16)), axis=1); c = CNT - rng.integers(0, 2, (k, 1)); tau = np.array(TAU)[rng.integers(0, RO, (k, 1))]
        low = np.where((o == c) | (rng.random((k, 16)) < 0.5), tau, 0)
        a = whole8(np.where(o < c, TOP * (0.5 + 0.5 * rng.random((k, 16))), low))
        return np.where(rng.random((k, 1)) < 0.3, a, vt_plain(rng, k))
    def vl(rng, k):
        a = whole8(TOP * (0.5 + 0.5 * rng.random((k, 16))))
        return np.where(rng.random((k, 1)) < 0.6, a, vl_plain(rng, k))
    m = make(rng, keys, False, vt, vl, name_plain, rng.uniform(0.3, 0.7, 8), [0, 1, 2, 3, 4, 5, 7, 16])
    return pack(*m[1:])
def setup_inputs_ends(rng):
    def keys(rng): return 255 * rng.integers(0, 2, (512, 16))
    def vt(rng, k):
        a = np.where(rng.random((k, 16)) < 0.75, TOP, 0); z = rng.random((k, 1)); one = np.arange(16)[None, :] == rng.integers(0, 16, (k, 1))
        a = np.where((z >= 0.6) & (z < 0.75) & (a == 0) & (rng.random((k, 16)) < 0.5), 1, a)
        a = np.where(z < 0.6, TOP, a); a = np.where((z >= 0.4) & (z < 0.6) & one, 130048, a)
        return np.where(z > 0.95, 0, a).astype(np.float32)
    def vl(rng, k):
        a = np.where(rng.random((k, 16)) < 0.8, TOP, 0); z = rng.random((k, 1))
        a = np.where((z >= 0.8) & (z < 0.95) & (a == 0), 1, a); a = np.where(z < 0.5, TOP, a)
        return np.where(z > 0.95, 0, a).astype(np.float32)
    def name(rng, shape): return rng.choice(np.array([255] * 8 + [254, 1]), shape)
    P, F, G, V, f, v, nm = make(rng, keys, True, vt, vl, name, rng.uniform(0.4, 0.6, 8), [0, 1, 1, 2, 3, 15, 16, 16])
    col = np.arange(16)
    for g in range(8):
        Q = P[g].reshape(-1, 16); H = look(Q[:, None, :], np.arange(1, 256)[None, :]); at = np.argwhere(H == W - 1)
        odd = np.nonzero(((Q @ WA) & 1) == 1)[0]
        for r in range(N):
            away = odd[(odd >> 2) != r]
            if len(away):
                for lane, ln in ((L - 2, 16), (L // 2, 2), (1, 1)):
                    x = Q[away[rng.integers(0, len(away))]]; n = int(rng.choice(np.array([1, 255]))); h = look(x[None, :], np.array([n]))[0]
                    j = int(rng.integers(0, 16)); a = np.full((16, 16), TOP); a[:, j] = 0; a[15, j] = 1; a[1:15, (j + 1) & 15] = 0
                    F[r, g, h] = x; G[r, g, h] = Q[rng.permutation(len(Q))[:16]]; V[r, g, h] = a
                    f[r, g, lane] = x; v[r, g, lane] = TOP; nm[r, g, lane] = np.where(col == 0, n, np.where(col < ln, 255, 0))
            if len(at) == 0: continue
            i, n, m = at[rng.integers(0, len(at))]; h = H[i, n]
            F[r, g, h] = Q[i]; G[r, g, h] = Q[rng.integers(0, len(Q), 16)]
            a = np.full((16, 16), TOP); a[:m, rng.integers(0, 16)] = 130048; V[r, g, h] = a
            for lane, ln in ((0, 2), (L // 2 + 1, 16), (L - 1, 16)):
                f[r, g, lane] = Q[i]; v[r, g, lane] = TOP; nm[r, g, lane] = np.where(col == 0, n + 1, np.where(col < ln, 255, 0))
    return pack(F, G, V, f, v, nm)
def setup_inputs_corners(rng):
    fill = np.array([1.0, 0.0, 0.0, 0.0, 0.5, 0.5, 0.5, 0.5])
    P, F, G, V, f, v, nm = make(rng, keys_plain, False, vt_plain, vl_plain, name_plain, fill, [0, 1, 1, 2, 3, 15, 16])
    F[:, 0, :, 0] = np.maximum(F[:, 0, :, 0], 1)
    cand = rng.integers(0, 256, (131072, 16)); cand[:, 0] = np.maximum(cand[:, 0], 1)
    kz = nought(cand)
    H = look(cand, np.zeros(len(cand), np.int64)); at = np.argwhere(H == W - 1)
    for r in range(N):
        v[r, 0, ::2] = np.where(rng.random((L // 2, 1)) < 0.5, 0, TOP)
        for g in (1, 2, 3): nm[r, g] = cut(rng, rng.integers(1, 256, (L, 16)), rng.choice(np.array([1, 16]), L))
        f[r, 2] = P[2, (r + 1) % N][rng.integers(0, 4, L)]
        to = np.concatenate([np.full(CAP, (r + 1) % N), np.full(CAP + 1, (r + 2) % N), np.full(CAP - 1, (r + 3) % N), (r + np.arange(4, N)) % N]).astype(np.int64)
        f[r, 3] = 0; f[r, 3, rng.permutation(L)[:len(to)]] = P[3][to, rng.integers(0, 4, len(to))]
        f[r, 4] = 0
        if r % 2:
            for lane in (0, L // 2, L - 1): f[r, 4, lane] = P[4, r, lane % 4]
        f[r, 5] = P[5, r, 0]; nm[r, 5] = 0
        if r == N - 1: f[r, 5, 1::2] = P[5, r, 1]
        f[r, 6, 1::2] = kz; nm[r, 6] = cut(rng, rng.integers(1, 256, (L, 16)), np.where(np.arange(L) % 4 == 3, 16, rng.choice(np.array([1, 2, 16]), L)))
        F[r, 6, 0] = 0 if r % 2 else kz; G[r, 6, 0] = kz; V[r, 6, 0] = TOP; v[r, 6, 3::4] = TOP
        if len(at):
            i = at[rng.integers(0, len(at)), 0]; h = H[i]
            F[r, 7, h] = P[7, r][rng.integers(0, 4, 16)]; F[r, 7, h, 0] = np.maximum(F[r, 7, h, 0], 1); F[r, 7, W - 1] = 0
            for lane in ((L - 1,) if r % 2 else (5, L - 1)): f[r, 7, lane] = cand[i]; nm[r, 7, lane] = 0
    return pack(F, G, V, f, v, nm)
def setup_inputs_thin(rng):
    P, F, G, V, f, v, nm = make(rng, keys_plain, False, vt_plain, vl_plain, name_plain, rng.uniform(0.4, 0.6, 8), [0, 1, 1, 2, 2, 3, 4, 6, 9, 16])
    cand = rng.integers(0, 256, (131072, 16)); cand[:, 0] = np.maximum(cand[:, 0], 1)
    kz = nought(cand); z = int(home(kz))
    for r in range(N):
        f[r, 0] = rng.integers(0, 256, (L, 16)); nm[r, 0, :, 0] *= (rng.random(L) < 0.25 * (r & 1))
        F[r, 1] = thin(rng, W) * (rng.random((W, 1)) < 0.5); G[r, 1] = np.where(rng.random((W, 1)) < 0.5, thin(rng, W), G[r, 1])
        f[r, 1] = thin(rng, L); nm[r, 1, ::2, 0] = 0
        for g in (2, 3):
            G[r, g] *= (rng.random((W, 1)) >= 0.5); V[r, g] = np.where(rng.random((W, 1)) < 0.5, TOP, V[r, g])
            v[r, g] = np.where(rng.random((L, 1)) < 0.5, TOP, v[r, g])
            nm[r, g] = cut(rng, rng.integers(1, 256, (L, 16)), rng.choice(np.array([2, 3, 4, 16]), L))
        keep = rng.permutation(L)[:CAP // 2]; m = np.zeros((L, 1), np.int64); m[keep] = 1
        f[r, 6] *= m; nm[r, 6, :, 0] = np.maximum(nm[r, 6, :, 0], 1)
        F[r, 6, 0] = 0 if r == z else kz; G[r, 6, 0] = P[6, (r + 1) % N, 0]; V[r, 6, 0] = TOP
        if r == 0: f[r, 6] = 0
        elif r != z:
            f[r, 6, keep[:3]] = kz; v[r, 6, keep[:3]] = TOP; nm[r, 6, keep[:3]] = cut(rng, rng.integers(1, 256, (3, 16)), np.ones(3, np.int64))
    F[0, 2, 0] = np.where(rng.permutation(16) < 16 - EQ, rng.integers(1, 256, 16), 0); F[0, 3, 0] = thin(rng, 1)[0]
    for g in (2, 3): G[0, g, 0] = P[g, N - 1, 0]; V[0, g, 0] = TOP
    return pack(F, G, V, f, v, nm)
def check_inputs(d):
    bad = []
    for k, hi in (("rf", 255), ("rg", 255), ("rv", TOP), ("wf", 255), ("wv", TOP), ("nm", 255)):
        a = np.asarray(d[k]).astype(np.float64)
        if not np.all((a >= 0) & (a <= hi) & (a == np.floor(a))): bad.append("range of " + k)
    on = np.any(np.asarray(d["rf"]).astype(np.float32).reshape(N, 8, 16, W) != 0, axis=2, keepdims=True)
    for k in ("rg", "rv"):
        if np.any((np.asarray(d[k]).astype(np.float32).reshape(N, 8, 16, W) != 0) & ~on): bad.append("empty places of " + k)
    return bad
def reference(rf, rg, rv, wf, wv, nm):
    F, G, V = [a.astype(np.float32).astype(np.int32).reshape(N, 8, 16, W) for a in (rf, rg, rv)]
    f, v = [a.astype(np.float32).astype(np.int64).reshape(N, 8, 16, L) for a in (wf, wv)]
    na = nm.astype(np.int64).reshape(N, 8, 16, L); f0 = f.copy(); n0 = na[:, :, 0].copy()
    for t in range(RO):
        there = np.any(f0 != 0, axis=2)
        done = there & (na[:, :, 0] == 0); wait = there & (na[:, :, 0] != 0)
        q = np.where(done[:, :, None], f0, f); n = np.where(done, n0, na[:, :, 0])
        u = np.sum(WA[:, None] * q, axis=2) & (W - 1)
        h = ((u * (2 * n + 1) >> 5)[:, :, None] + KP[:, None] * u[:, :, None]) & (W - 1)
        ix = h.reshape(N, 8, 1, 16 * L)
        Fh = np.take_along_axis(F, ix, 3).reshape(N, 8, 16, 16, L)
        lo = np.minimum(np.take_along_axis(V, ix, 3).reshape(N, 8, 16, 16, L), v[:, :, :, None, :].astype(np.int32))
        same = np.sum(Fh == f[:, :, :, None, :].astype(np.int32), axis=2); over = np.sum(lo > TAU[t], axis=2)
        ok = (same >= EQ) & (over >= CNT) & wait[:, :, None]
        best = np.argmax(np.where(ok, np.sum(lo, axis=2), -1), axis=2)
        hit = np.any(ok, axis=2)[:, :, None]; bh = np.take_along_axis(h, best[:, :, None], 2)
        Gb = np.take_along_axis(G, bh, 3); Vb = np.take_along_axis(V, bh, 3)
        free = np.all(Fh == 0, axis=2); can = np.any(free, axis=2) & done
        place = np.take_along_axis(h, np.argmax(free, axis=2)[:, :, None], 2)[:, :, 0]
        for r in range(N):
            for g in range(8):
                lanes = np.nonzero(can[r, g])[0]; pl, first = np.unique(place[r, g, lanes], return_index=True); w = lanes[first]
                F[r, g][:, pl] = f0[r, g][:, w]; G[r, g][:, pl] = f[r, g][:, w]; V[r, g][:, pl] = v[r, g][:, w]
        f = np.where(hit, Gb, f); v = np.where(hit, np.minimum(v, Vb), v)
        na = np.where(hit, np.concatenate([na[:, :, 1:], np.zeros((N, 8, 1, L), np.int64)], axis=2), na)
        if t < RO - 1:
            goal = np.sum(WB[:, None] * np.where(na[:, :, :1] == 0, f0, f), axis=2) & (N - 1)
            S = np.concatenate([f0, f, v, na, n0[:, :, None]], axis=2); S2 = np.zeros_like(S)
            for q in range(N):
                for d in range(N):
                    go = (wait[q] & (goal[q] == d)).astype(np.int64); before = np.add.accumulate(go, axis=1) - go
                    gi, li = np.nonzero((go == 1) & (before < CAP))
                    S2[d, gi, :, q * CAP + before[gi, li]] = S[q, gi, :, li]
            f0, f, v, na, n0 = S2[:, :, :16], S2[:, :, 16:32], S2[:, :, 32:48], S2[:, :, 48:64], S2[:, :, 64]
    yf = np.where(wait[:, :, None], f, 0); yv = np.where(wait[:, :, None], v, 0)
    z = [np.sum(a.reshape(N, 128, 32, W // 32), axis=2).astype(np.float32) for a in (F, G, V)]
    return {"zf": z[0], "zg": z[1], "zv": z[2], "yf": yf.reshape(N, 128, L).astype(np.float32).astype(BF), "yv": yv.reshape(N, 128, L).astype(np.float32).astype(BF)}

@@ -1,0 +1,543 @@
+from concourse.bass import DstId, RemoteDMATransfer
+from concourse.mybir import AluOpType as OP, AxisListType as AX, ActivationFunctionType as AF
+
+N = 8
+RO = 4
+TAU = [96, 700, 24, 2496]
+WA = [7, 113, 51, 229, 87, 19, 161, 203, 35, 149, 71, 247, 93, 181, 125, 11]
+WB = [1, 3, 2, 7, 5, 1, 6, 3, 7, 2, 5, 4, 1, 6, 3, 5]
+KP = [3, 18, 45, 71, 102, 125, 150, 187, 208, 233, 260, 291, 318, 345, 382, 407]
+TOP = 130560
+BIG = float(2 ** 38)
+T0 = -float(2 ** 36)
+XO, YO, NO = 4352, 4608, 4864
+
+B, F, H, I, U = "bfloat16", "float32", "float16", "int32", "uint16"
+SCRATCH = {}
+
+
+def _decl(dt, where, **kw):
+    for k, n in kw.items():
+        SCRATCH[k] = (where, [128, n], dt)
+
+
+_decl(B, "sbuf", FW=4352, VW=4608, GW=5632, VG=4096, LO=4096, EQ=4096, OV=4096, X0=256, V0=256, N0=256, NB=256,
+      AL=256, BB=256, land1=1024, land2=1024, land3=1024, send1=1024, send2=1024, send3=1024,
+      inv1=2304, inv2=2304, inv3=2304, NX=272, NY=272, NV=272, NN=272, PEN=384, FL=256, VQ=256, FQ=1024,
+      EE=1024, OHD=256, YF=256, YV=256, ZR=256, SG=256,
+      ID=128, NI=128, BLK=128, BW=128, RN=128, RB=128, S1=128, S2=128, P0=128, W1=144, W16=144, WZ=144,
+      TRI=2048, AB8=16, NW=32, CT=256, CK=256, NEG=128, ONE=128, JN=256, DW=256, DF=256)
+_decl(H, "sbuf", UB=256, XP=256, WR=144, BR=2048, D1=256, DK=256, ON16=128, PN=256, PL16=16)
+_decl(F, "sbuf", TQ=128, QQ=144, QG=128, QL=128, TT=128, COL=48, E16=16, LT=16, TAB=16, DQ=256, KS=256, KT=256,
+      HT=256, BT=256, SS=256, SM=256, ST=192, PD=192, OO=128, LT4=64, LT2=32, JW=64, PB=128, ZF=128, ZG=128, ZV=128)
+_decl(I, "sbuf", NI32=256, SI=128, UI=256, WI=128, H0=256, HI=256, RI=256, CI=16)
+_decl(U, "sbuf", HU=256, OU=64, PU=16, IU=16, CU=16, REP=16, DIV=16, TRN=16, END=16)
+_decl(F, "psum", B0=1024, B1=512, B2=512, B3=512, B4=512, B5=512, B6=512)
+
+SEMAPHORES = ["sv", "sa", "sp", "sg", "d0", "d1", "d2", "d3", "d4", "d5", "o0", "o1", "o2", "o3", "o4",
+              "arr1", "arr2", "arr3", "sent", "fq"]
+
+
+def plan(src, cores, topo):
+    near = [d for d in range(N) if cores[d] != src and topo.chip(cores[d]) == topo.chip(src)]
+    me = cores.index(src)
+    far = [(me + k) % N for k in range(1, N) if (me + k) % N not in near]
+    off = topo.engines(src, cores[far[0]])
+    on = [e for e in topo.engines(src, cores[near[0]]) if e not in off]
+    h, q = len(off) // 2, len(off) // 4
+    one = [(far[0], off[:h]), (far[1], off[h:h + q]), (far[2], off[h + q:]), (near[0], on)]
+    two = [(far[3], off[h:]), (far[4], off[:q]), (far[5], off[q:h])]
+    return [one, two]
+
+
+def rank_program(g, core, T, topo):
+    me = T.rank_of(core)
+    if me is None:
+        return
+    cores = list(T.cores)
+    Q = {"v": g.vector, "a": g.scalar, "p": g.tensor, "g": g, "s": g.sync}
+    cnt = {"v": 0, "a": 0, "p": 0, "g": 0}
+    seen = {e: {} for e in Q}
+    wr, rd, knew = {}, {}, {}
+
+    def need(e, r, w):
+        deps = []
+        for k in r:
+            deps += wr.get(k, [])
+            if k[0] == "B" and len(k) == 2 and k[1] in "0123456":
+                deps += [t for t in rd.get(k, []) if t[2] != e]
+        for k in w:
+            deps += wr.get(k, []) + rd.get(k, [])
+        top = {}
+        for s, val, who in deps:
+            if who == "p" and e == "p":
+                continue
+            top[s] = max(top.get(s, 0), val)
+        for s, val in top.items():
+            if any(knew.get((s2, v2), {}).get(s, 0) >= val for s2, v2 in top.items() if s2 != s):
+                continue
+            if seen[e].get(s, 0) < val:
+                Q[e].wait_ge(T.sem[s], val)
+                seen[e][s] = val
+        for tok in top.items():
+            for s, val in knew.get(tok, {}).items():
+                seen[e][s] = max(seen[e].get(s, 0), val)
+
+    def note(tok, r, w, more=False, e=None):
+        if e:
+            knew[tok[0:2]] = dict(seen[e])
+        for k in r:
+            rd.setdefault(k, []).append(tok)
+        for k in w:
+            wr[k] = (wr.get(k, []) if more else []) + [tok]
+            rd[k] = []
+
+    def op(e, fn, r, w):
+        r, w = r.split(), w.split()
+        need(e, r, w)
+        cnt[e] += 1
+        fn().then_inc(T.sem["s" + e], 1)
+        note(("s" + e, cnt[e], e), r, w, False, e)
+
+    def dma(e, sem, out, in_, r, w):
+        r, w = r.split(), w.split()
+        need(e, r, w)
+        Q[e].dma_start(out, in_).then_inc(T.sem[sem], 16)
+        note((sem, 16, "d"), r, w)
+
+    def ts(out, in0, s1, s2, o0, o1, r, w):
+        if o1 is None:
+            op("v", lambda: g.vector.tensor_scalar(out, in0, s1, None, o0), r, w)
+        else:
+            op("v", lambda: g.vector.tensor_scalar(out, in0, s1, s2, o0, o1), r, w)
+
+    def tt(out, a, b, o, r, w):
+        op("v", lambda: g.vector.tensor_tensor(out, a, b, o), r, w)
+
+    def cp(out, a, r, w):
+        op("v", lambda: g.vector.tensor_copy(out, a), r, w)
+
+    def ms(out, c, w):
+        op("v", lambda: g.vector.memset(out, c), "", w)
+
+    def scan(out, a, b, ini, o0, o1, r, w):
+        op("v", lambda: g.vector.tensor_tensor_scan(out, a, b, ini, o0, o1), r, w)
+
+    def act(out, a, r, w, f=AF.Identity, bias=0.0, scale=1.0):
+        op("a", lambda: g.scalar.activation(out, a, f, bias=bias, scale=scale), r, w)
+
+    def mm(out, l, rhs, st, sp, r, w):
+        op("p", lambda: g.tensor.matmul(out, l, rhs, st, sp), r, w)
+
+    def iota(out, pat, base, ch, w, flt=True):
+        if flt:
+            op("g", lambda: g.iota(out, pat, base, ch, allow_small_or_imprecise_dtypes=True), "", w)
+        else:
+            op("g", lambda: g.iota(out, pat, base, ch), "", w)
+
+    def fill(name, a, b, val, w):
+        iota(T[name][:, a:b], [[0, b - a]], val, 0, w)
+
+    def to_w(out, wname, src, r, w, first=True, last=True):
+        for k in range(16):
+            mm(out, T[wname][:, 15 - k:143 - k], src(k), first and k == 0, last and k == 15, r + " " + wname, w)
+
+    def lane(t, o, a, b, s=1):
+        if t == 0:
+            return T[("X0", "X0", "V0", "N0")[o]][:, a:b:s]
+        return T["land%d" % t][:, 4 * a + o:4 * b:4 * s]
+
+    def lkey(t, o):
+        return ("X0", "X0", "V0", "N0")[o] if t == 0 else "land%d" % t
+
+    C = {}
+
+    def col(n):
+        if n not in C:
+            C[n] = len(C)
+        return T.COL[:, C[n]:C[n] + 1]
+
+    def E(k):
+        return T.E16[:, k:k + 1]
+
+    def names(p, n):
+        return " ".join(p + str(k) for k in range(n))
+
+    dma("s", "d0", T.X0[:], T.wf[:], "", "X0")
+    dma("a", "d1", T.NI32[:], T.nm[:], "", "NI32")
+    dma("s", "d2", T.V0[:], T.wv[:], "", "V0")
+    dma("s", "d4", T.FW[:, 0:4096], T.rf[:], "", "FW")
+    dma("s", "d3", T.VW[:, 0:4096], T.rv[:], "", "VW")
+
+    iota(T.CI[:, 0:1], [[0, 1]], 0, 1, "CI0", False)
+    iota(T.QQ[:], [[1, 144]], 0, 0, "QQ")
+    iota(T.QG[:], [[1, 8], [0, 16]], 0, 0, "QG")
+    iota(T.TQ[:], [[1, 128]], 0, -1, "TQ")
+    iota(T.DQ[0:16, :], [[0, 16], [1, 16]], 0, -1, "DQ")
+    iota(T.CK[:], [[-4096, 16], [0, 16]], 15 * 4096, 0, "CK")
+    fill("NEG", 0, 128, -2 ** 17, "NEG")
+    fill("ONE", 0, 128, 4096, "ONE")
+    iota(T.QL[:], [[1, 8], [100, 2], [0, 8]], 0, 0, "QL")
+    fill("ST", 0, 192, 0, "ST")
+    fill("ST", 112, 128, 1, "ST")
+    fill("ST", 176, 192, -1, "ST")
+    iota(T.JN[:], [[1, 256]], 0, 0, "JN")
+    fill("SG", 0, 256, 0, "SG")
+    fill("ZR", 0, 256, 0, "ZR")
+    fill("VW", 4096, 4352, 0, "VWd")
+    fill("VW", 4352, 4608, TOP, "VWt")
+    fill("GW", 4096, 4352, 0, "GWd")
+    fill("FW", 4096, 4352, 0, "FWd")
+    for n in ("NX", "NY", "NV", "NN"):
+        fill(n, 256, 272, 0, n + "z")
+    fill("inv1", 256, 512, 256, "inv1")
+    fill("EE", 0, 768, 0, names("EE", 16))
+    fill("inv2", 256, 512, 256, "inv2")
+    fill("inv3", 256, 512, 256, "inv3")
+
+    for k in range(16):
+        ms(T.TAB[:, k:k + 1], float(8 * WA[k] + WB[k]), "TAB%d" % k)
+    ts(T.CI[:, 1:2], T.CI[:, 0:1], 15, None, OP.bitwise_and, None, "CI0", "CI1")
+    ts(T.CI[:, 2:3], T.CI[:, 0:1], 4, None, OP.arith_shift_right, None, "CI0", "CI2")
+    col("R"), col("G")
+    cp(T.COL[:, 0:2], T.CI[:, 1:3], "CI1 CI2", "R G")
+    ts(T.E16[:], T.QQ[:, 0:16], col("R"), None, OP.is_equal, None, "QQ R", "E16")
+    ts(T.BLK[:], T.QG[:], col("G"), None, OP.is_equal, None, "QG G", "BLK")
+    tt(T.SM[:, 0:16], T.TAB[:], T.E16[:], OP.mult, "E16 " + names("TAB", 16), "SMa")
+    tt(col("e23"), E(2), E(3), OP.add, "E16", "e23")
+    op("v", lambda: g.vector.tensor_reduce(col("AB"), T.SM[:, 0:16], AX.X, OP.add), "SMa", "AB")
+    ts(col("lo"), col("R"), 1.0, 3.0, OP.min, OP.mult, "R", "lo")
+    cp(T.CI[:, 3:4], col("AB"), "AB", "CI3")
+    ts(col("lt4"), col("R"), 4.0, None, OP.is_lt, None, "R", "lt4")
+    ts(T.CI[:, 4:5], T.CI[:, 3:4], 3, None, OP.arith_shift_right, None, "CI3", "CI4")
+    ts(T.TT[:], T.TQ[:], 3.0, None, OP.is_le, None, "TQ", "TT")
+    cp(col("A"), T.CI[:, 4:5], "CI4", "A")
+    ts(T.PB[:], T.TQ[:], col("lo"), col("lt4"), OP.is_ge, OP.mult, "TQ lo lt4", "PB")
+    ts(T.D1[0:16, :], T.DQ[0:16, :], 0.0, None, OP.is_equal, None, "DQ", "D1")
+    tt(T.P0[:], T.TT[:], T.PB[:], OP.mult, "TT PB", "P0")
+    cp(T.NB[:], T.NI32[:], "NI32", "NB")
+    act(col("g15"), col("G"), "G", "g15", scale=16.0, bias=15.0)
+    act(col("c1"), col("e23"), "e23", "c1", scale=-254.0, bias=255.0)
+    act(col("sg"), E(3), "E16", "sg", scale=-2.0, bias=1.0)
+    act(col("n0"), E(0), "E16 e23", "n0", scale=2.0, bias=col("e23"))
+    act(T.NW[:, 8:16], T.BLK[:, 0:128:16], "BLK E16", "NW1", scale=E(2))
+    act(T.NW[:, 16:24], T.BLK[:, 0:128:16], "BLK E16", "NW2", scale=E(3))
+    act(T.NW[:, 0:8], T.BLK[:, 0:128:16], "BLK n0", "NW0", scale=col("n0"))
+    act(T.AB8[:, 0:8], T.BLK[:, 0:128:16], "BLK A", "AB8", scale=col("A"))
+    act(T.BW[:], T.BLK[:], "BLK E16", "BW", scale=E(2))
+    act(T.ON16[0:16, :], T.TQ[0:16, :], "TQ", "ON16", scale=0.0, bias=2048.0)
+    for m in range(16):
+        act(T.DK[0:16, 16 * m:16 * m + 16], T.D1[0:16, 0:16], "D1", "DK%d" % m, scale=float(KP[m]))
+    dk = names("DK", 16)
+    mm(T.B1[:, 0:256], T.BLK[:], T.X0[:], True, True, "BLK X0", "B1")
+    mm(T.B2[:, 0:256], T.P0[:], T.NB[:], True, True, "P0 NB", "B2")
+    ts(T.B1[:, 256:512], T.B1[:, 0:256], 0.0, col("sg"), OP.is_gt, OP.mult, "B1 sg", "B1")
+    ts(T.BB[:], T.B2[:, 0:256], col("c1"), E(3), OP.min, OP.subtract, "B2 c1 E16", "BB")
+    tt(T.N0[:], T.B1[:, 256:512], T.BB[:], OP.mult, "B1 BB", "N0")
+    ts(T.ID[:], T.TQ[:], 0.0, None, OP.is_equal, None, "TQ", "ID")
+    ts(col("lt8"), col("R"), 8.0, None, OP.is_lt, None, "R", "lt8")
+    ts(T.W1[:], T.QQ[:], col("g15"), None, OP.is_equal, None, "QQ g15", "W1")
+    act(col("da"), E(4), "E16", "da", scale=-4.0)
+    act(col("d2"), E(1), "E16", "d2", scale=-1.0, bias=E(2))
+    act(col("db"), E(5), "E16 da", "db", scale=-1.0, bias=col("da"))
+    act(col("r8"), col("R"), "R", "r8", scale=-0.125, bias=0.0625)
+    act(col("d1"), E(6), "E16 db", "d1", scale=-1.0, bias=col("db"))
+    ts(T.S2[:], T.TQ[:], col("d2"), col("R"), OP.is_equal, OP.min, "TQ d2 R", "S2")
+    ts(T.S1[:], T.TQ[:], col("d1"), col("R"), OP.is_equal, OP.min, "TQ d1 R", "S1")
+    for k, (a, b) in enumerate(((64.0, 72.0), (60.0, 104.0))):
+        d = (T.DW, T.DF)[k]
+        act(d[0:16, 0:128], T.D1[0:16, 0:128], "D1", "DW%da" % k, scale=a)
+        act(d[0:16, 128:256], T.D1[0:16, 0:128], "D1", "DW%db" % k, scale=b)
+
+    def late_constants():
+        ts(T.LT[:], T.QQ[:, 0:16], col("R"), 8192.0, OP.is_gt, OP.mult, "QQ R", "LT")
+        ts(T.REP[:], T.QQ[:, 0:16], 0.0, col("R"), OP.mult, OP.add, "QQ R", "REP")
+        cp(T.DIV[:], T.QQ[:, 0:16], "QQ", "DIV")
+        ts(T.TRN[:], T.QQ[:, 0:16], col("r16"), None, OP.add, None, "QQ r16", "TRN")
+        ts(T.END[:], T.REP[:], 16.0, 15.0, OP.mult, OP.add, "REP", "END")
+        ts(T.RB[:], T.QL[:], col("G"), col("b8"), OP.is_equal, OP.mult, "QL G b8", "RB")
+        ms(T.SG[:, 0:256:16], -float(2 ** 60), "SG")
+
+    def early_constants():
+        act(col("wz"), E(2), "E16", "wz", scale=-256.0, bias=E(4))
+        act(col("wr"), col("lt8"), "E16 lt8", "wr", scale=8.0, bias=E(8))
+        act(col("rb"), col("lt8"), "lt8 r8", "rb", scale=col("r8"))
+        act(col("i0"), col("lt8"), "lt8", "i0", scale=256.0625, bias=-257.0)
+        act(col("nA"), col("A"), "A", "nA", scale=-1.0)
+        act(T.JW[:, 48:64], T.QQ[:, 0:16], "QQ R", "JW", scale=16.0, bias=col("R"))
+        act(col("r16"), col("R"), "R", "r16", scale=16.0)
+        act(col("ini"), col("rb"), "i0 rb", "ini", scale=-1.0, bias=col("i0"))
+        act(col("b8"), col("AB"), "AB nA", "b8", scale=0.125, bias=col("nA"))
+        act(T.W16[:], T.W1[:], "W1", "W16", scale=65536.0)
+        act(T.WZ[:], T.W1[:], "W1 wz", "WZ", scale=col("wz"))
+        act(T.NI[:], T.ID[:], "ID", "NI", scale=-1.0)
+        J = T.JW[:, 48:64]
+        for a, sc, bi in ((32, 1.0, YO), (48, 3.0, NO + 1), (80, 1.0, YO), (96, -1.0, -YO), (128, 1.0, XO), (144, 1.0, XO)):
+            act(T.ST[:, a:a + 16], J, "JW ST", "ST%d" % a, scale=sc, bias=float(bi))
+
+    def tail_constants():
+        J = T.JW[:, 48:64]
+        act(T.RN[:], T.BW[:], "BW", "RN", scale=-0.0625)
+        act(T.CT[:], T.JN[:], "JN rb", "CT", scale=0.0, bias=col("rb"))
+        act(T.WR[:], T.W1[:], "W1 wr", "WR", scale=col("wr"))
+        for k in range(3):
+            act(T.JW[:, 16 * k:16 * k + 16], J, "JW", "DJ%d" % k, bias=4096.0)
+        for k in range(12):
+            act(T.BR[:, 128 * k:128 * k + 128], T.BLK[:], "BLK E16", "BR%d" % k, scale=E(k))
+
+    def tail_constants2():
+        for k in range(12, 16):
+            act(T.BR[:, 128 * k:128 * k + 128], T.BLK[:], "BLK E16", "BR%d" % k, scale=E(k))
+        for k in range(16):
+            act(T.TRI[:, 128 * k:128 * k + 128], T.W1[:, 15 - k:143 - k], "W1 LT", "TRI%d" % k, scale=T.LT[:, k:k + 1])
+
+    st = "ST ST32 ST48 ST80 ST96 ST128 ST144"
+    XJ, DJ = T.ST[:, 128:144], T.JW[:, 0:16]
+    calls = plan(core, cores, topo)
+    comes = sum(len(es) for q in range(N) if q != me for c in plan(cores[q], cores, topo) for d, es in c if d == me)
+    where = {"EQ": ((T.B3, "B3", 0), (T.B4, "B4", 0)), "OV": ((T.B3, "B3", 128), (T.B5, "B5", 0)),
+             "LO": ((T.B1, "B1", 0), (T.B2, "B2", 0))}
+
+    def sm(k):
+        return T.SM[:, 16 * k:16 * k + 16]
+
+    for t in range(RO):
+        last = t == RO - 1
+        kx, ky, kv, kn = [lkey(t, o) for o in range(4)]
+        NM = lane(t, 3, 0, 256)
+
+        def versions():
+            mm(T.B2[:, 0:256], T.S1[:], NM, True, True, kn + " S1", "B2")
+            mm(T.B2[:, 256:512], T.S2[:], NM, True, True, kn + " S2", "B2")
+            act(T.GW[:, NO + 1:NO + 768:3], T.B2[:, 0:256], "B2", "NMW1")
+            act(T.GW[:, NO + 2:NO + 768:3], T.B2[:, 256:512], "B2", "NMW2")
+        for k in range(16):
+            mm(T.B3[0:16, k:128:16], lane(t, 0, k, 256, 16), T.AB8[:, 0:8], True, True, kx + " AB8", "B3")
+        for k in range(16):
+            mm(T.B3[0:16, 128 + k:512:16], lane(t, 3, k, 256, 16), T.NW[:, 0:24], True, True, kn + " NW0 NW1 NW2", "B3")
+        mm(T.B5[:, 0:256], T.BW[:], NM, True, True, kn + " BW", "B5")
+        mm(T.B4[:, 0:256], T.ON16[0:16, :], T.DK[0:16, :], True, False, "ON16 " + dk, "B4")
+        mm(T.B4[:, 0:256], T.ON16[0:16, :], T.D1[0:16, :], False, False, "ON16 D1", "B4")
+        if not last:
+            act(T.GW[:, YO:YO + 256], lane(t, 1, 0, 256), ky, "GY")
+            act(T.GW[:, NO:NO + 768:3], NM, kn, "NMW0")
+            versions()
+        cp(T.SI[0:16, :], T.B3[0:16, 0:128], "B3", "SI")
+        ts(T.UI[0:16, 0:128], T.SI[0:16, :], 4095, None, OP.bitwise_and, None, "SI", "UI0")
+        tt(T.WI[0:16, :], T.UI[0:16, 0:128], T.B3[0:16, 128:256], OP.mult, "UI0 B3", "WI")
+        ts(T.UI[0:16, 128:256], T.WI[0:16, :], 5, 4095, OP.arith_shift_right, OP.bitwise_and, "WI", "UI1")
+        ts(T.UB[0:16, :], T.UI[0:16, :], 2048.0, None, OP.subtract, None, "UI0 UI1", "UB")
+        mm(T.B4[:, 0:256], T.UB[0:16, 0:128], T.DK[0:16, :], False, False, "UB " + dk, "B4")
+        mm(T.B4[:, 0:256], T.UB[0:16, 128:256], T.D1[0:16, :], False, True, "UB D1", "B4")
+        for k in range(4):
+            mm(T.B0[:, 256 * k:256 * k + 256], T.ID[:], lane(t, 2, 0, 256), True, True, kv + " ID", "B0")
+        act(T.FL[0:16, :], T.B3[0:16, 256:512], "B3", "FL")
+        if t == 0:
+            early_constants()
+        tt(T.GW[:, XO:XO + 256], lane(t, 0, 0, 256), T.B5[:, 0:256], OP.mult, kx + " B5", "GX")
+        need("s", ["GX"], ["FQ"])
+        for k in range(4):
+            g.sync.dma_start(T.FQ[:, 256 * k:256 * k + 256], T.GW[:, XO:XO + 256]).then_inc(T.sem.fq, 16)
+        note(("fq", 64 * (t + 1), "d"), ["GX"], ["FQ"])
+        if t == 0:
+            dma("s", "d5", T.GW[:, 0:4096], T.rg[:], "", "GW")
+        cp(T.H0[:], T.B4[:, 0:256], "B4", "H0")
+        ts(T.HI[:], T.H0[:], 4095, None, OP.bitwise_and, None, "H0", "HI")
+        cp(T.HU[:], T.HI[:], "HI", "HU")
+        if last:
+            tt(T.VQ[:], lane(t, 2, 0, 256), T.B5[:, 0:256], OP.mult, kv + " B5", "VQ")
+        if t == 0:
+            late_constants()
+        for k, (a, b) in enumerate(((0, 0), (128, 1))):
+            fl, dw, r = T.FL[0:16, a:a + 128], (T.DW, T.DF)[b], "FL DW%da DW%db" % (b, b)
+            mm(T.B3[:, 0:256], fl, dw[0:16, :], k == 0, False, r, "B3")
+            mm(T.B4[:, 0:128], fl, dw[0:16, 0:128], k == 0, False, r, "B4")
+            mm(T.B5[:, 0:128], fl, dw[0:16, 128:256], k == 0, False, r, "B5")
+        for h in range(2):
+            bk, bn, c = where["LO"][h]
+            mm(bk[:, 0:128], T.ID[:], T.CK[:, 128 * h:128 * h + 128], True, False, "ID CK", bn)
+            mm(bk[:, 0:128], T.NEG[:], T.ONE[:], False, False, "NEG ONE", bn)
+        if not last:
+            to_w(T.B6[:, 0:16], "WZ", lambda k: lane(t, 3, k, 256, 16), kn, "B6")
+
+        def gv(k):
+            act(T.VG[:, 1024 * k:1024 * k + 1024], T.VW[:, 0:4096].indirect(T.HU[:, 64 * k:64 * k + 64]),
+                "VW HU", "VG%d" % k)
+
+        def sums(k, name, wname, close):
+            bk, bn, c = where[name][k // 2]
+            c += 64 * (k % 2)
+            to_w(bk[:, c:c + 64], wname, lambda r: T[name][:, 1024 * k + r:1024 * k + 1024:16],
+                 " ".join("%s%d%s" % (name, k, s) for s in "abcd"), bn, False, close)
+
+        def eq(k):
+            if k == 0 or (k == 1 and t == 0):
+                for m in range(4 * k, 4 * k + 4):
+                    tt(T.EQ[:, 256 * m:256 * m + 256], T.FW[:, 0:4096].indirect(T.HU[:, 16 * m:16 * m + 16]),
+                       T.GW[:, XO:XO + 256], OP.is_equal, "FW HU GX", "EQ%d%s" % (k, "abcd"[m % 4]))
+            else:
+                tt(T.EQ[:, 1024 * k:1024 * k + 1024], T.FW[:, 0:4096].indirect(T.HU[:, 64 * k:64 * k + 64]),
+                   T.FQ[:], OP.is_equal, "FW HU FQ", "EQ%da" % k)
+
+        def mn(k):
+            a = 1024 * k
+            tt(T.LO[:, a:a + 1024], T.VG[:, a:a + 1024], T.B0[:], OP.min, "VG%d B0" % k, "LO%da" % k)
+            sums(k, "LO", "W16", False)
+
+        def sg(k):
+            act(T.OV[:, 1024 * k:1024 * k + 1024], T.LO[:, 1024 * k:1024 * k + 1024], "LO%da" % k,
+                "OV%da" % k, AF.Sign, bias=-TAU[t] - 0.5)
+
+        gv(0); gv(1); gv(2)
+        eq(0); sums(0, "EQ", "W1", False)
+        if t == 0:
+            eq(1); sums(1, "EQ", "W1", False); mn(0); sg(0); gv(3)
+        else:
+            mn(0); sg(0); gv(3); eq(1); sums(1, "EQ", "W1", False)
+        mn(1); sums(0, "OV", "W1", False); sg(1)
+        eq(2); sums(2, "EQ", "W1", False); mn(2); sums(1, "OV", "W1", True); sg(2)
+        mn(3); sums(2, "OV", "W1", False)
+        if not last:
+            ts(sm(0), T.B6[:, 0:16], -256.0, None, OP.is_equal, None, "B6", "z1")
+            tt(T.PD[:, 128:192], sm(0).indirect(T.REP[:, 0:4]), T.ST[:, 64:128], OP.mult, "z1 REP " + st, "zp")
+        sg(3); sums(3, "OV", "W1", True)
+        act(T.PEN[:, 0:256], T.B3[:, 0:256], "B3", "PENa", AF.Relu, bias=76.0 * BIG, scale=-BIG)
+        act(T.PEN[:, 256:384], T.B5[:, 0:128], "B5", "PENb", AF.Relu, bias=76.0 * BIG, scale=-BIG)
+        eq(3)
+        for i in range(2):
+            mm(T.B1[:, 0:128], T.NI[:], T.PEN[:, 128 * i:128 * i + 128], False, i == 1, "NI PENa", "B1")
+        act(T.KS[:, 0:128], T.B1[:, 0:128], "B1", "KSa")
+        sums(3, "EQ", "W1", True)
+        mm(T.B2[:, 0:128], T.NI[:], T.PEN[:, 256:384], False, True, "NI PENb", "B2")
+        if t == 0:
+            tail_constants()
+        cp(T.HT[:], T.HI[:].indirect(T.TRN[:]), "HI TRN", "HT")
+        if not last:
+            tt(T.PD[:, 0:64], T.PD[:, 128:192], T.ST[:, 0:64], OP.add, "zp " + st, "PP")
+            tt(T.PD[:, 64:128], T.ST[:, 128:192], T.PD[:, 128:192], OP.subtract, "zp " + st, "DD")
+        ts(T.PB[:], T.B4[:, 0:128], 76.0, -BIG, OP.is_lt, OP.mult, "B4", "PB")
+        tt(T.KS[:, 128:256], T.B2[:, 0:128], T.PB[:], OP.add, "B2 PB", "KSb")
+        if not last:
+            mm(T.B4[:, 0:256], T.ID[:], T.CT[:], True, False, "ID CT", "B4")
+            mm(T.B4[:, 0:256], T.RN[:], NM, False, False, kn + " RN", "B4")
+        cp(T.KT[:], T.KS[:].indirect(T.TRN[:]), "KSa KSb TRN", "KT")
+        scan(T.B3[:, 0:256], T.SG[:], T.KT[:], 0.0, OP.add, OP.max, "SG KT", "B3")
+        tt(T.B5[:, 0:256], T.B3[:, 0:256], T.KT[:], OP.subtract, "B3 KT", "B5")
+        M = T.B3[:, 15:256:16]
+        ts(sm(1), M, T0 + 409600.0, None, OP.is_lt, None, "B3", "nh")
+        tt(T.BT[:], T.HT[:], T.B5[:, 0:256], OP.subtract, "HT B5", "BT")
+        if last:
+            tt(sm(2), sm(1), XJ, OP.mult, "nh " + st, "nhx")
+        else:
+            tt(T.OO[:, 64:128], sm(1).indirect(T.REP[:, 0:4]), T.PD[:, 64:128], OP.mult, "nh REP DD", "o2")
+        scan(T.SS[:], T.B5[:, 0:256], T.BT[:], 0.0, OP.min, OP.max, "B5 BT", "S")
+        S = T.SS[:, 15:256:16]
+
+        def claim_places():
+            ts(sm(8), M, T0, None, OP.is_lt, None, "B3", "nf")
+            tt(sm(9), S, DJ, OP.subtract, "S DJ0", "dcl")
+            tt(sm(10), sm(1), sm(8), OP.subtract, "nh nf", "can")
+            tt(sm(11), sm(9), sm(10), OP.mult, "dcl can", "dcc")
+            tt(T.LT4[:, 48:64], sm(11), DJ, OP.add, "dcc DJ0", "pl")
+            ts(T.PL16[:], T.LT4[:, 48:64], 4096.0, 2048.0, OP.min, OP.subtract, "pl", "PL16")
+            ts(sm(12), T.LT4[:, 48:64], 4096.0, 2048.0, OP.min, OP.subtract, "pl", "pl32")
+
+        def claim_rows():
+            for k in range(16):
+                mm(T.B1[:, k:256:16], T.BR[:, 128 * k:128 * k + 128], T.PL16[:], True, True, "PL16 BR%d" % k, "B1")
+
+        def claim_rest():
+            cp(T.PN[:], T.B1[:, 0:256], "B1", "PN")
+            tt(T.EE[:, 768:1024], sm(12).indirect(T.DIV[:]), T.PN[:], OP.is_equal, "pl32 DIV PN", "EE16")
+            mm(T.B6[:, 64:112], T.ID[:], T.ZR[:, 0:48], True, False, "ID ZR", "B6")
+            for k in range(16):
+                mm(T.B6[:, 64:80], T.TRI[:, 128 * k:128 * k + 128], T.EE[:, 768 + k:1024:16], False, False,
+                   "EE16 TRI%d" % k, "B6")
+            for c in range(16):
+                if c % 4 != 3:
+                    a, b = 16 * c + 16, 64 * (c // 4) + 64
+                    s = 256 * (c % 4)
+                    ts(T.EE[:, s + a:s + b], T.PN[:, a:b], T.SM[:, 192 + c:193 + c], 8192.0, OP.is_equal, OP.mult,
+                       "PN pl32", "EE%d" % c)
+            to_w(T.B6[:, 64:112], "W1", lambda r: T.EE[:, r:768:16], names("EE", 16), "B6", False, True)
+
+        def claim_writes():
+            tt(T.LT4[:, 0:48], T.B6[:, 64:112], T.JW[:, 0:48], OP.min, "B6 DJ0 DJ1 DJ2", "l4")
+            tt(T.LT2[:], T.LT4[:, 0:32], T.LT4[:, 32:64], OP.max, "l4 pl", "l2")
+            tt(sm(13), T.LT2[:, 0:16], T.LT2[:, 16:32], OP.max, "l2", "l1")
+            cp(T.CU[:], sm(13), "l1", "CU")
+            order = [(n, b) for b in (3, 2, 1, 0) for n in ("VW", "FW")] + [("GW", b) for b in (3, 2, 1, 0)]
+            if last:
+                order = [(n, b) for n in ("FW", "VW", "GW") for b in (3, 2, 1, 0)]
+            for n, b in order:
+                o = {"FW": 0, "VW": 2, "GW": 1}[n]
+                cp(T[n][:, 0:4352].indirect(T.CU[:, 4 * b:4 * b + 4]), lane(t, o, 64 * b, 64 * b + 64),
+                   "CU " + lkey(t, o), n + " " + n + "d")
+                if last and b == 0:
+                    bk, bn, z, out, sem = {"FW": (T.B1, "B1", "ZF", T.zf, "o2"), "VW": (T.B2, "B2", "ZV", T.zv, "o3"),
+                                           "GW": (T.B4, "B4", "ZG", T.zg, "o4")}[n]
+                    for k in range(32):
+                        mm(bk[:, 0:128], T.ID[:], T[n][:, 128 * k:128 * k + 128], k == 0, k == 31, "ID " + n, bn)
+                    act(T[z][:], bk[:, 0:128], bn, z)
+                    dma("s", sem, out[:], T[z][:], z, "out" + z)
+
+        if last:
+            claim_places()
+            claim_rows()
+            tt(T.OO[:, 0:16], S, sm(2), OP.max, "S nhx", "o1")
+            cp(T.OU[:, 0:16], T.OO[:, 0:16], "o1", "OU")
+            act(T.YF[:], T.GW[:, 0:YO].indirect(T.OU[:, 0:16]), "GW GWd GX OU", "YF")
+            dma("s", "o1", T.yf[:], T.YF[:], "YF", "outyf")
+            claim_rest()
+            tt(T.YV[:], T.VW[:].indirect(T.OU[:, 0:16]), T.VQ[:], OP.min, "VW VWd VWt OU VQ", "YV")
+            dma("s", "o0", T.yv[:], T.YV[:], "YV", "outyv")
+            claim_writes()
+            break
+        gw = "GW GWd GX GY NMW0 NMW1 NMW2 OU"
+        tt(T.OO[:, 64:128], T.OO[:, 64:128], T.PD[:, 0:64], OP.add, "o2 PP", "o2")
+        tt(T.OO[:, 0:64], T.SS[:].indirect(T.END[:, 0:4]), T.OO[:, 64:128], OP.max, "S END o2", "o1")
+        cp(T.OU[:], T.OO[:, 0:64], "o1", "OU")
+        cp(T.NX[:, 0:256], T.GW[:].indirect(T.OU[:, 16:32]), gw, "NX")
+        mm(T.B4[:, 0:256], T.RB[:], T.NX[:, 0:256], False, True, "RB NX", "B4")
+        act(T.NY[:, 0:256], T.GW[:].indirect(T.OU[:, 32:48]), gw, "NY")
+        act(T.NN[:, 0:256], T.GW[:].indirect(T.OU[:, 48:64]), gw, "NN")
+        if t == 0:
+            tail_constants2()
+        cp(T.RI[:], T.B4[:, 0:256], "B4", "RI")
+        tt(T.OHD[:], T.B4[:, 0:256], T.RI[:], OP.is_equal, "B4 RI", "OHD")
+        scan(T.B5[:, 0:256], T.OHD[:], T.ZR[:], col("ini"), OP.add, OP.add, "OHD ZR ini", "B5")
+        tt(T.XP[:], T.OHD[:], T.B5[:, 0:256], OP.mult, "OHD B5", "XP")
+        to_w(T.B6[:, 16:32], "WR", lambda r: T.XP[:, r:256:16], "XP", "B6")
+        tt(T.NV[:, 0:256], T.VW[:].indirect(T.OU[:, 0:16]), lane(t, 2, 0, 256), OP.min, "VW VWd VWt OU " + kv, "NV")
+        inv, snd, lnd = "inv%d" % (t + 1), "send%d" % (t + 1), "land%d" % (t + 1)
+        ts(T.PU[:], T.B6[:, 16:32], 256.0, None, OP.add, None, "B6", "PU")
+        cp(T[inv][:].indirect(T.PU[:]), T.JN[:], "PU JN", inv)
+        to_w(T.B6[:, 32:48], "W1", lambda r: T[inv][:, 256 + 16 * r:272 + 16 * r], inv, "B6")
+        claim_places()
+        claim_rows()
+        ts(T.IU[:], T.B6[:, 32:48], 0.0625, None, OP.mult, None, "B6", "IU")
+        parts = []
+        for o, n in enumerate(("NX", "NY", "NV", "NN")):
+            for k in range(2):
+                parts.append("%s%d%d" % (snd, o, k))
+                (act if o % 2 else cp)(T[snd][:, 4 * k + o:1024:8], T[n][:].indirect(T.IU[:, 8 * k:8 * k + 8]),
+                                       "%s %sz IU" % (n, n), parts[-1])
+        need("g", parts, [])
+        for c in calls:
+            xs = []
+            for d, es in c:
+                rid, pid = topo.addr(cores[d])[0:2]
+                xs.append(RemoteDMATransfer(dst_ids=[DstId(rid=rid, pnc=pid)], dma_engine_mask=sum(1 << e for e in es),
+                                            remote_sem=T.sem["arr%d" % (t + 1)], src=T[snd][:, 128 * d:128 * d + 128],
+                                            dst=T[lnd][:, 128 * me:128 * me + 128]))
+            g.remote_dma_fused(xs, local_sem=T.sem.sent)
+        act(T[lnd][:, 128 * me:128 * me + 128], T[snd][:, 128 * me:128 * me + 128], " ".join(parts), lnd)
+        note(("arr%d" % (t + 1), comes, "d"), [], [lnd], True)
+        claim_rest()
+        claim_writes()
+
+    g.wait_ge(T.sem.sent, (RO - 1) * sum(len(es) for c in calls for d, es in c))
+    for e in "vapg":
+        g.wait_ge(T.sem["s" + e], cnt[e])
+    for s in ("o0", "o1", "o2", "o3", "o4"):
+        g.wait_ge(T.sem[s], 16)

@@ -25,11 +25,11 @@ _decl(B, "sbuf", FW=4352, VW=4608, GW=5632, VG=4096, LO=4096, EQ=4096, OV=4096, 
       AL=256, BB=256, land1=1024, land2=1024, land3=1024, send1=1024, send2=1024, send3=1024,
       inv1=2304, inv2=2304, inv3=2304, NX=272, NY=272, NV=272, NN=272, PEN=384, FL=256, VQ=256, FQ=1024,
       EE=1024, OHD=256, YF=256, YV=256, ZR=256, SG=256,
-      ID=128, NI=128, BLK=128, BW=128, RN=128, RB=128, S1=128, S2=128, P0=128, W1=144, W16=144, WZ=144,
-      TRI=2048, AB8=16, NW=32, CT=256, CK=256, NEG=128, ONE=128, JN=256, DW=256, DF=256)
+      ID=128, NI=128, BLK=128, BW=128, RN=128, RB=128, S1=128, S2=128, P0=128, W1=144, W16=144, WZ=144, W8=144,
+      TRI=2048, AB8=16, NW=32, CT=256, CK=256, NEG=128, ONE=128, JN=256, DW=256, DF=256, DL=256)
 _decl(H, "sbuf", UB=256, XP=256, WR=144, BR=2048, D1=256, DK=256, ON16=128, PN=256, PL16=16)
 _decl(F, "sbuf", TQ=128, QQ=144, QG=128, QL=128, TT=128, COL=48, E16=16, LT=16, TAB=16, DQ=256, KS=256, KT=256,
-      HT=256, BT=256, SS=256, SM=256, ST=192, PD=192, OO=128, LT4=64, LT2=32, JW=64, PB=128, ZF=128, ZG=128, ZV=128)
+      HT=256, BT=256, DF2=192, SS=256, SM=256, ST=192, PD=192, OO=128, LT4=64, LT2=32, JW=64, PB=128, ZF=128, ZG=128, ZV=128)
 _decl(I, "sbuf", NI32=256, SI=128, UI=256, WI=128, H0=256, HI=256, RI=256, CI=16)
 _decl(U, "sbuf", HU=256, OU=64, PU=16, IU=16, CU=16, REP=16, DIV=16, TRN=16, END=16)
 _decl(F, "psum", B0=1024, B1=512, B2=512, B3=512, B4=512, B5=512, B6=512)
@@ -44,10 +44,12 @@ def plan(src, cores, topo):
     far = [(me + k) % N for k in range(1, N) if (me + k) % N not in near]
     off = topo.engines(src, cores[far[0]])
     on = [e for e in topo.engines(src, cores[near[0]]) if e not in off]
-    h, q = len(off) // 2, len(off) // 4
-    one = [(far[0], off[:h]), (far[1], off[h:h + q]), (far[2], off[h + q:]), (near[0], on)]
-    two = [(far[3], off[h:]), (far[4], off[:q]), (far[5], off[q:h])]
-    return [one, two]
+    out = []
+    for own in (False, True):
+        ds = [d for d in far if (d // 4 == me // 4) == own]
+        n = len(off) // len(ds)
+        out.append([(d, off[n * k:n * k + n]) for k, d in enumerate(ds)] + ([(near[0], on)] if own else []))
+    return out
 
 
 def rank_program(g, core, T, topo):
@@ -59,6 +61,7 @@ def rank_program(g, core, T, topo):
     cnt = {"v": 0, "a": 0, "p": 0, "g": 0}
     seen = {e: {} for e in Q}
     wr, rd, knew = {}, {}, {}
+    skip = [False]
 
     def need(e, r, w):
         deps = []
@@ -93,6 +96,8 @@ def rank_program(g, core, T, topo):
             rd[k] = []
 
     def op(e, fn, r, w):
+        if skip[0]:
+            return
         r, w = r.split(), w.split()
         need(e, r, w)
         cnt[e] += 1
@@ -250,7 +255,6 @@ def rank_program(g, core, T, topo):
         act(d[0:16, 128:256], T.D1[0:16, 0:128], "D1", "DW%db" % k, scale=b)
 
     def late_constants():
-        ts(T.LT[:], T.QQ[:, 0:16], col("R"), 8192.0, OP.is_gt, OP.mult, "QQ R", "LT")
         ts(T.REP[:], T.QQ[:, 0:16], 0.0, col("R"), OP.mult, OP.add, "QQ R", "REP")
         cp(T.DIV[:], T.QQ[:, 0:16], "QQ", "DIV")
         ts(T.TRN[:], T.QQ[:, 0:16], col("r16"), None, OP.add, None, "QQ r16", "TRN")
@@ -270,26 +274,27 @@ def rank_program(g, core, T, topo):
         act(col("b8"), col("AB"), "AB nA", "b8", scale=0.125, bias=col("nA"))
         act(T.W16[:], T.W1[:], "W1", "W16", scale=65536.0)
         act(T.WZ[:], T.W1[:], "W1 wz", "WZ", scale=col("wz"))
+        act(T.W8[:], T.W1[:], "W1", "W8", scale=8192.0)
+        tail_constants2(0, 16)
         act(T.NI[:], T.ID[:], "ID", "NI", scale=-1.0)
+        act(T.RN[:], T.BW[:], "BW", "RN", scale=-0.0625)
+        act(T.CT[:], T.JN[:], "JN rb", "CT", scale=0.0, bias=col("rb"))
+        act(T.WR[:], T.W1[:], "W1 wr", "WR", scale=col("wr"))
         J = T.JW[:, 48:64]
         for a, sc, bi in ((32, 1.0, YO), (48, 3.0, NO + 1), (80, 1.0, YO), (96, -1.0, -YO), (128, 1.0, XO), (144, 1.0, XO)):
             act(T.ST[:, a:a + 16], J, "JW ST", "ST%d" % a, scale=sc, bias=float(bi))
 
     def tail_constants():
         J = T.JW[:, 48:64]
-        act(T.RN[:], T.BW[:], "BW", "RN", scale=-0.0625)
-        act(T.CT[:], T.JN[:], "JN rb", "CT", scale=0.0, bias=col("rb"))
-        act(T.WR[:], T.W1[:], "W1 wr", "WR", scale=col("wr"))
         for k in range(3):
             act(T.JW[:, 16 * k:16 * k + 16], J, "JW", "DJ%d" % k, bias=4096.0)
-        for k in range(12):
+        for k in range(16):
             act(T.BR[:, 128 * k:128 * k + 128], T.BLK[:], "BLK E16", "BR%d" % k, scale=E(k))
 
-    def tail_constants2():
-        for k in range(12, 16):
-            act(T.BR[:, 128 * k:128 * k + 128], T.BLK[:], "BLK E16", "BR%d" % k, scale=E(k))
-        for k in range(16):
-            act(T.TRI[:, 128 * k:128 * k + 128], T.W1[:, 15 - k:143 - k], "W1 LT", "TRI%d" % k, scale=T.LT[:, k:k + 1])
+    def tail_constants2(a, b):
+        for k in range(a, b):
+            op("g", lambda: g.affine_select(T.TRI[:, 128 * k:128 * k + 128], T.W8[:, 15 - k:143 - k], [[1, 128]],
+                                            OP.is_gt, 0.0, 0, -1), "W8", "TRI%d" % k)
 
     st = "ST ST32 ST48 ST80 ST96 ST128 ST144"
     XJ, DJ = T.ST[:, 128:144], T.JW[:, 0:16]
@@ -314,7 +319,7 @@ def rank_program(g, core, T, topo):
         for k in range(16):
             mm(T.B3[0:16, k:128:16], lane(t, 0, k, 256, 16), T.AB8[:, 0:8], True, True, kx + " AB8", "B3")
         for k in range(16):
-            mm(T.B3[0:16, 128 + k:512:16], lane(t, 3, k, 256, 16), T.NW[:, 0:24], True, True, kn + " NW0 NW1 NW2", "B3")
+            mm(T.B6[0:16, 128 + k:512:16], lane(t, 3, k, 256, 16), T.NW[:, 0:24], True, True, kn + " NW0 NW1 NW2", "B6")
         mm(T.B5[:, 0:256], T.BW[:], NM, True, True, kn + " BW", "B5")
         mm(T.B4[:, 0:256], T.ON16[0:16, :], T.DK[0:16, :], True, False, "ON16 " + dk, "B4")
         mm(T.B4[:, 0:256], T.ON16[0:16, :], T.D1[0:16, :], False, False, "ON16 D1", "B4")
@@ -322,16 +327,23 @@ def rank_program(g, core, T, topo):
             act(T.GW[:, YO:YO + 256], lane(t, 1, 0, 256), ky, "GY")
             act(T.GW[:, NO:NO + 768:3], NM, kn, "NMW0")
             versions()
+        def write_g(b):
+            if t:
+                cp(T.GW[:, 0:4352].indirect(T.CU[:, 4 * b:4 * b + 4]), lane(t - 1, 1, 64 * b, 64 * b + 64),
+                   "CU " + lkey(t - 1, 1), "GW GWd")
+        for b in (3, 2, 1, 0):
+            write_g(b)
         cp(T.SI[0:16, :], T.B3[0:16, 0:128], "B3", "SI")
         ts(T.UI[0:16, 0:128], T.SI[0:16, :], 4095, None, OP.bitwise_and, None, "SI", "UI0")
-        tt(T.WI[0:16, :], T.UI[0:16, 0:128], T.B3[0:16, 128:256], OP.mult, "UI0 B3", "WI")
+        tt(T.WI[0:16, :], T.UI[0:16, 0:128], T.B6[0:16, 128:256], OP.mult, "UI0 B6", "WI")
+        ts(T.UB[0:16, 0:128], T.UI[0:16, 0:128], 2048.0, None, OP.subtract, None, "UI0", "UBa")
+        mm(T.B4[:, 0:256], T.UB[0:16, 0:128], T.DK[0:16, :], False, False, "UBa " + dk, "B4")
         ts(T.UI[0:16, 128:256], T.WI[0:16, :], 5, 4095, OP.arith_shift_right, OP.bitwise_and, "WI", "UI1")
-        ts(T.UB[0:16, :], T.UI[0:16, :], 2048.0, None, OP.subtract, None, "UI0 UI1", "UB")
-        mm(T.B4[:, 0:256], T.UB[0:16, 0:128], T.DK[0:16, :], False, False, "UB " + dk, "B4")
+        ts(T.UB[0:16, 128:256], T.UI[0:16, 128:256], 2048.0, None, OP.subtract, None, "UI1", "UB")
         mm(T.B4[:, 0:256], T.UB[0:16, 128:256], T.D1[0:16, :], False, True, "UB D1", "B4")
         for k in range(4):
             mm(T.B0[:, 256 * k:256 * k + 256], T.ID[:], lane(t, 2, 0, 256), True, True, kv + " ID", "B0")
-        act(T.FL[0:16, :], T.B3[0:16, 256:512], "B3", "FL")
+        act(T.FL[0:16, :], T.B6[0:16, 256:512], "B6", "FL")
         if t == 0:
             early_constants()
         tt(T.GW[:, XO:XO + 256], lane(t, 0, 0, 256), T.B5[:, 0:256], OP.mult, kx + " B5", "GX")
@@ -345,9 +357,20 @@ def rank_program(g, core, T, topo):
         ts(T.HI[:], T.H0[:], 4095, None, OP.bitwise_and, None, "H0", "HI")
         cp(T.HU[:], T.HI[:], "HI", "HU")
         if last:
-            tt(T.VQ[:], lane(t, 2, 0, 256), T.B5[:, 0:256], OP.mult, kv + " B5", "VQ")
+            act(T.VW[:, XO:XO + 256], T.B5[:, 0:256], "B5", "VWt", scale=float(TOP))
         if t == 0:
             late_constants()
+        if last:
+            where = {"EQ": ((T.B4, "B4", 0), (T.B4, "B4", 128)), "OV": ((T.B5, "B5", 0), (T.B5, "B5", 128)),
+                     "LO": ((T.B1, "B1", 0), (T.B1, "B1", 128))}
+            mm(T.B4[:, 0:256], T.FL[0:16, 128:256], T.DL[0:16, :], True, False, "FL DL", "B4")
+            mm(T.B5[:, 0:256], T.ID[:], T.ZR[:], True, False, "ID ZR", "B5")
+            mm(T.B1[:, 0:256], T.ID[:], T.CK[:], True, False, "ID CK", "B1")
+            for a in (0, 128):
+                mm(T.B4[:, a:a + 128], T.FL[0:16, 0:128], T.DW[0:16, 0:128], False, False, "FL DW0a", "B4")
+                mm(T.B5[:, a:a + 128], T.FL[0:16, 0:128], T.DW[0:16, 128:256], False, False, "FL DW0b", "B5")
+                mm(T.B1[:, a:a + 128], T.NEG[:], T.ONE[:], False, False, "NEG ONE", "B1")
+        skip[0] = last
         for k, (a, b) in enumerate(((0, 0), (128, 1))):
             fl, dw, r = T.FL[0:16, a:a + 128], (T.DW, T.DF)[b], "FL DW%da DW%db" % (b, b)
             mm(T.B3[:, 0:256], fl, dw[0:16, :], k == 0, False, r, "B3")
@@ -425,105 +448,164 @@ def rank_program(g, core, T, topo):
         tt(T.B5[:, 0:256], T.B3[:, 0:256], T.KT[:], OP.subtract, "B3 KT", "B5")
         M = T.B3[:, 15:256:16]
         ts(sm(1), M, T0 + 409600.0, None, OP.is_lt, None, "B3", "nh")
+        act(sm(8), M, "B3", "off", AF.Abs, bias=-(T0 + 32768.0))
+        act(sm(9), sm(8), "off", "far", AF.Relu, bias=-40000.0)
         tt(T.BT[:], T.HT[:], T.B5[:, 0:256], OP.subtract, "HT B5", "BT")
-        if last:
-            tt(sm(2), sm(1), XJ, OP.mult, "nh " + st, "nhx")
-        else:
-            tt(T.OO[:, 64:128], sm(1).indirect(T.REP[:, 0:4]), T.PD[:, 64:128], OP.mult, "nh REP DD", "o2")
+        tt(T.OO[:, 64:128], sm(1).indirect(T.REP[:, 0:4]), T.PD[:, 64:128], OP.mult, "nh REP DD", "o2")
         scan(T.SS[:], T.B5[:, 0:256], T.BT[:], 0.0, OP.min, OP.max, "B5 BT", "S")
+        tt(T.OO[:, 64:128], T.OO[:, 64:128], T.PD[:, 0:64], OP.add, "o2 PP", "o2")
         S = T.SS[:, 15:256:16]
+        skip[0] = False
+        pb, pn = (T.B3, "B3") if last else (T.B1, "B1")
 
         def claim_places():
-            ts(sm(8), M, T0, None, OP.is_lt, None, "B3", "nf")
-            tt(sm(9), S, DJ, OP.subtract, "S DJ0", "dcl")
-            tt(sm(10), sm(1), sm(8), OP.subtract, "nh nf", "can")
-            tt(sm(11), sm(9), sm(10), OP.mult, "dcl can", "dcc")
-            tt(T.LT4[:, 48:64], sm(11), DJ, OP.add, "dcc DJ0", "pl")
+            tt(sm(10), sm(9), DJ, OP.min, "far DJ0", "dcc")
+            tt(T.LT4[:, 48:64], sm(10), S, OP.max, "dcc S", "pl")
             ts(T.PL16[:], T.LT4[:, 48:64], 4096.0, 2048.0, OP.min, OP.subtract, "pl", "PL16")
-            ts(sm(12), T.LT4[:, 48:64], 4096.0, 2048.0, OP.min, OP.subtract, "pl", "pl32")
+            act(sm(12), T.PL16[:], "PL16", "pl32")
 
         def claim_rows():
             for k in range(16):
-                mm(T.B1[:, k:256:16], T.BR[:, 128 * k:128 * k + 128], T.PL16[:], True, True, "PL16 BR%d" % k, "B1")
+                mm(pb[:, k:256:16], T.BR[:, 128 * k:128 * k + 128], T.PL16[:], True, True, "PL16 BR%d" % k, pn)
 
-        def claim_rest():
-            cp(T.PN[:], T.B1[:, 0:256], "B1", "PN")
+        def claim_early():
+            by_act = (1, 2, 5, 6, 10, 14)
+            for i, c in enumerate(by_act):
+                a, b = 16 * c + 16, 64 * (c // 4) + 64
+                act(T.DF2[:, 32 * i:32 * i + b - a], T.PN[:, a:b], "PN pl32", "ab%d" % c,
+                    AF.Abs, bias=T.SM[:, 192 + c:193 + c], scale=-1.0)
+            for i, c in enumerate(by_act):
+                a, b = 16 * c + 16, 64 * (c // 4) + 64
+                act(T.EE[:, 256 * (c % 4) + a:256 * (c % 4) + b], T.DF2[:, 32 * i:32 * i + b - a], "ab%d" % c,
+                    "EE%d" % c, AF.Relu, bias=8192.0, scale=-8192.0)
             tt(T.EE[:, 768:1024], sm(12).indirect(T.DIV[:]), T.PN[:], OP.is_equal, "pl32 DIV PN", "EE16")
-            mm(T.B6[:, 64:112], T.ID[:], T.ZR[:, 0:48], True, False, "ID ZR", "B6")
+            mm(T.B2[:, 0:48], T.ID[:], T.ZR[:, 0:48], True, False, "ID ZR", "B2")
             for k in range(16):
-                mm(T.B6[:, 64:80], T.TRI[:, 128 * k:128 * k + 128], T.EE[:, 768 + k:1024:16], False, False,
-                   "EE16 TRI%d" % k, "B6")
-            for c in range(16):
-                if c % 4 != 3:
-                    a, b = 16 * c + 16, 64 * (c // 4) + 64
-                    s = 256 * (c % 4)
-                    ts(T.EE[:, s + a:s + b], T.PN[:, a:b], T.SM[:, 192 + c:193 + c], 8192.0, OP.is_equal, OP.mult,
-                       "PN pl32", "EE%d" % c)
-            to_w(T.B6[:, 64:112], "W1", lambda r: T.EE[:, r:768:16], names("EE", 16), "B6", False, True)
+                mm(T.B2[:, 0:16], T.TRI[:, 128 * k:128 * k + 128], T.EE[:, 768 + k:1024:16], False, False,
+                   "EE16 TRI%d" % k, "B2")
+
+        def claim_pairs(cs):
+            for c in cs:
+                a, b = 16 * c + 16, 64 * (c // 4) + 64
+                s = 256 * (c % 4)
+                ts(T.EE[:, s + a:s + b], T.PN[:, a:b], T.SM[:, 192 + c:193 + c], 8192.0, OP.is_equal, OP.mult,
+                   "PN pl32", "EE%d" % c)
+
+        def claim_rest(cs):
+            claim_pairs(cs)
+            to_w(T.B2[:, 0:48], "W1", lambda r: T.EE[:, r:768:16], names("EE", 16), "B2", False, True)
 
         def claim_writes():
-            tt(T.LT4[:, 0:48], T.B6[:, 64:112], T.JW[:, 0:48], OP.min, "B6 DJ0 DJ1 DJ2", "l4")
+            tt(T.LT4[:, 0:48], T.B2[:, 0:48], T.JW[:, 0:48], OP.min, "B2 DJ0 DJ1 DJ2", "l4")
             tt(T.LT2[:], T.LT4[:, 0:32], T.LT4[:, 32:64], OP.max, "l4 pl", "l2")
             tt(sm(13), T.LT2[:, 0:16], T.LT2[:, 16:32], OP.max, "l2", "l1")
             cp(T.CU[:], sm(13), "l1", "CU")
-            order = [(n, b) for b in (3, 2, 1, 0) for n in ("VW", "FW")] + [("GW", b) for b in (3, 2, 1, 0)]
-            if last:
-                order = [(n, b) for n in ("FW", "VW", "GW") for b in (3, 2, 1, 0)]
+
+        def write(order):
             for n, b in order:
                 o = {"FW": 0, "VW": 2, "GW": 1}[n]
                 cp(T[n][:, 0:4352].indirect(T.CU[:, 4 * b:4 * b + 4]), lane(t, o, 64 * b, 64 * b + 64),
                    "CU " + lkey(t, o), n + " " + n + "d")
-                if last and b == 0:
-                    bk, bn, z, out, sem = {"FW": (T.B1, "B1", "ZF", T.zf, "o2"), "VW": (T.B2, "B2", "ZV", T.zv, "o3"),
-                                           "GW": (T.B4, "B4", "ZG", T.zg, "o4")}[n]
-                    for k in range(32):
-                        mm(bk[:, 0:128], T.ID[:], T[n][:, 128 * k:128 * k + 128], k == 0, k == 31, "ID " + n, bn)
-                    act(T[z][:], bk[:, 0:128], bn, z)
-                    dma("s", sem, out[:], T[z][:], z, "out" + z)
+
+        def zsum(n, bk, bn, a, b):
+            for k in range(a, b):
+                mm(bk, T.ID[:], T[n][:, 128 * k:128 * k + 128], k == 0, k == 31, "ID " + n, bn)
+
+        def zout(bk, bn, z, out, sem):
+            act(T[z][:], bk, bn, z)
+            dma("s", sem, out[:], T[z][:], z, "out" + z)
 
         if last:
-            claim_places()
+            for k in range(4):
+                gv(k); eq(k); sums(k, "EQ", "W1", k == 3)
+                if k == 0:
+                    cp(T.HT[:], T.HI[:].indirect(T.TRN[:]), "HI TRN", "HT")
+            tt(T.BT[:], T.HI[:], T.CK[:], OP.add, "HI CK", "BT")
+            ts(T.B3[:, 0:256], T.B4[:, 0:256], 215.5, 131072.0, OP.subtract, OP.mult, "B4", "B3")
+            act(T.PEN[:, 0:256], T.B4[:, 0:256], "B4", "PENa", AF.Relu, bias=76.0 * BIG, scale=-BIG)
+            tt(T.SS[:], T.B3[:, 0:256], T.BT[:], OP.min, "B3 BT", "S")
+            tt(T.KT[:, 0:128], T.SS[:, 0:128], T.SS[:, 128:256], OP.max, "S", "KT")
+            tt(T.SS[:, 0:64], T.KT[:, 0:64], T.KT[:, 64:128], OP.max, "KT", "S")
+            tt(T.KT[:, 0:32], T.SS[:, 0:32], T.SS[:, 32:64], OP.max, "S", "KT")
+            tt(T.CI[:], T.KT[:, 0:16], T.KT[:, 16:32], OP.max, "KT", "CIa")
+            ts(sm(9), T.CI[:], -1.0, None, OP.mult, None, "CIa", "far")
+            ts(T.RI[:, 0:16], T.CI[:], 4095, None, OP.bitwise_and, None, "CIa", "RI")
+            tt(sm(10), sm(9), DJ, OP.min, "far DJ0", "dcc")
+            tt(T.LT4[:, 48:64], sm(10), T.RI[:, 0:16], OP.max, "dcc RI", "pl")
+            ts(T.PL16[:], T.LT4[:, 48:64], 4096.0, 2048.0, OP.min, OP.subtract, "pl", "PL16")
+            act(sm(12), T.PL16[:], "PL16", "pl32")
             claim_rows()
+            act(T.PN[:], T.B3[:, 0:256], "B3", "PN")
+            mn(0)
+            claim_early()
+            claim_rest((0, 4, 8, 9, 12, 13))
+            mn(1); sg(0)
+            claim_writes()
+            write([("FW", b) for b in (3, 2, 1, 0)])
+            zf, zv, zg = T.B3[:, 0:128], T.B2[:, 0:128], T.B6[:, 0:128]
+            sums(0, "OV", "W1", False); sg(1); sums(1, "OV", "W1", False)
+            zsum("FW", zf, "B3", 0, 16)
+            mn(2); sg(2)
+            zsum("FW", zf, "B3", 16, 32)
+            mn(3); sums(2, "OV", "W1", False); sg(3)
+            write([(n, b) for n in ("VW", "GW") for b in (3, 2, 1, 0)])
+            mm(T.B1[:, 0:256], T.NI[:], T.PEN[:, 0:256], False, False, "NI PENa", "B1")
+            sums(3, "OV", "W1", True)
+            ts(T.BT[:], T.B5[:, 0:256], 76.0, -BIG, OP.is_lt, OP.mult, "B5", "BT")
+            zout(zf, "B3", "ZF", T.zf, "o2")
+            mm(T.B1[:, 0:16], T.ID[:], T.ZR[:, 0:16], False, True, "ID ZR", "B1")
+            zsum("VW", zv, "B2", 0, 32)
+            zsum("GW", zg, "B6", 0, 32)
+            tt(T.KS[:], T.B1[:, 0:256], T.BT[:], OP.add, "B1 BT", "KSa KSb")
+            cp(T.KT[:], T.KS[:].indirect(T.TRN[:]), "KSa KSb TRN", "KT")
+            scan(T.B4[:, 0:256], T.SG[:], T.KT[:], 0.0, OP.add, OP.max, "SG KT", "B4")
+            tt(T.B5[:, 0:256], T.B4[:, 0:256], T.KT[:], OP.subtract, "B4 KT", "B5")
+            ts(sm(1), T.B4[:, 15:256:16], T0 + 409600.0, None, OP.is_lt, None, "B4", "nh")
+            tt(T.BT[:], T.HT[:], T.B5[:, 0:256], OP.subtract, "HT B5", "BT")
+            tt(sm(2), sm(1), XJ, OP.mult, "nh " + st, "nhx")
+            scan(T.SS[:], T.B5[:, 0:256], T.BT[:], 0.0, OP.min, OP.max, "B5 BT", "S")
+            zout(zv, "B2", "ZV", T.zv, "o3")
             tt(T.OO[:, 0:16], S, sm(2), OP.max, "S nhx", "o1")
             cp(T.OU[:, 0:16], T.OO[:, 0:16], "o1", "OU")
             act(T.YF[:], T.GW[:, 0:YO].indirect(T.OU[:, 0:16]), "GW GWd GX OU", "YF")
+            tt(T.YV[:], T.VW[:].indirect(T.OU[:, 0:16]), lane(t, 2, 0, 256), OP.min, "VW VWd VWt OU " + kv, "YV")
             dma("s", "o1", T.yf[:], T.YF[:], "YF", "outyf")
-            claim_rest()
-            tt(T.YV[:], T.VW[:].indirect(T.OU[:, 0:16]), T.VQ[:], OP.min, "VW VWd VWt OU VQ", "YV")
             dma("s", "o0", T.yv[:], T.YV[:], "YV", "outyv")
-            claim_writes()
+            zout(zg, "B6", "ZG", T.zg, "o4")
             break
         gw = "GW GWd GX GY NMW0 NMW1 NMW2 OU"
-        tt(T.OO[:, 64:128], T.OO[:, 64:128], T.PD[:, 0:64], OP.add, "o2 PP", "o2")
         tt(T.OO[:, 0:64], T.SS[:].indirect(T.END[:, 0:4]), T.OO[:, 64:128], OP.max, "S END o2", "o1")
         cp(T.OU[:], T.OO[:, 0:64], "o1", "OU")
         cp(T.NX[:, 0:256], T.GW[:].indirect(T.OU[:, 16:32]), gw, "NX")
         mm(T.B4[:, 0:256], T.RB[:], T.NX[:, 0:256], False, True, "RB NX", "B4")
         act(T.NY[:, 0:256], T.GW[:].indirect(T.OU[:, 32:48]), gw, "NY")
+        act(T.YV[:], T.VW[:].indirect(T.OU[:, 0:16]), "VW VWd VWt OU", "YV")
         act(T.NN[:, 0:256], T.GW[:].indirect(T.OU[:, 48:64]), gw, "NN")
-        if t == 0:
-            tail_constants2()
         cp(T.RI[:], T.B4[:, 0:256], "B4", "RI")
         tt(T.OHD[:], T.B4[:, 0:256], T.RI[:], OP.is_equal, "B4 RI", "OHD")
         scan(T.B5[:, 0:256], T.OHD[:], T.ZR[:], col("ini"), OP.add, OP.add, "OHD ZR ini", "B5")
         tt(T.XP[:], T.OHD[:], T.B5[:, 0:256], OP.mult, "OHD B5", "XP")
         to_w(T.B6[:, 16:32], "WR", lambda r: T.XP[:, r:256:16], "XP", "B6")
-        tt(T.NV[:, 0:256], T.VW[:].indirect(T.OU[:, 0:16]), lane(t, 2, 0, 256), OP.min, "VW VWd VWt OU " + kv, "NV")
+        claim_places()
+        claim_rows()
+        tt(T.NV[:, 0:256], T.YV[:], T.B0[:, 0:256], OP.min, "YV B0", "NV")
         inv, snd, lnd = "inv%d" % (t + 1), "send%d" % (t + 1), "land%d" % (t + 1)
         ts(T.PU[:], T.B6[:, 16:32], 256.0, None, OP.add, None, "B6", "PU")
         cp(T[inv][:].indirect(T.PU[:]), T.JN[:], "PU JN", inv)
         to_w(T.B6[:, 32:48], "W1", lambda r: T[inv][:, 256 + 16 * r:272 + 16 * r], inv, "B6")
-        claim_places()
-        claim_rows()
+        act(T.PN[:], T.B1[:, 0:256], "B1", "PN")
+        claim_early()
         ts(T.IU[:], T.B6[:, 32:48], 0.0625, None, OP.mult, None, "B6", "IU")
-        parts = []
-        for o, n in enumerate(("NX", "NY", "NV", "NN")):
-            for k in range(2):
-                parts.append("%s%d%d" % (snd, o, k))
-                (act if o % 2 else cp)(T[snd][:, 4 * k + o:1024:8], T[n][:].indirect(T.IU[:, 8 * k:8 * k + 8]),
-                                       "%s %sz IU" % (n, n), parts[-1])
-        need("g", parts, [])
         for c in calls:
+            h = c[0][0] // 4
+            parts = []
+            for o, n in enumerate(("NX", "NY", "NV", "NN")):
+                for k in range(2):
+                    parts.append("%s%d%d%d" % (snd, h, o, k))
+                    (act if o % 2 else cp)(T[snd][:, 512 * h + 4 * k + o:512 * h + 512:8],
+                                           T[n][:].indirect(T.IU[:, 8 * k + 4 * h:8 * k + 4 * h + 4]),
+                                           "%s %sz IU" % (n, n), parts[-1])
+            need("g", parts, [])
             xs = []
             for d, es in c:
                 rid, pid = topo.addr(cores[d])[0:2]
@@ -533,8 +615,11 @@ def rank_program(g, core, T, topo):
             g.remote_dma_fused(xs, local_sem=T.sem.sent)
         act(T[lnd][:, 128 * me:128 * me + 128], T[snd][:, 128 * me:128 * me + 128], " ".join(parts), lnd)
         note(("arr%d" % (t + 1), comes, "d"), [], [lnd], True)
-        claim_rest()
+        claim_rest((0, 4, 8, 9, 12, 13))
         claim_writes()
+        write([(n, b) for b in (3, 2, 1, 0) for n in ("VW", "FW")])
+        if t == 1:
+            act(T.DL[0:16, :], T.D1[0:16, :], "D1", "DL", scale=200.0)
 
     g.wait_ge(T.sem.sent, (RO - 1) * sum(len(es) for c in calls for d, es in c))
     for e in "vapg":

@@ -1,3 +1,4 @@
+import numpy as np
 from concourse.bass import DstId, RemoteDMATransfer
 from concourse.mybir import AluOpType as OP, AxisListType as AX, ActivationFunctionType as AF
 
@@ -8,9 +9,11 @@ WA = [7, 113, 51, 229, 87, 19, 161, 203, 35, 149, 71, 247, 93, 181, 125, 11]
 WB = [1, 3, 2, 7, 5, 1, 6, 3, 7, 2, 5, 4, 1, 6, 3, 5]
 KP = [3, 18, 45, 71, 102, 125, 150, 187, 208, 233, 260, 291, 318, 345, 382, 407]
 TOP = 130560
-BIG = float(2 ** 38)
 T0 = -float(2 ** 36)
-XO, YO, NO = 4352, 4608, 4864
+HG = float(2 ** 37)
+N1, N2, X0, N0, LB = 4352, 4608, 4864, 5120, 5376
+VZ, VT = 4352, 4368
+ix = np.s_
 
 B, F, H, I, U = "bfloat16", "float32", "float16", "int32", "uint16"
 SCRATCH = {}
@@ -18,24 +21,24 @@ SCRATCH = {}
 
 def _decl(dt, where, **kw):
     for k, n in kw.items():
-        SCRATCH[k] = (where, [128, n], dt)
+        SCRATCH[k] = (where, [128] + (list(n) if isinstance(n, tuple) else [n]), dt)
 
 
-_decl(B, "sbuf", FW=4352, VW=4608, GW=5632, VG=4096, LO=4096, EQ=4096, OV=4096, X0=256, V0=256, N0=256, NB=256,
-      AL=256, BB=256, land1=1024, land2=1024, land3=1024, send1=1024, send2=1024, send3=1024,
-      inv1=2304, inv2=2304, inv3=2304, NX=272, NY=272, NV=272, NN=272, PEN=384, FL=256, VQ=256, FQ=1024,
-      EE=1024, OHD=256, YF=256, YV=256, ZR=256, SG=256,
-      ID=128, NI=128, BLK=128, BW=128, RN=128, RB=128, S1=128, S2=128, P0=128, W1=144, W16=144, WZ=144, W8=144,
-      TRI=2048, AB8=16, NW=32, CT=256, CK=256, NEG=128, ONE=128, JN=256, DW=256, DF=256, DL=256)
-_decl(H, "sbuf", UB=256, XP=256, WR=144, BR=2048, D1=256, DK=256, ON16=128, PN=256, PL16=16)
-_decl(F, "sbuf", TQ=128, QQ=144, QG=128, QL=128, TT=128, COL=48, E16=16, LT=16, TAB=16, DQ=256, KS=256, KT=256,
-      HT=256, BT=256, DF2=192, SS=256, SM=256, ST=192, PD=192, OO=128, LT4=64, LT2=32, JW=64, PB=128, ZF=128, ZG=128, ZV=128)
-_decl(I, "sbuf", NI32=256, SI=128, UI=256, WI=128, H0=256, HI=256, RI=256, CI=16)
-_decl(U, "sbuf", HU=256, OU=64, PU=16, IU=16, CU=16, REP=16, DIV=16, TRN=16, END=16)
-_decl(F, "psum", B0=1024, B1=512, B2=512, B3=512, B4=512, B5=512, B6=512)
+_decl(B, "sbuf", FW=4352, VW=4384, GW=LB + 3072, VG=4096, LO=4096, EQ=4096, OV=4096, V0=256, NB=256, BB=256,
+      send1=1024, send2=1024, send3=1024, inv1=512, inv2=512, inv3=512, N4=1088, FL=384, FQ=1024,
+      EE=1024, OHD=256, YF=256, YV=256, ZR=48, SG=128, CAP=128,
+      ID=128, BLK=128, BW=128, RN=128, RB=128, S1=128, S2=128, P0=128, W1=144, W16=144, WZ=144, W8=144, WE=144,
+      WO=144, WK=144, TRI=2048, AB8=16, NW=32, CT=128, CK=256, NEG=128, ONE=256, JN=256, DE=256, DO=256)
+_decl(H, "sbuf", UB=256, XP=256, WR=144, BR=2048, D1=256, DK=256, O16=128, PN=256, PL16=16)
+_decl(F, "sbuf", TQ=128, QQ=144, QG=128, QK=144, TT=128, COL=48, E16=16, TAB=16, DQ=256, KS=256, KO=256, KK=256,
+      BT=256, DF2=384, SS=256, SM=256, ST=160, J3=48, PP=64, ZP=48, OO=128, LT4=64, LT2=32, JW=80, PB=128,
+      ZF=128, ZG=128, ZV=128)
+_decl(I, "sbuf", NI32=256, SI=128, UI=256, WI=128, H0=(16, 16), HI=(16, 16), RI=256, CI=16)
+_decl(U, "sbuf", HU=256, OU=64, PU=16, IU=64, CU=16, REP=16, DIV=16, END=16)
+_decl(F, "psum", PV=(64, 16), PK=(32, 16), PE=(32, 16), PO=(32, 16), Pa=512, Pb=512, Pc=512)
 
 SEMAPHORES = ["sv", "sa", "sp", "sg", "d0", "d1", "d2", "d3", "d4", "d5", "o0", "o1", "o2", "o3", "o4",
-              "arr1", "arr2", "arr3", "sent", "fq"]
+              "arr1", "arr2", "arr3", "sent"]
 
 
 def plan(src, cores, topo):
@@ -60,22 +63,38 @@ def rank_program(g, core, T, topo):
     Q = {"v": g.vector, "a": g.scalar, "p": g.tensor, "g": g, "s": g.sync}
     cnt = {"v": 0, "a": 0, "p": 0, "g": 0}
     seen = {e: {} for e in Q}
-    wr, rd, knew = {}, {}, {}
-    skip = [False]
+    acc, banks, knew, views = {}, {}, {}, {}
+
+    def vw(name, s):
+        key = (name, repr(s))
+        if key not in views:
+            where, shape, _ = SCRATCH[name]
+            n = int(np.prod(shape[1:]))
+            cols = np.arange(n).reshape(shape[1:])[s[1:]].ravel()
+            m = np.zeros(n, bool)
+            m[cols] = True
+            p = range(128)[s[0]]
+            bk = sorted(set((name, int(c) // 512) for c in cols)) if where == "psum" else []
+            views[key] = (T[name][s], [(name, p[0], p[-1], int.from_bytes(np.packbits(m).tobytes(), "big"), bk)], [])
+        return views[key]
+
+    def c(name, a=0, b=None, s=1, p=128):
+        return vw(name, ix[0:p, a:b:s])
+
+    def ind(win, off):
+        return (win[0].indirect(off[0]), win[1], off[1])
 
     def need(e, r, w):
         deps = []
-        for k in r:
-            deps += wr.get(k, [])
-            if k[0] == "B" and len(k) == 2 and k[1] in "0123456":
-                deps += [t for t in rd.get(k, []) if t[2] != e]
-        for k in w:
-            deps += wr.get(k, []) + rd.get(k, [])
+        for cells, write in ((r, False), (w, True)):
+            for name, p0, p1, m, bk in cells:
+                deps += [x[4] for x in acc.get(name, []) if (write or x[0]) and x[1] <= p1 and p0 <= x[2] and x[3] & m]
+                for b in bk:
+                    deps += [t for e2, t in banks.get(b, {}).items() if e2 != e]
         top = {}
         for s, val, who in deps:
-            if who == "p" and e == "p":
-                continue
-            top[s] = max(top.get(s, 0), val)
+            if not (who == "p" and e == "p"):
+                top[s] = max(top.get(s, 0), val)
         for s, val in top.items():
             if any(knew.get((s2, v2), {}).get(s, 0) >= val for s2, v2 in top.items() if s2 != s):
                 continue
@@ -86,542 +105,580 @@ def rank_program(g, core, T, topo):
             for s, val in knew.get(tok, {}).items():
                 seen[e][s] = max(seen[e].get(s, 0), val)
 
-    def note(tok, r, w, more=False, e=None):
+    def note(tok, r, w, e=None):
         if e:
             knew[tok[0:2]] = dict(seen[e])
-        for k in r:
-            rd.setdefault(k, []).append(tok)
-        for k in w:
-            wr[k] = (wr.get(k, []) if more else []) + [tok]
-            rd[k] = []
+        for cells, write in ((r, False), (w, True)):
+            for name, p0, p1, m, bk in cells:
+                L = acc.setdefault(name, [])
+                L[:] = [x for x in L if not ((write or (not x[0] and x[4][0] == tok[0]))
+                                             and p0 <= x[1] and x[2] <= p1 and not x[3] & ~m)]
+                L.append((write, p0, p1, m, tok))
+                for b in bk:
+                    banks.setdefault(b, {})[e] = tok
 
-    def op(e, fn, r, w):
-        if skip[0]:
-            return
-        r, w = r.split(), w.split()
+    def cells(out, ins):
+        ins = [x for x in ins if isinstance(x, tuple)]
+        return sum((x[1] + x[2] for x in ins), []) + out[2], out[1]
+
+    def op(e, fn, out, *ins):
+        r, w = cells(out, ins)
         need(e, r, w)
         cnt[e] += 1
         fn().then_inc(T.sem["s" + e], 1)
-        note(("s" + e, cnt[e], e), r, w, False, e)
+        note(("s" + e, cnt[e], e), r, w, e)
 
-    def dma(e, sem, out, in_, r, w):
-        r, w = r.split(), w.split()
-        need(e, r, w)
-        Q[e].dma_start(out, in_).then_inc(T.sem[sem], 16)
-        note((sem, 16, "d"), r, w)
+    def load(e, sem, out, src):
+        need(e, [], out[1])
+        Q[e].dma_start(out[0], src).then_inc(T.sem[sem], 16)
+        note((sem, 16, "d"), [], out[1])
 
-    def ts(out, in0, s1, s2, o0, o1, r, w):
+    def store(e, sem, dst, src):
+        need(e, src[1], [])
+        Q[e].dma_start(dst, src[0]).then_inc(T.sem[sem], 16)
+
+    def A(x):
+        return x[0] if isinstance(x, tuple) else x
+
+    def ts(out, a, s1, o0, s2=None, o1=None):
         if o1 is None:
-            op("v", lambda: g.vector.tensor_scalar(out, in0, s1, None, o0), r, w)
+            op("v", lambda: g.vector.tensor_scalar(out[0], a[0], A(s1), None, o0), out, a, s1)
         else:
-            op("v", lambda: g.vector.tensor_scalar(out, in0, s1, s2, o0, o1), r, w)
+            op("v", lambda: g.vector.tensor_scalar(out[0], a[0], A(s1), A(s2), o0, o1), out, a, s1, s2)
 
-    def tt(out, a, b, o, r, w):
-        op("v", lambda: g.vector.tensor_tensor(out, a, b, o), r, w)
+    def tt(out, a, b, o):
+        op("v", lambda: g.vector.tensor_tensor(out[0], a[0], b[0], o), out, a, b)
 
-    def cp(out, a, r, w):
-        op("v", lambda: g.vector.tensor_copy(out, a), r, w)
+    def cp(out, a):
+        op("v", lambda: g.vector.tensor_copy(out[0], a[0]), out, a)
 
-    def ms(out, c, w):
-        op("v", lambda: g.vector.memset(out, c), "", w)
+    def ms(out, k):
+        op("v", lambda: g.vector.memset(out[0], k), out)
 
-    def scan(out, a, b, ini, o0, o1, r, w):
-        op("v", lambda: g.vector.tensor_tensor_scan(out, a, b, ini, o0, o1), r, w)
+    def scan(out, a, b, ini, o0, o1):
+        op("v", lambda: g.vector.tensor_tensor_scan(out[0], a[0], b[0], A(ini), o0, o1), out, a, b, ini)
 
-    def act(out, a, r, w, f=AF.Identity, bias=0.0, scale=1.0):
-        op("a", lambda: g.scalar.activation(out, a, f, bias=bias, scale=scale), r, w)
+    def act(out, a, f=AF.Identity, bias=0.0, scale=1.0):
+        op("a", lambda: g.scalar.activation(out[0], a[0], f, bias=A(bias), scale=A(scale)), out, a, bias, scale)
 
-    def mm(out, l, rhs, st, sp, r, w):
-        op("p", lambda: g.tensor.matmul(out, l, rhs, st, sp), r, w)
+    def mm(out, l, rhs, st=True, sp=True):
+        op("p", lambda: g.tensor.matmul(out[0], l[0], rhs[0], st, sp), out, l, rhs)
 
-    def iota(out, pat, base, ch, w, flt=True):
+    def iota(out, pat, base, ch, flt=True):
         if flt:
-            op("g", lambda: g.iota(out, pat, base, ch, allow_small_or_imprecise_dtypes=True), "", w)
+            op("g", lambda: g.iota(out[0], pat, base, ch, allow_small_or_imprecise_dtypes=True), out)
         else:
-            op("g", lambda: g.iota(out, pat, base, ch), "", w)
+            op("g", lambda: g.iota(out[0], pat, base, ch), out)
 
-    def fill(name, a, b, val, w):
-        iota(T[name][:, a:b], [[0, b - a]], val, 0, w)
+    def fill(name, a, b, val):
+        iota(c(name, a, b), [[0, b - a]], val, 0)
 
-    def to_w(out, wname, src, r, w, first=True, last=True):
+    def to_w(out, wname, src, first=True, last=True):
         for k in range(16):
-            mm(out, T[wname][:, 15 - k:143 - k], src(k), first and k == 0, last and k == 15, r + " " + wname, w)
+            mm(out, c(wname, 15 - k, 143 - k), src(k), first and k == 0, last and k == 15)
 
-    def lane(t, o, a, b, s=1):
-        if t == 0:
-            return T[("X0", "X0", "V0", "N0")[o]][:, a:b:s]
-        return T["land%d" % t][:, 4 * a + o:4 * b:4 * s]
+    def base(t, o):
+        return ((X0, X0, 0, N0)[o], 1) if t == 0 else (LB + 1024 * (t - 1) + o, 4)
 
-    def lkey(t, o):
-        return ("X0", "X0", "V0", "N0")[o] if t == 0 else "land%d" % t
+    def lane(t, o, a=0, b=256, s=1):
+        z, st = base(t, o)
+        return c("V0" if (t, o) == (0, 2) else "GW", z + st * a, z + st * (b - 1) + 1, st * s)
 
     C = {}
 
     def col(n):
         if n not in C:
             C[n] = len(C)
-        return T.COL[:, C[n]:C[n] + 1]
+        return c("COL", C[n], C[n] + 1)
 
     def E(k):
-        return T.E16[:, k:k + 1]
-
-    def names(p, n):
-        return " ".join(p + str(k) for k in range(n))
-
-    dma("s", "d0", T.X0[:], T.wf[:], "", "X0")
-    dma("a", "d1", T.NI32[:], T.nm[:], "", "NI32")
-    dma("s", "d2", T.V0[:], T.wv[:], "", "V0")
-    dma("s", "d4", T.FW[:, 0:4096], T.rf[:], "", "FW")
-    dma("s", "d3", T.VW[:, 0:4096], T.rv[:], "", "VW")
-
-    iota(T.CI[:, 0:1], [[0, 1]], 0, 1, "CI0", False)
-    iota(T.QQ[:], [[1, 144]], 0, 0, "QQ")
-    iota(T.QG[:], [[1, 8], [0, 16]], 0, 0, "QG")
-    iota(T.TQ[:], [[1, 128]], 0, -1, "TQ")
-    iota(T.DQ[0:16, :], [[0, 16], [1, 16]], 0, -1, "DQ")
-    iota(T.CK[:], [[-4096, 16], [0, 16]], 15 * 4096, 0, "CK")
-    fill("NEG", 0, 128, -2 ** 17, "NEG")
-    fill("ONE", 0, 128, 4096, "ONE")
-    iota(T.QL[:], [[1, 8], [100, 2], [0, 8]], 0, 0, "QL")
-    fill("ST", 0, 192, 0, "ST")
-    fill("ST", 112, 128, 1, "ST")
-    fill("ST", 176, 192, -1, "ST")
-    iota(T.JN[:], [[1, 256]], 0, 0, "JN")
-    fill("SG", 0, 256, 0, "SG")
-    fill("ZR", 0, 256, 0, "ZR")
-    fill("VW", 4096, 4352, 0, "VWd")
-    fill("VW", 4352, 4608, TOP, "VWt")
-    fill("GW", 4096, 4352, 0, "GWd")
-    fill("FW", 4096, 4352, 0, "FWd")
-    for n in ("NX", "NY", "NV", "NN"):
-        fill(n, 256, 272, 0, n + "z")
-    fill("inv1", 256, 512, 256, "inv1")
-    fill("EE", 0, 768, 0, names("EE", 16))
-    fill("inv2", 256, 512, 256, "inv2")
-    fill("inv3", 256, 512, 256, "inv3")
-
-    for k in range(16):
-        ms(T.TAB[:, k:k + 1], float(8 * WA[k] + WB[k]), "TAB%d" % k)
-    ts(T.CI[:, 1:2], T.CI[:, 0:1], 15, None, OP.bitwise_and, None, "CI0", "CI1")
-    ts(T.CI[:, 2:3], T.CI[:, 0:1], 4, None, OP.arith_shift_right, None, "CI0", "CI2")
-    col("R"), col("G")
-    cp(T.COL[:, 0:2], T.CI[:, 1:3], "CI1 CI2", "R G")
-    ts(T.E16[:], T.QQ[:, 0:16], col("R"), None, OP.is_equal, None, "QQ R", "E16")
-    ts(T.BLK[:], T.QG[:], col("G"), None, OP.is_equal, None, "QG G", "BLK")
-    tt(T.SM[:, 0:16], T.TAB[:], T.E16[:], OP.mult, "E16 " + names("TAB", 16), "SMa")
-    tt(col("e23"), E(2), E(3), OP.add, "E16", "e23")
-    op("v", lambda: g.vector.tensor_reduce(col("AB"), T.SM[:, 0:16], AX.X, OP.add), "SMa", "AB")
-    ts(col("lo"), col("R"), 1.0, 3.0, OP.min, OP.mult, "R", "lo")
-    cp(T.CI[:, 3:4], col("AB"), "AB", "CI3")
-    ts(col("lt4"), col("R"), 4.0, None, OP.is_lt, None, "R", "lt4")
-    ts(T.CI[:, 4:5], T.CI[:, 3:4], 3, None, OP.arith_shift_right, None, "CI3", "CI4")
-    ts(T.TT[:], T.TQ[:], 3.0, None, OP.is_le, None, "TQ", "TT")
-    cp(col("A"), T.CI[:, 4:5], "CI4", "A")
-    ts(T.PB[:], T.TQ[:], col("lo"), col("lt4"), OP.is_ge, OP.mult, "TQ lo lt4", "PB")
-    ts(T.D1[0:16, :], T.DQ[0:16, :], 0.0, None, OP.is_equal, None, "DQ", "D1")
-    tt(T.P0[:], T.TT[:], T.PB[:], OP.mult, "TT PB", "P0")
-    cp(T.NB[:], T.NI32[:], "NI32", "NB")
-    act(col("g15"), col("G"), "G", "g15", scale=16.0, bias=15.0)
-    act(col("c1"), col("e23"), "e23", "c1", scale=-254.0, bias=255.0)
-    act(col("sg"), E(3), "E16", "sg", scale=-2.0, bias=1.0)
-    act(col("n0"), E(0), "E16 e23", "n0", scale=2.0, bias=col("e23"))
-    act(T.NW[:, 8:16], T.BLK[:, 0:128:16], "BLK E16", "NW1", scale=E(2))
-    act(T.NW[:, 16:24], T.BLK[:, 0:128:16], "BLK E16", "NW2", scale=E(3))
-    act(T.NW[:, 0:8], T.BLK[:, 0:128:16], "BLK n0", "NW0", scale=col("n0"))
-    act(T.AB8[:, 0:8], T.BLK[:, 0:128:16], "BLK A", "AB8", scale=col("A"))
-    act(T.BW[:], T.BLK[:], "BLK E16", "BW", scale=E(2))
-    act(T.ON16[0:16, :], T.TQ[0:16, :], "TQ", "ON16", scale=0.0, bias=2048.0)
-    for m in range(16):
-        act(T.DK[0:16, 16 * m:16 * m + 16], T.D1[0:16, 0:16], "D1", "DK%d" % m, scale=float(KP[m]))
-    dk = names("DK", 16)
-    mm(T.B1[:, 0:256], T.BLK[:], T.X0[:], True, True, "BLK X0", "B1")
-    mm(T.B2[:, 0:256], T.P0[:], T.NB[:], True, True, "P0 NB", "B2")
-    ts(T.B1[:, 256:512], T.B1[:, 0:256], 0.0, col("sg"), OP.is_gt, OP.mult, "B1 sg", "B1")
-    ts(T.BB[:], T.B2[:, 0:256], col("c1"), E(3), OP.min, OP.subtract, "B2 c1 E16", "BB")
-    tt(T.N0[:], T.B1[:, 256:512], T.BB[:], OP.mult, "B1 BB", "N0")
-    ts(T.ID[:], T.TQ[:], 0.0, None, OP.is_equal, None, "TQ", "ID")
-    ts(col("lt8"), col("R"), 8.0, None, OP.is_lt, None, "R", "lt8")
-    ts(T.W1[:], T.QQ[:], col("g15"), None, OP.is_equal, None, "QQ g15", "W1")
-    act(col("da"), E(4), "E16", "da", scale=-4.0)
-    act(col("d2"), E(1), "E16", "d2", scale=-1.0, bias=E(2))
-    act(col("db"), E(5), "E16 da", "db", scale=-1.0, bias=col("da"))
-    act(col("r8"), col("R"), "R", "r8", scale=-0.125, bias=0.0625)
-    act(col("d1"), E(6), "E16 db", "d1", scale=-1.0, bias=col("db"))
-    ts(T.S2[:], T.TQ[:], col("d2"), col("R"), OP.is_equal, OP.min, "TQ d2 R", "S2")
-    ts(T.S1[:], T.TQ[:], col("d1"), col("R"), OP.is_equal, OP.min, "TQ d1 R", "S1")
-    for k, (a, b) in enumerate(((64.0, 72.0), (60.0, 104.0))):
-        d = (T.DW, T.DF)[k]
-        act(d[0:16, 0:128], T.D1[0:16, 0:128], "D1", "DW%da" % k, scale=a)
-        act(d[0:16, 128:256], T.D1[0:16, 0:128], "D1", "DW%db" % k, scale=b)
-
-    def late_constants():
-        ts(T.REP[:], T.QQ[:, 0:16], 0.0, col("R"), OP.mult, OP.add, "QQ R", "REP")
-        cp(T.DIV[:], T.QQ[:, 0:16], "QQ", "DIV")
-        ts(T.TRN[:], T.QQ[:, 0:16], col("r16"), None, OP.add, None, "QQ r16", "TRN")
-        ts(T.END[:], T.REP[:], 16.0, 15.0, OP.mult, OP.add, "REP", "END")
-        ts(T.RB[:], T.QL[:], col("G"), col("b8"), OP.is_equal, OP.mult, "QL G b8", "RB")
-        ms(T.SG[:, 0:256:16], -float(2 ** 60), "SG")
-
-    def early_constants():
-        act(col("wz"), E(2), "E16", "wz", scale=-256.0, bias=E(4))
-        act(col("wr"), col("lt8"), "E16 lt8", "wr", scale=8.0, bias=E(8))
-        act(col("rb"), col("lt8"), "lt8 r8", "rb", scale=col("r8"))
-        act(col("i0"), col("lt8"), "lt8", "i0", scale=256.0625, bias=-257.0)
-        act(col("nA"), col("A"), "A", "nA", scale=-1.0)
-        act(T.JW[:, 48:64], T.QQ[:, 0:16], "QQ R", "JW", scale=16.0, bias=col("R"))
-        act(col("r16"), col("R"), "R", "r16", scale=16.0)
-        act(col("ini"), col("rb"), "i0 rb", "ini", scale=-1.0, bias=col("i0"))
-        act(col("b8"), col("AB"), "AB nA", "b8", scale=0.125, bias=col("nA"))
-        act(T.W16[:], T.W1[:], "W1", "W16", scale=65536.0)
-        act(T.WZ[:], T.W1[:], "W1 wz", "WZ", scale=col("wz"))
-        act(T.W8[:], T.W1[:], "W1", "W8", scale=8192.0)
-        tail_constants2(0, 16)
-        act(T.NI[:], T.ID[:], "ID", "NI", scale=-1.0)
-        act(T.RN[:], T.BW[:], "BW", "RN", scale=-0.0625)
-        act(T.CT[:], T.JN[:], "JN rb", "CT", scale=0.0, bias=col("rb"))
-        act(T.WR[:], T.W1[:], "W1 wr", "WR", scale=col("wr"))
-        J = T.JW[:, 48:64]
-        for a, sc, bi in ((32, 1.0, YO), (48, 3.0, NO + 1), (80, 1.0, YO), (96, -1.0, -YO), (128, 1.0, XO), (144, 1.0, XO)):
-            act(T.ST[:, a:a + 16], J, "JW ST", "ST%d" % a, scale=sc, bias=float(bi))
-
-    def tail_constants():
-        J = T.JW[:, 48:64]
-        for k in range(3):
-            act(T.JW[:, 16 * k:16 * k + 16], J, "JW", "DJ%d" % k, bias=4096.0)
-        for k in range(16):
-            act(T.BR[:, 128 * k:128 * k + 128], T.BLK[:], "BLK E16", "BR%d" % k, scale=E(k))
-
-    def tail_constants2(a, b):
-        for k in range(a, b):
-            op("g", lambda: g.affine_select(T.TRI[:, 128 * k:128 * k + 128], T.W8[:, 15 - k:143 - k], [[1, 128]],
-                                            OP.is_gt, 0.0, 0, -1), "W8", "TRI%d" % k)
-
-    st = "ST ST32 ST48 ST80 ST96 ST128 ST144"
-    XJ, DJ = T.ST[:, 128:144], T.JW[:, 0:16]
-    calls = plan(core, cores, topo)
-    comes = sum(len(es) for q in range(N) if q != me for c in plan(cores[q], cores, topo) for d, es in c if d == me)
-    where = {"EQ": ((T.B3, "B3", 0), (T.B4, "B4", 0)), "OV": ((T.B3, "B3", 128), (T.B5, "B5", 0)),
-             "LO": ((T.B1, "B1", 0), (T.B2, "B2", 0))}
+        return c("E16", k, k + 1)
 
     def sm(k):
-        return T.SM[:, 16 * k:16 * k + 16]
+        return c("SM", 16 * k, 16 * k + 16)
+
+    def rows(name, a, b, s=1):
+        return vw(name, ix[:, a:b:s, :])
+
+    load("s", "d0", c("GW", X0, X0 + 256), T.wf[:])
+    load("a", "d1", c("NI32"), T.nm[:])
+    load("s", "d2", c("V0"), T.wv[:])
+    load("s", "d4", c("FW", 0, 4096), T.rf[:])
+    load("s", "d3", c("VW", 0, 4096), T.rv[:])
+    load("s", "d5", c("GW", 0, 4096), T.rg[:])
+
+    iota(c("DQ", 0, 16, 1, 32), [[1, 16]], 0, -1)
+    ms(vw("DQ", ix[32:33, 0:16]), 0.0)
+    ms(vw("KS", ix[32:33, :]), 0.0)
+    iota(c("CI", 0, 1), [[0, 1]], 0, 1, False)
+    iota(c("QQ"), [[1, 144]], 0, 0)
+    iota(c("QG"), [[1, 8], [0, 16]], 0, 0)
+    iota(c("TQ"), [[1, 128]], 0, -1)
+    iota(c("KS", p=32), [[1, 16], [0, 16]], 0, -1)
+    iota(c("CK"), [[0, 16], [-4096, 16]], 15 * 4096, 0)
+    fill("NEG", 0, 128, -2 ** 17)
+    fill("ONE", 0, 256, 4096)
+    iota(c("QK"), [[1, 36], [0, 4]], 0, 0)
+    fill("ST", 0, 160, 0)
+    fill("ST", 32, 48, 256)
+    fill("ST", 96, 112, VT)
+    fill("PP", 0, 16, 0)
+    fill("SG", 0, 128, 0)
+    iota(c("JN"), [[1, 256]], 0, 0)
+    fill("ZR", 0, 48, 0)
+    fill("VW", 4096, VT, 0)
+    fill("VW", VT, VT + 16, TOP)
+    fill("GW", 4096, 4352, 0)
+    fill("FW", 4096, 4352, 0)
+    for o in range(4):
+        fill("N4", 272 * o + 256, 272 * o + 272, 0)
+    fill("inv1", 0, 256, 256)
+
+    for k in range(16):
+        ms(c("TAB", k, k + 1), float(8 * WA[k] + WB[k]))
+        if k == 1:
+            ts(c("DQ", 16, 32, 1, 33), c("DQ", 0, 16, 1, 33), 0.0, OP.is_equal)
+            for m in range(8):
+                act(c("DK", m, 256, 16, 33), c("DQ", 16, 32, 1, 33), scale=float(KP[m]))
+    ts(c("CI", 1, 2), c("CI", 0, 1), 15, OP.bitwise_and)
+    ts(c("CI", 2, 3), c("CI", 0, 1), 4, OP.arith_shift_right)
+    ts(c("CI", 5, 6), c("CI", 0, 1), 7, OP.bitwise_and)
+    ts(c("CI", 6, 7), c("CI", 0, 1), 3, OP.bitwise_and)
+    col("R"), col("G"), col("R8"), col("R4")
+    cp(c("COL", 0, 2), c("CI", 1, 3))
+    cp(c("COL", 2, 4), c("CI", 5, 7))
+    ts(c("E16"), c("QQ", 0, 16), col("R"), OP.is_equal)
+    ts(c("BLK"), c("QG"), col("G"), OP.is_equal)
+    tt(sm(0), c("TAB"), c("E16"), OP.mult)
+    tt(col("e23"), E(2), E(3), OP.add)
+    op("v", lambda: g.vector.tensor_reduce(col("AB")[0], sm(0)[0], AX.X, OP.add), col("AB"), sm(0))
+    ts(col("lo"), col("R"), 1.0, OP.min, 3.0, OP.mult)
+    cp(c("CI", 3, 4), col("AB"))
+    ts(col("lt4"), col("R"), 4.0, OP.is_lt)
+    ts(c("CI", 4, 5), c("CI", 3, 4), 3, OP.arith_shift_right)
+    ts(c("TT"), c("TQ"), 3.0, OP.is_le)
+    cp(col("A"), c("CI", 4, 5))
+    ts(c("PB"), c("TQ"), col("lo"), OP.is_ge, col("lt4"), OP.mult)
+    tt(c("P0"), c("TT"), c("PB"), OP.mult)
+    cp(c("NB"), c("NI32"))
+    blk8 = c("BLK", 0, 128, 16)
+    act(col("c1"), col("e23"), scale=-254.0, bias=255.0)
+    act(col("sg"), E(3), scale=-2.0, bias=1.0)
+    act(c("AB8", 0, 8), blk8, scale=col("A"))
+    act(col("n0"), E(0), scale=2.0, bias=col("e23"))
+    act(col("ne"), E(2), scale=5.0, bias=E(3))
+    act(col("no"), E(3), scale=20.0)
+    act(col("bw"), E(2), scale=256.0)
+    for k, w in enumerate((col("n0"), col("ne"), col("no"), E(2))):
+        act(c("NW", 8 * k, 8 * k + 8), blk8, scale=w)
+    act(c("BW"), c("BLK"), scale=col("bw"))
+    act(c("UB", p=33), c("KS", p=33), scale=0.0, bias=2048.0)
+    for m in range(8, 16):
+        act(c("DK", m, 256, 16, 33), c("DQ", 16, 32, 1, 33), scale=float(KP[m]))
+    mm(c("Pa", 0, 256), c("BLK"), lane(0, 1))
+    mm(c("Pb", 0, 256), c("P0"), c("NB"))
+    ts(c("Pa", 256, 512), c("Pa", 0, 256), 0.0, OP.is_gt, col("sg"), OP.mult)
+    ts(c("BB"), c("Pb", 0, 256), col("c1"), OP.min, E(3), OP.subtract)
+    ts(c("ID"), c("TQ"), 0.0, OP.is_equal)
+    tt(lane(0, 3), c("Pa", 256, 512), c("BB"), OP.mult)
+    ts(c("D1", p=33), c("KS", p=33), 0.0, OP.is_equal)
+    ts(col("g15"), col("G"), 16.0, OP.mult, 15.0, OP.add)
+    ts(c("DE", p=16), c("D1", p=16), 2 * HG, OP.mult)
+    ts(c("W1"), c("QQ"), col("g15"), OP.is_equal)
+    ts(c("DO", p=16), c("D1", p=16), HG, OP.mult)
+    J, DJ, DP = c("JW", 48, 64), c("JW", 0, 16), c("JW", 64, 80)
+
+    def probe_constants():
+        ts(c("WE"), c("W1"), 2 * HG, OP.mult)
+        ts(c("W16"), c("W1"), 65536.0, OP.mult)
+        ts(c("WO"), c("W1"), HG, OP.mult)
+
+    def early_constants():
+        act(col("da"), E(4), scale=-4.0)
+        act(col("d2"), E(1), scale=-1.0, bias=E(2))
+        act(col("db"), E(5), scale=-1.0, bias=col("da"))
+        act(col("wz"), E(2), scale=-256.0, bias=E(4))
+        act(col("d1"), E(6), scale=-1.0, bias=col("db"))
+        act(c("O16"), c("TQ"), scale=0.0, bias=1.0)
+        act(c("W8"), c("W1"), scale=8192.0)
+        for k in range(16):
+            out, src = c("BR", 128 * k, 128 * k + 128), c("O16")
+            op("g", lambda: g.affine_select(out[0], src[0], [[-16, 8], [0, 16]], OP.is_equal, 0.0, -k, 1), out, src)
+        fill("EE", 0, 768, 0)
+        for k in range(16):
+            out, src = c("TRI", 128 * k, 128 * k + 128), c("W8", 15 - k, 143 - k)
+            op("g", lambda: g.affine_select(out[0], src[0], [[1, 128]], OP.is_gt, 0.0, 0, -1), out, src)
+        act(J, c("QQ", 0, 16), scale=16.0, bias=col("R"))
+        act(col("g3"), col("G"), scale=4.0, bias=3.0)
+        act(c("WZ"), c("W1"), scale=col("wz"))
+        act(c("ST", 80, 96), J, bias=float(N1))
+        lane_offsets(0)
+        act(col("nA"), col("A"), scale=-1.0)
+        act(col("rb"), col("R8"), scale=-0.125, bias=0.0625)
+        act(c("RN"), c("BW"), scale=-0.0625 / 256)
+        act(col("b8"), col("AB"), scale=0.125, bias=col("nA"))
+        act(c("CT"), c("TQ"), scale=0.0, bias=col("rb"))
+        act(col("d8"), col("R8"), scale=-1.0, bias=col("R"))
+        act(c("RB"), c("BLK"), scale=col("b8"))
+
+    def tail_constants():
+        act(col("ini"), col("R8"), scale=32.0, bias=-1.0)
+        act(col("c8"), col("d8"), scale=128.0, bias=32.0)
+        act(col("wr"), col("d8"), scale=255.875, bias=-1023.0)
+        act(col("cap"), col("c8"), bias=col("ini"))
+        act(c("WR"), c("W1"), scale=col("wr"))
+        act(c("CAP"), c("TQ"), scale=0.0, bias=col("cap"))
+        act(DP, J, bias=256.0)
+        act(col("o4"), col("R4"), scale=272.0)
+        for k in range(3):
+            act(c("JW", 16 * k, 16 * k + 16), J, bias=4096.0)
+
+    def late_constants():
+        ts(c("S2"), c("TQ"), col("d2"), OP.is_equal, col("R"), OP.min)
+        ts(c("S1"), c("TQ"), col("d1"), OP.is_equal, col("R"), OP.min)
+        ts(c("REP"), c("QQ", 0, 16), 0.0, OP.mult, col("R"), OP.add)
+        cp(c("DIV"), c("QQ", 0, 16))
+        ts(c("WK"), c("QK"), col("g3"), OP.is_equal, E(0), OP.mult)
+        ts(c("END"), c("REP"), 16.0, OP.mult, 15.0, OP.add)
+        ms(c("SG", 0, 128, 16), -float(2 ** 60))
+
+    def lane_offsets(t):
+        if t == 0:
+            for a, z in ((112, X0), (128, X0), (144, N0)):
+                act(c("ST", a, a + 16), J, bias=float(z))
+        else:
+            act(c("ST", 112, 160), c("J3"), bias=float(base(t, 0)[0]))
+        y, st = base(t, 0)
+        for a, sg in ((0, 1.0), (16, -1.0), (64, 1.0)):
+            act(c("ST", a, a + 16), J, scale=sg * st, bias=sg * y)
+
+    calls = plan(core, cores, topo)
+    comes = sum(len(es) for q in range(N) if q != me for cl in plan(cores[q], cores, topo) for d, es in cl if d == me)
+    K3, E3, O3 = rows("PK", 0, 16), rows("PE", 0, 16), rows("PO", 0, 16)
+
+    def write(t, order):
+        for n, b in order:
+            o = {"FW": 1, "VW": 2, "GW": 0}[n]
+            cp(ind(c(n, 0, 4352), c("CU", 4 * b, 4 * b + 4)), lane(t, o, 64 * b, 64 * b + 64))
 
     for t in range(RO):
         last = t == RO - 1
-        kx, ky, kv, kn = [lkey(t, o) for o in range(4)]
-        NM = lane(t, 3, 0, 256)
-
-        def versions():
-            mm(T.B2[:, 0:256], T.S1[:], NM, True, True, kn + " S1", "B2")
-            mm(T.B2[:, 256:512], T.S2[:], NM, True, True, kn + " S2", "B2")
-            act(T.GW[:, NO + 1:NO + 768:3], T.B2[:, 0:256], "B2", "NMW1")
-            act(T.GW[:, NO + 2:NO + 768:3], T.B2[:, 256:512], "B2", "NMW2")
+        NM = lane(t, 3)
         for k in range(16):
-            mm(T.B3[0:16, k:128:16], lane(t, 0, k, 256, 16), T.AB8[:, 0:8], True, True, kx + " AB8", "B3")
+            mm(c("Pa", k, 128, 16, 16), lane(t, 1, k, 256, 16), c("AB8", 0, 8))
         for k in range(16):
-            mm(T.B6[0:16, 128 + k:512:16], lane(t, 3, k, 256, 16), T.NW[:, 0:24], True, True, kn + " NW0 NW1 NW2", "B6")
-        mm(T.B5[:, 0:256], T.BW[:], NM, True, True, kn + " BW", "B5")
-        mm(T.B4[:, 0:256], T.ON16[0:16, :], T.DK[0:16, :], True, False, "ON16 " + dk, "B4")
-        mm(T.B4[:, 0:256], T.ON16[0:16, :], T.D1[0:16, :], False, False, "ON16 D1", "B4")
-        if not last:
-            act(T.GW[:, YO:YO + 256], lane(t, 1, 0, 256), ky, "GY")
-            act(T.GW[:, NO:NO + 768:3], NM, kn, "NMW0")
-            versions()
-        def write_g(b):
-            if t:
-                cp(T.GW[:, 0:4352].indirect(T.CU[:, 4 * b:4 * b + 4]), lane(t - 1, 1, 64 * b, 64 * b + 64),
-                   "CU " + lkey(t - 1, 1), "GW GWd")
-        for b in (3, 2, 1, 0):
-            write_g(b)
-        cp(T.SI[0:16, :], T.B3[0:16, 0:128], "B3", "SI")
-        ts(T.UI[0:16, 0:128], T.SI[0:16, :], 4095, None, OP.bitwise_and, None, "SI", "UI0")
-        tt(T.WI[0:16, :], T.UI[0:16, 0:128], T.B6[0:16, 128:256], OP.mult, "UI0 B6", "WI")
-        ts(T.UB[0:16, 0:128], T.UI[0:16, 0:128], 2048.0, None, OP.subtract, None, "UI0", "UBa")
-        mm(T.B4[:, 0:256], T.UB[0:16, 0:128], T.DK[0:16, :], False, False, "UBa " + dk, "B4")
-        ts(T.UI[0:16, 128:256], T.WI[0:16, :], 5, 4095, OP.arith_shift_right, OP.bitwise_and, "WI", "UI1")
-        ts(T.UB[0:16, 128:256], T.UI[0:16, 128:256], 2048.0, None, OP.subtract, None, "UI1", "UB")
-        mm(T.B4[:, 0:256], T.UB[0:16, 128:256], T.D1[0:16, :], False, True, "UB D1", "B4")
-        for k in range(4):
-            mm(T.B0[:, 256 * k:256 * k + 256], T.ID[:], lane(t, 2, 0, 256), True, True, kv + " ID", "B0")
-        act(T.FL[0:16, :], T.B6[0:16, 256:512], "B6", "FL")
+            mm(c("Pb", k, 128, 16, 16), lane(t, 3, k, 256, 16), c("NW", 0, 8))
+        for h, bk in enumerate(("PK", "PO")):
+            for m in range(4):
+                mm(rows(bk, m, 32, 4), c("ID"), lane(t, 1, 128 * h, 128 * h + 128), True, False)
+                mm(rows(bk, m, 32, 4), c("BW"), lane(t, 3, 128 * h, 128 * h + 128), False, True)
+            act(c("FQ", 512 * h, 512 * h + 512), rows(bk, 0, 32), AF.Relu, bias=-256.0)
+        hs = ((0, 64), (64, 128))
+        for a, b in hs:
+            cp(c("SI", a, b, 1, 16), c("Pa", a, b, 1, 16))
+        for a, b in hs:
+            ts(c("UI", a, b, 1, 16), c("SI", a, b, 1, 16), 4095, OP.bitwise_and)
+        for a, b in hs:
+            tt(c("WI", a, b, 1, 16), c("UI", a, b, 1, 16), c("Pb", a, b, 1, 16), OP.mult)
+        ts(c("UB", 0, 128, 1, 16), c("UI", 0, 128, 1, 16), 2048.0, OP.subtract)
+        mm(E3, c("UB", 0, 128, 1, 33), c("DK", p=33), True, False)
+        for a, b in hs:
+            ts(c("UI", 128 + a, 128 + b, 1, 16), c("WI", a, b, 1, 16), 5, OP.arith_shift_right, 4095, OP.bitwise_and)
+        for a, b in hs:
+            ts(c("UB", 128 + a, 128 + b, 1, 16), c("UI", 128 + a, 128 + b, 1, 16), 2048.0, OP.subtract)
+        mm(E3, c("UB", 128, 256, 1, 33), c("D1", p=33), False, True)
+        for k in range(16):
+            mm(c("Pb", 128 + k, 512, 16, 16), lane(t, 3, k, 256, 16), c("NW", 8, 32))
+        for m in range(4):
+            for h in range(2):
+                mm(rows("PV", 32 * h + m, 32 * h + 32, 4), c("ID"), lane(t, 2, 128 * h, 128 * h + 128))
+        act(c("FL", 0, 128, 1, 16), c("Pb", 128, 256, 1, 16), bias=-16.5)
+        act(c("FL", 128, 256, 1, 16), c("Pb", 256, 384, 1, 16), bias=-3.0)
+        if last:
+            act(c("FL", 256, 384, 1, 16), c("Pb", 256, 384, 1, 16), scale=2.0 ** -20, bias=-3.0 * 2.0 ** -20)
+            for h, bk in enumerate(("PK", "PO")):
+                act(c("GW", N1 + 128 * h, N1 + 128 * h + 128), rows(bk, 0, 32, 4), AF.Relu, bias=-256.0)
         if t == 0:
+            probe_constants()
             early_constants()
-        tt(T.GW[:, XO:XO + 256], lane(t, 0, 0, 256), T.B5[:, 0:256], OP.mult, kx + " B5", "GX")
-        need("s", ["GX"], ["FQ"])
-        for k in range(4):
-            g.sync.dma_start(T.FQ[:, 256 * k:256 * k + 256], T.GW[:, XO:XO + 256]).then_inc(T.sem.fq, 16)
-        note(("fq", 64 * (t + 1), "d"), ["GX"], ["FQ"])
-        if t == 0:
-            dma("s", "d5", T.GW[:, 0:4096], T.rg[:], "", "GW")
-        cp(T.H0[:], T.B4[:, 0:256], "B4", "H0")
-        ts(T.HI[:], T.H0[:], 4095, None, OP.bitwise_and, None, "H0", "HI")
-        cp(T.HU[:], T.HI[:], "HI", "HU")
-        if last:
-            act(T.VW[:, XO:XO + 256], T.B5[:, 0:256], "B5", "VWt", scale=float(TOP))
-        if t == 0:
-            late_constants()
-        if last:
-            where = {"EQ": ((T.B4, "B4", 0), (T.B4, "B4", 128)), "OV": ((T.B5, "B5", 0), (T.B5, "B5", 128)),
-                     "LO": ((T.B1, "B1", 0), (T.B1, "B1", 128))}
-            mm(T.B4[:, 0:256], T.FL[0:16, 128:256], T.DL[0:16, :], True, False, "FL DL", "B4")
-            mm(T.B5[:, 0:256], T.ID[:], T.ZR[:], True, False, "ID ZR", "B5")
-            mm(T.B1[:, 0:256], T.ID[:], T.CK[:], True, False, "ID CK", "B1")
-            for a in (0, 128):
-                mm(T.B4[:, a:a + 128], T.FL[0:16, 0:128], T.DW[0:16, 0:128], False, False, "FL DW0a", "B4")
-                mm(T.B5[:, a:a + 128], T.FL[0:16, 0:128], T.DW[0:16, 128:256], False, False, "FL DW0b", "B5")
-                mm(T.B1[:, a:a + 128], T.NEG[:], T.ONE[:], False, False, "NEG ONE", "B1")
-        skip[0] = last
-        for k, (a, b) in enumerate(((0, 0), (128, 1))):
-            fl, dw, r = T.FL[0:16, a:a + 128], (T.DW, T.DF)[b], "FL DW%da DW%db" % (b, b)
-            mm(T.B3[:, 0:256], fl, dw[0:16, :], k == 0, False, r, "B3")
-            mm(T.B4[:, 0:128], fl, dw[0:16, 0:128], k == 0, False, r, "B4")
-            mm(T.B5[:, 0:128], fl, dw[0:16, 128:256], k == 0, False, r, "B5")
-        for h in range(2):
-            bk, bn, c = where["LO"][h]
-            mm(bk[:, 0:128], T.ID[:], T.CK[:, 128 * h:128 * h + 128], True, False, "ID CK", bn)
-            mm(bk[:, 0:128], T.NEG[:], T.ONE[:], False, False, "NEG ONE", bn)
-        if not last:
-            to_w(T.B6[:, 0:16], "WZ", lambda k: lane(t, 3, k, 256, 16), kn, "B6")
+        ms_ = (ix[:, :, 0:4], ix[:, :, 4:16])
+        for s in ms_:
+            cp(vw("H0", s), vw("PE", ix[:, 0:16, s[2]]))
+        for s in ms_:
+            ts(vw("HI", s), vw("H0", s), 4095, OP.bitwise_and)
+
+        def hu(k):
+            cp(c("HU", 64 * k, 64 * k + 64), vw("HI", ix[:, :, 4 * k:4 * k + 4]))
+        hu(0); hu(1)
+        mm(E3, c("FL", 0, 128, 1, 16), c("DE", p=16), True, False)
+        mm(O3, c("FL", 128, 256, 1, 16), c("DO", p=16), True, False)
+        mm(K3, c("ID"), c("CK"), True, False)
+        mm(K3, c("NEG"), c("ONE"), False, False)
+
+        def ch(name, k):
+            return c(name, 1024 * k, 1024 * k + 1024)
+
+        def hk(k):
+            return c("HU", 64 * k, 64 * k + 64)
+
+        def sums(k, name, bank, wname, close=False):
+            to_w(vw(bank, ix[:, 0:16, 4 * k:4 * k + 4]), wname,
+                 lambda r: c(name, 1024 * k + r, 1024 * k + 1024, 16), False, close)
 
         def gv(k):
-            act(T.VG[:, 1024 * k:1024 * k + 1024], T.VW[:, 0:4096].indirect(T.HU[:, 64 * k:64 * k + 64]),
-                "VW HU", "VG%d" % k)
+            act(ch("VG", k), ind(c("VW", 0, 4096), hk(k)))
 
-        def sums(k, name, wname, close):
-            bk, bn, c = where[name][k // 2]
-            c += 64 * (k % 2)
-            to_w(bk[:, c:c + 64], wname, lambda r: T[name][:, 1024 * k + r:1024 * k + 1024:16],
-                 " ".join("%s%d%s" % (name, k, s) for s in "abcd"), bn, False, close)
-
-        def eq(k):
-            if k == 0 or (k == 1 and t == 0):
-                for m in range(4 * k, 4 * k + 4):
-                    tt(T.EQ[:, 256 * m:256 * m + 256], T.FW[:, 0:4096].indirect(T.HU[:, 16 * m:16 * m + 16]),
-                       T.GW[:, XO:XO + 256], OP.is_equal, "FW HU GX", "EQ%d%s" % (k, "abcd"[m % 4]))
-            else:
-                tt(T.EQ[:, 1024 * k:1024 * k + 1024], T.FW[:, 0:4096].indirect(T.HU[:, 64 * k:64 * k + 64]),
-                   T.FQ[:], OP.is_equal, "FW HU FQ", "EQ%da" % k)
+        def eq(k, close=False):
+            tt(ch("EQ", k), ind(c("FW", 0, 4096), hk(k)), c("FQ"), OP.is_equal)
+            sums(k, "EQ", "PE", "WE", close)
 
         def mn(k):
-            a = 1024 * k
-            tt(T.LO[:, a:a + 1024], T.VG[:, a:a + 1024], T.B0[:], OP.min, "VG%d B0" % k, "LO%da" % k)
-            sums(k, "LO", "W16", False)
+            tt(ch("LO", k), ch("VG", k), rows("PV", 0, 64), OP.min)
+            sums(k, "LO", "PK", "W16", k == 3)
 
         def sg(k):
-            act(T.OV[:, 1024 * k:1024 * k + 1024], T.LO[:, 1024 * k:1024 * k + 1024], "LO%da" % k,
-                "OV%da" % k, AF.Sign, bias=-TAU[t] - 0.5)
+            act(ch("OV", k), ch("LO", k), AF.Sign, bias=-TAU[t] - 0.5)
 
-        gv(0); gv(1); gv(2)
-        eq(0); sums(0, "EQ", "W1", False)
-        if t == 0:
-            eq(1); sums(1, "EQ", "W1", False); mn(0); sg(0); gv(3)
-        else:
-            mn(0); sg(0); gv(3); eq(1); sums(1, "EQ", "W1", False)
-        mn(1); sums(0, "OV", "W1", False); sg(1)
-        eq(2); sums(2, "EQ", "W1", False); mn(2); sums(1, "OV", "W1", True); sg(2)
-        mn(3); sums(2, "OV", "W1", False)
-        if not last:
-            ts(sm(0), T.B6[:, 0:16], -256.0, None, OP.is_equal, None, "B6", "z1")
-            tt(T.PD[:, 128:192], sm(0).indirect(T.REP[:, 0:4]), T.ST[:, 64:128], OP.mult, "z1 REP " + st, "zp")
-        sg(3); sums(3, "OV", "W1", True)
-        act(T.PEN[:, 0:256], T.B3[:, 0:256], "B3", "PENa", AF.Relu, bias=76.0 * BIG, scale=-BIG)
-        act(T.PEN[:, 256:384], T.B5[:, 0:128], "B5", "PENb", AF.Relu, bias=76.0 * BIG, scale=-BIG)
-        eq(3)
-        for i in range(2):
-            mm(T.B1[:, 0:128], T.NI[:], T.PEN[:, 128 * i:128 * i + 128], False, i == 1, "NI PENa", "B1")
-        act(T.KS[:, 0:128], T.B1[:, 0:128], "B1", "KSa")
-        sums(3, "EQ", "W1", True)
-        mm(T.B2[:, 0:128], T.NI[:], T.PEN[:, 256:384], False, True, "NI PENb", "B2")
-        if t == 0:
-            tail_constants()
-        cp(T.HT[:], T.HI[:].indirect(T.TRN[:]), "HI TRN", "HT")
-        if not last:
-            tt(T.PD[:, 0:64], T.PD[:, 128:192], T.ST[:, 0:64], OP.add, "zp " + st, "PP")
-            tt(T.PD[:, 64:128], T.ST[:, 128:192], T.PD[:, 128:192], OP.subtract, "zp " + st, "DD")
-        ts(T.PB[:], T.B4[:, 0:128], 76.0, -BIG, OP.is_lt, OP.mult, "B4", "PB")
-        tt(T.KS[:, 128:256], T.B2[:, 0:128], T.PB[:], OP.add, "B2 PB", "KSb")
-        if not last:
-            mm(T.B4[:, 0:256], T.ID[:], T.CT[:], True, False, "ID CT", "B4")
-            mm(T.B4[:, 0:256], T.RN[:], NM, False, False, kn + " RN", "B4")
-        cp(T.KT[:], T.KS[:].indirect(T.TRN[:]), "KSa KSb TRN", "KT")
-        scan(T.B3[:, 0:256], T.SG[:], T.KT[:], 0.0, OP.add, OP.max, "SG KT", "B3")
-        tt(T.B5[:, 0:256], T.B3[:, 0:256], T.KT[:], OP.subtract, "B3 KT", "B5")
-        M = T.B3[:, 15:256:16]
-        ts(sm(1), M, T0 + 409600.0, None, OP.is_lt, None, "B3", "nh")
-        act(sm(8), M, "B3", "off", AF.Abs, bias=-(T0 + 32768.0))
-        act(sm(9), sm(8), "off", "far", AF.Relu, bias=-40000.0)
-        tt(T.BT[:], T.HT[:], T.B5[:, 0:256], OP.subtract, "HT B5", "BT")
-        tt(T.OO[:, 64:128], sm(1).indirect(T.REP[:, 0:4]), T.PD[:, 64:128], OP.mult, "nh REP DD", "o2")
-        scan(T.SS[:], T.B5[:, 0:256], T.BT[:], 0.0, OP.min, OP.max, "B5 BT", "S")
-        tt(T.OO[:, 64:128], T.OO[:, 64:128], T.PD[:, 0:64], OP.add, "o2 PP", "o2")
-        S = T.SS[:, 15:256:16]
-        skip[0] = False
-        pb, pn = (T.B3, "B3") if last else (T.B1, "B1")
+        def so(k, close=False):
+            sums(k, "OV", "PO", "WO", close)
 
-        def claim_places():
-            tt(sm(10), sm(9), DJ, OP.min, "far DJ0", "dcc")
-            tt(T.LT4[:, 48:64], sm(10), S, OP.max, "dcc S", "pl")
-            ts(T.PL16[:], T.LT4[:, 48:64], 4096.0, 2048.0, OP.min, OP.subtract, "pl", "PL16")
-            act(sm(12), T.PL16[:], "PL16", "pl32")
+        def ov(k, close=False):
+            ts(ch("OV", k), ch("LO", k), float(TAU[t]), OP.is_gt, 0.5, OP.subtract)
+            sums(k, "OV", "PO", "WE", close)
+
+        def names_up():
+            to_w(c("Pc", 256, 272), "WZ", lambda k: lane(t, 3, k, 256, 16))
+            act(c("FL", 256, 384, 1, 16), c("Pb", 384, 512, 1, 16), scale=-2.0 ** -27, bias=2.0 ** -27)
+            mm(c("Pb", 0, 256), c("S1"), NM)
+            mm(c("Pb", 256, 512), c("S2"), NM)
+
+        hv = ((0, 128), (128, 256))
+
+        def best(k3, miss, other):
+            for a, b in hv:
+                tt(c("KK", a, b), rows(k3, a // 16, b // 16), c("KO", a, b), OP.min)
+            for a, b in hv:
+                scan(c("Pa", a, b), c("SG"), c("KK", a, b), 0.0, OP.add, OP.max)
+            for a, b in hv:
+                tt(c("Pb", a, b), c("Pa", a, b), c("KK", a, b), OP.subtract)
+                if a == 0:
+                    ts(sm(1), c("Pa", 15, 256, 16), -1.0, OP.mult, T0 + 409600.0, OP.add)
+            for a, b in hv:
+                tt(c("BT", a, b), rows("HI", a // 16, b // 16), c("Pb", a, b), OP.subtract)
+                if a == 0:
+                    miss()
+            for a, b in hv:
+                scan(c("SS", a, b), c("Pb", a, b), c("BT", a, b), 0.0, OP.min, OP.max)
+                if a == 0:
+                    other()
+
+        def claim_places(S):
+            tt(sm(10), sm(9), DJ, OP.min)
+            tt(c("LT4", 48, 64), sm(10), S, OP.max)
+            ts(c("PL16"), c("LT4", 48, 64), 4096.0, OP.min, 2048.0, OP.subtract)
 
         def claim_rows():
+            act(sm(12), c("PL16"))
             for k in range(16):
-                mm(pb[:, k:256:16], T.BR[:, 128 * k:128 * k + 128], T.PL16[:], True, True, "PL16 BR%d" % k, pn)
+                mm(c("Pc", k, 256, 16), c("BR", 128 * k, 128 * k + 128), c("PL16"))
+            act(c("PN"), c("Pc", 0, 256))
 
-        def claim_early():
-            by_act = (1, 2, 5, 6, 10, 14)
-            for i, c in enumerate(by_act):
-                a, b = 16 * c + 16, 64 * (c // 4) + 64
-                act(T.DF2[:, 32 * i:32 * i + b - a], T.PN[:, a:b], "PN pl32", "ab%d" % c,
-                    AF.Abs, bias=T.SM[:, 192 + c:193 + c], scale=-1.0)
-            for i, c in enumerate(by_act):
-                a, b = 16 * c + 16, 64 * (c // 4) + 64
-                act(T.EE[:, 256 * (c % 4) + a:256 * (c % 4) + b], T.DF2[:, 32 * i:32 * i + b - a], "ab%d" % c,
-                    "EE%d" % c, AF.Relu, bias=8192.0, scale=-8192.0)
-            tt(T.EE[:, 768:1024], sm(12).indirect(T.DIV[:]), T.PN[:], OP.is_equal, "pl32 DIV PN", "EE16")
-            mm(T.B2[:, 0:48], T.ID[:], T.ZR[:, 0:48], True, False, "ID ZR", "B2")
+        def pair(cc):
+            return 16 * cc + 16, 64 * (cc // 4) + 64, 256 * (cc % 4), c("SM", 192 + cc, 193 + cc)
+
+        def pairs_a(cs):
+            for i, cc in enumerate(cs):
+                a, b, s, pl = pair(cc)
+                act(c("DF2", 48 * i, 48 * i + b - a), c("PN", a, b), AF.Abs, bias=pl, scale=-1.0)
+            for i, cc in enumerate(cs):
+                a, b, s, pl = pair(cc)
+                act(c("EE", s + a, s + b), c("DF2", 48 * i, 48 * i + b - a), AF.Relu, bias=8192.0, scale=-8192.0)
+
+        def pairs_v(cs):
+            for cc in cs:
+                a, b, s, pl = pair(cc)
+                ts(c("EE", s + a, s + b), c("PN", a, b), pl, OP.is_equal, 8192.0, OP.mult)
+
+        def claim_same():
+            tt(c("EE", 768, 1024), ind(sm(12), c("DIV")), c("PN"), OP.is_equal)
+            mm(c("Pb", 0, 48), c("ID"), c("ZR"), True, False)
             for k in range(16):
-                mm(T.B2[:, 0:16], T.TRI[:, 128 * k:128 * k + 128], T.EE[:, 768 + k:1024:16], False, False,
-                   "EE16 TRI%d" % k, "B2")
+                mm(c("Pb", 0, 16), c("TRI", 128 * k, 128 * k + 128), c("EE", 768 + k, 1024, 16), False, False)
 
-        def claim_pairs(cs):
-            for c in cs:
-                a, b = 16 * c + 16, 64 * (c // 4) + 64
-                s = 256 * (c % 4)
-                ts(T.EE[:, s + a:s + b], T.PN[:, a:b], T.SM[:, 192 + c:193 + c], 8192.0, OP.is_equal, OP.mult,
-                   "PN pl32", "EE%d" % c)
-
-        def claim_rest(cs):
-            claim_pairs(cs)
-            to_w(T.B2[:, 0:48], "W1", lambda r: T.EE[:, r:768:16], names("EE", 16), "B2", False, True)
+        def claim_sum():
+            to_w(c("Pb", 0, 48), "W1", lambda r: c("EE", r, 768, 16), False, True)
 
         def claim_writes():
-            tt(T.LT4[:, 0:48], T.B2[:, 0:48], T.JW[:, 0:48], OP.min, "B2 DJ0 DJ1 DJ2", "l4")
-            tt(T.LT2[:], T.LT4[:, 0:32], T.LT4[:, 32:64], OP.max, "l4 pl", "l2")
-            tt(sm(13), T.LT2[:, 0:16], T.LT2[:, 16:32], OP.max, "l2", "l1")
-            cp(T.CU[:], sm(13), "l1", "CU")
+            tt(c("LT4", 0, 48), c("Pb", 0, 48), c("JW", 0, 48), OP.min)
+            tt(c("LT2"), c("LT4", 0, 32), c("LT4", 32, 64), OP.max)
+            tt(sm(13), c("LT2", 0, 16), c("LT2", 16, 32), OP.max)
+            cp(c("CU"), sm(13))
 
-        def write(order):
-            for n, b in order:
-                o = {"FW": 0, "VW": 2, "GW": 1}[n]
-                cp(T[n][:, 0:4352].indirect(T.CU[:, 4 * b:4 * b + 4]), lane(t, o, 64 * b, 64 * b + 64),
-                   "CU " + lkey(t, o), n + " " + n + "d")
-
-        def zsum(n, bk, bn, a, b):
+        def zsum(n, out, a=0, b=32):
             for k in range(a, b):
-                mm(bk, T.ID[:], T[n][:, 128 * k:128 * k + 128], k == 0, k == 31, "ID " + n, bn)
+                mm(out, c("ID"), c(n, 128 * k, 128 * k + 128), k == 0, k == 31)
 
-        def zout(bk, bn, z, out, sem):
-            act(T[z][:], bk, bn, z)
-            dma("s", sem, out[:], T[z][:], z, "out" + z)
+        def zout(src, z, out, sem):
+            act(c(z), src)
+            store("s", sem, out[:], c(z))
 
         if last:
-            for k in range(4):
-                gv(k); eq(k); sums(k, "EQ", "W1", k == 3)
-                if k == 0:
-                    cp(T.HT[:], T.HI[:].indirect(T.TRN[:]), "HI TRN", "HT")
-            tt(T.BT[:], T.HI[:], T.CK[:], OP.add, "HI CK", "BT")
-            ts(T.B3[:, 0:256], T.B4[:, 0:256], 215.5, 131072.0, OP.subtract, OP.mult, "B4", "B3")
-            act(T.PEN[:, 0:256], T.B4[:, 0:256], "B4", "PENa", AF.Relu, bias=76.0 * BIG, scale=-BIG)
-            tt(T.SS[:], T.B3[:, 0:256], T.BT[:], OP.min, "B3 BT", "S")
-            tt(T.KT[:, 0:128], T.SS[:, 0:128], T.SS[:, 128:256], OP.max, "S", "KT")
-            tt(T.SS[:, 0:64], T.KT[:, 0:64], T.KT[:, 64:128], OP.max, "KT", "S")
-            tt(T.KT[:, 0:32], T.SS[:, 0:32], T.SS[:, 32:64], OP.max, "S", "KT")
-            tt(T.CI[:], T.KT[:, 0:16], T.KT[:, 16:32], OP.max, "KT", "CIa")
-            ts(sm(9), T.CI[:], -1.0, None, OP.mult, None, "CIa", "far")
-            ts(T.RI[:, 0:16], T.CI[:], 4095, None, OP.bitwise_and, None, "CIa", "RI")
-            tt(sm(10), sm(9), DJ, OP.min, "far DJ0", "dcc")
-            tt(T.LT4[:, 48:64], sm(10), T.RI[:, 0:16], OP.max, "dcc RI", "pl")
-            ts(T.PL16[:], T.LT4[:, 48:64], 4096.0, 2048.0, OP.min, OP.subtract, "pl", "PL16")
-            act(sm(12), T.PL16[:], "PL16", "pl32")
+            mm(c("Pa", 0, 256), c("ID"), c("CK"), True, False)
+            mm(c("Pa", 0, 256), c("FL", 256, 384, 1, 16), c("DO", p=16), False, True)
+            to_w(c("Pc", 256, 272), "WZ", lambda k: lane(t, 3, k, 256, 16))
+            gv(0); eq(0); hu(2); hu(3); gv(1); gv(2); gv(3)
+            tt(c("BT"), rows("HI", 0, 16), c("Pa", 0, 256), OP.add)
+            eq(1); eq(2); eq(3, True)
+            mn(0); sg(0)
+            for a, b in hv:
+                tt(c("KK", a, b), rows("PE", a // 16, b // 16), c("BT", a, b), OP.min)
+            for a, b in hv:
+                scan(c("SS", a, b), c("SG"), c("KK", a, b), 0.0, OP.add, OP.max)
+            ts(c("OO", 16, 32), c("Pc", 256, 272), 0.0, OP.is_lt, 16.0, OP.mult)
+            ts(c("CI"), c("SS", 15, 256, 16), -8192.0, OP.max)
+            ts(sm(9), c("SS", 15, 256, 16), -1.0, OP.mult)
+            ts(c("ST", 128, 144), c("OO", 16, 32), float(VZ), OP.add)
+            ts(c("RI", 0, 16), c("CI"), 4095, OP.bitwise_and)
+            claim_places(c("RI", 0, 16))
             claim_rows()
-            act(T.PN[:], T.B3[:, 0:256], "B3", "PN")
-            mn(0)
-            claim_early()
-            claim_rest((0, 4, 8, 9, 12, 13))
-            mn(1); sg(0)
+            mn(1); so(0); sg(1)
+            claim_same()
+            pairs_v((0, 1, 2, 4, 5, 6, 8, 9, 10, 12, 13, 14))
+            claim_sum()
+            mn(2); so(1); sg(2)
             claim_writes()
-            write([("FW", b) for b in (3, 2, 1, 0)])
-            zf, zv, zg = T.B3[:, 0:128], T.B2[:, 0:128], T.B6[:, 0:128]
-            sums(0, "OV", "W1", False); sg(1); sums(1, "OV", "W1", False)
-            zsum("FW", zf, "B3", 0, 16)
-            mn(2); sg(2)
-            zsum("FW", zf, "B3", 16, 32)
-            mn(3); sums(2, "OV", "W1", False); sg(3)
-            write([(n, b) for n in ("VW", "GW") for b in (3, 2, 1, 0)])
-            mm(T.B1[:, 0:256], T.NI[:], T.PEN[:, 0:256], False, False, "NI PENa", "B1")
-            sums(3, "OV", "W1", True)
-            ts(T.BT[:], T.B5[:, 0:256], 76.0, -BIG, OP.is_lt, OP.mult, "B5", "BT")
-            zout(zf, "B3", "ZF", T.zf, "o2")
-            mm(T.B1[:, 0:16], T.ID[:], T.ZR[:, 0:16], False, True, "ID ZR", "B1")
-            zsum("VW", zv, "B2", 0, 32)
-            zsum("GW", zg, "B6", 0, 32)
-            tt(T.KS[:], T.B1[:, 0:256], T.BT[:], OP.add, "B1 BT", "KSa KSb")
-            cp(T.KT[:], T.KS[:].indirect(T.TRN[:]), "KSa KSb TRN", "KT")
-            scan(T.B4[:, 0:256], T.SG[:], T.KT[:], 0.0, OP.add, OP.max, "SG KT", "B4")
-            tt(T.B5[:, 0:256], T.B4[:, 0:256], T.KT[:], OP.subtract, "B4 KT", "B5")
-            ts(sm(1), T.B4[:, 15:256:16], T0 + 409600.0, None, OP.is_lt, None, "B4", "nh")
-            tt(T.BT[:], T.HT[:], T.B5[:, 0:256], OP.subtract, "HT B5", "BT")
-            tt(sm(2), sm(1), XJ, OP.mult, "nh " + st, "nhx")
-            scan(T.SS[:], T.B5[:, 0:256], T.BT[:], 0.0, OP.min, OP.max, "B5 BT", "S")
-            zout(zv, "B2", "ZV", T.zv, "o3")
-            tt(T.OO[:, 0:16], S, sm(2), OP.max, "S nhx", "o1")
-            cp(T.OU[:, 0:16], T.OO[:, 0:16], "o1", "OU")
-            act(T.YF[:], T.GW[:, 0:YO].indirect(T.OU[:, 0:16]), "GW GWd GX OU", "YF")
-            tt(T.YV[:], T.VW[:].indirect(T.OU[:, 0:16]), lane(t, 2, 0, 256), OP.min, "VW VWd VWt OU " + kv, "YV")
-            dma("s", "o1", T.yf[:], T.YF[:], "YF", "outyf")
-            dma("s", "o0", T.yv[:], T.YV[:], "YV", "outyv")
-            zout(zg, "B6", "ZG", T.zg, "o4")
+            zf, zv, zg = c("Pc", 0, 128), rows("PV", 32, 40), rows("PV", 0, 8)
+            so(2)
+            write(t, [("FW", b) for b in (3, 2, 1, 0)])
+            zsum("FW", zf, 0, 16)
+            mn(3); sg(3)
+            act(c("KS"), K3)
+            zsum("FW", zf, 16, 32)
+            so(3, True)
+            zout(zf, "ZF", T.zf, "o2")
+            write(t, [(n, b) for b in (3, 2, 1, 0) for n in ("GW", "VW")])
+            zsum("GW", zg)
+            zsum("VW", zv)
+            tt(c("KO"), O3, c("KS"), OP.min)
+            best("PE", lambda: tt(c("OO", 64, 80), sm(1), c("ST", 112, 128), OP.min),
+                 lambda: tt(c("OO", 80, 96), sm(1), c("ST", 128, 144), OP.min))
+            zout(zg, "ZG", T.zg, "o4")
+            for a in (0, 16):
+                tt(c("OO", a, a + 16), c("SS", 15, 256, 16), c("OO", 64 + a, 80 + a), OP.max)
+            for a in (0, 16):
+                cp(c("OU", a, a + 16), c("OO", a, a + 16))
+            act(c("YF"), ind(c("GW", 0, N2), c("OU", 0, 16)))
+            tt(c("YV"), ind(c("VW"), c("OU", 16, 32)), lane(t, 2), OP.min)
+            store("a", "o1", T.yf[:], c("YF"))
+            store("s", "o0", T.yv[:], c("YV"))
+            zout(zv, "ZV", T.zv, "o3")
             break
-        gw = "GW GWd GX GY NMW0 NMW1 NMW2 OU"
-        tt(T.OO[:, 0:64], T.SS[:].indirect(T.END[:, 0:4]), T.OO[:, 64:128], OP.max, "S END o2", "o1")
-        cp(T.OU[:], T.OO[:, 0:64], "o1", "OU")
-        cp(T.NX[:, 0:256], T.GW[:].indirect(T.OU[:, 16:32]), gw, "NX")
-        mm(T.B4[:, 0:256], T.RB[:], T.NX[:, 0:256], False, True, "RB NX", "B4")
-        act(T.NY[:, 0:256], T.GW[:].indirect(T.OU[:, 32:48]), gw, "NY")
-        act(T.YV[:], T.VW[:].indirect(T.OU[:, 0:16]), "VW VWd VWt OU", "YV")
-        act(T.NN[:, 0:256], T.GW[:].indirect(T.OU[:, 48:64]), gw, "NN")
-        cp(T.RI[:], T.B4[:, 0:256], "B4", "RI")
-        tt(T.OHD[:], T.B4[:, 0:256], T.RI[:], OP.is_equal, "B4 RI", "OHD")
-        scan(T.B5[:, 0:256], T.OHD[:], T.ZR[:], col("ini"), OP.add, OP.add, "OHD ZR ini", "B5")
-        tt(T.XP[:], T.OHD[:], T.B5[:, 0:256], OP.mult, "OHD B5", "XP")
-        to_w(T.B6[:, 16:32], "WR", lambda r: T.XP[:, r:256:16], "XP", "B6")
-        claim_places()
+
+        if t == 0:
+            eq(0); hu(2); hu(3); late_constants(); names_up()
+            gv(0); gv(1); gv(2); gv(3)
+            eq(1); eq(2); mn(0); sg(0); eq(3, True); mn(1); ov(1); mn(2); ov(2); so(0); mn(3)
+            act(c("KS"), E3)
+            ov(3, True)
+            first, second = "PK", "PO"
+        else:
+            gv(0); names_up(); eq(0); hu(2); hu(3); gv(1); gv(2); gv(3)
+            mn(0); eq(1); mn(1); sg(0); eq(2); mn(2); sg(1); so(0); mn(3); sg(2); so(1); ov(3)
+            act(c("KS"), K3)
+            so(2, True); eq(3, True)
+            first, second = "PO", "PE"
+        act(sm(0), c("Pc", 256, 272), AF.Relu, scale=-1.0, bias=-255.0)
+        act(c("GW", N1, N1 + 256), c("Pb", 0, 256))
+        act(c("GW", N2, N2 + 256), c("Pb", 256, 512))
+        tt(c("KO"), rows(first, 0, 16), c("KS"), OP.min)
+        tt(c("ZP"), ind(sm(0), c("REP", 0, 3)), c("ST", 0, 48), OP.mult)
+        tt(c("PP", 16, 64), c("ZP"), c("ST", 48, 96), OP.add)
+        zs = (c("Pc", 0, 128), rows(first, 0, 8))
+        for h, (a, b) in enumerate(hv):
+            mm(zs[h], c("ID"), c("CT"), True, False)
+            mm(zs[h], c("RN"), lane(t, 3, a, b), False, False)
+        if t == 0:
+            tail_constants()
+        best(second, lambda: tt(c("OO", 64, 128), ind(sm(1), c("REP", 0, 4)), c("ST", 96, 160), OP.min),
+             lambda: tt(c("OO", 64, 128), c("OO", 64, 128), c("PP"), OP.max))
+        act(sm(8), sm(1), AF.Abs, bias=-376832.0)
+        act(sm(9), sm(8), AF.Relu, bias=-40000.0)
+        S = c("SS", 15, 256, 16)
+        for a in (16, 0, 32):
+            tt(c("OO", a, a + 16), S, c("OO", 64 + a, 80 + a), OP.max)
+        cp(c("OU", 0, 32), c("OO", 0, 32))
+        cp(c("OU", 48, 64), c("OO", 112, 128))
+        cp(c("OU", 32, 48), c("OO", 32, 48))
+        gw = c("GW", 0, LB + 1024 * t)
+        for h, (a, b) in enumerate(hv):
+            cp(c("N4", 272 + a, 272 + b), ind(gw, c("OU", 16 + 8 * h, 24 + 8 * h)))
+            mm(zs[h], c("RB"), c("N4", 272 + a, 272 + b), False, True)
+        act(c("YV"), ind(c("VW"), c("OU", 0, 16)))
+        act(c("N4", 0, 256), ind(gw, c("OU", 32, 48)))
+        act(c("N4", 816, 1072), ind(gw, c("OU", 48, 64)))
+        Y = vw(second, ix[:, 16, :])
+        mm(Y, c("FL", 256, 384, 1, 16), c("DO", 0, 256, 16, 16), True, False)
+        for h, (a, b) in enumerate(hv):
+            cp(c("RI", a, b), zs[h])
+        for h, (a, b) in enumerate(hv):
+            tt(c("OHD", a, b), zs[h], c("RI", a, b), OP.is_equal)
+        scan(c("Pa", 256, 384), c("OHD", 0, 128), c("CAP"), col("ini"), OP.add, OP.min)
+        tt(sm(10), sm(9), DJ, OP.min)
+        scan(c("Pa", 384, 512), c("OHD", 128, 256), c("CAP"), c("Pa", 383, 384), OP.add, OP.min)
+        for a, b in hv:
+            tt(c("XP", a, b), c("OHD", a, b), c("Pa", 256 + a, 256 + b), OP.mult)
+        to_w(Y, "WR", lambda r: c("XP", r, 256, 16), False, True)
+        tt(c("LT4", 48, 64), sm(10), c("SS", 15, 256, 16), OP.max)
+        tt(c("N4", 544, 800), c("YV"), rows("PV", 0, 64, 4), OP.min)
+        ts(c("PL16"), c("LT4", 48, 64), 4096.0, OP.min, 2048.0, OP.subtract)
         claim_rows()
-        tt(T.NV[:, 0:256], T.YV[:], T.B0[:, 0:256], OP.min, "YV B0", "NV")
-        inv, snd, lnd = "inv%d" % (t + 1), "send%d" % (t + 1), "land%d" % (t + 1)
-        ts(T.PU[:], T.B6[:, 16:32], 256.0, None, OP.add, None, "B6", "PU")
-        cp(T[inv][:].indirect(T.PU[:]), T.JN[:], "PU JN", inv)
-        to_w(T.B6[:, 32:48], "W1", lambda r: T[inv][:, 256 + 16 * r:272 + 16 * r], inv, "B6")
-        act(T.PN[:], T.B1[:, 0:256], "B1", "PN")
-        claim_early()
-        ts(T.IU[:], T.B6[:, 32:48], 0.0625, None, OP.mult, None, "B6", "IU")
-        for c in calls:
-            h = c[0][0] // 4
-            parts = []
-            for o, n in enumerate(("NX", "NY", "NV", "NN")):
-                for k in range(2):
-                    parts.append("%s%d%d%d" % (snd, h, o, k))
-                    (act if o % 2 else cp)(T[snd][:, 512 * h + 4 * k + o:512 * h + 512:8],
-                                           T[n][:].indirect(T.IU[:, 8 * k + 4 * h:8 * k + 4 * h + 4]),
-                                           "%s %sz IU" % (n, n), parts[-1])
-            need("g", parts, [])
+        inv, snd, lnd = "inv%d" % (t + 1), "send%d" % (t + 1), LB + 1024 * t
+        tt(sm(2), Y, DP, OP.min)
+        cp(c("PU"), sm(2))
+        cp(ind(c(inv), c("PU")), c("JN"))
+        for k in range(4):
+            mm(rows("PK", 0, 4), c("WK", 12 - 4 * k, 140 - 4 * k), c(inv, k, 256, 4), k == 0, k == 3)
+        pairs_a((2, 6, 10, 14))
+        claim_same()
+        ts(c("IU"), rows("PK", 0, 4), col("o4"), OP.add)
+
+        def pack(fn, d0, d1):
+            out = c("GW", lnd + 128 * me, lnd + 128 * me + 128) if d0 == me else c(snd, 128 * d0, 128 * d1)
+            fn(out, ind(c("N4"), c("IU", 8 * d0, 8 * d1)))
+
+        for cl in calls:
+            ds = sorted(d for d, es in cl)
+            if len(ds) == 4:
+                pack(cp, ds[0], ds[0] + 2); pack(act, ds[2], ds[2] + 2)
+            else:
+                far, near = sorted(d for d, es in cl[:-1]), cl[-1][0]
+                pack(cp, far[0], far[-1] + 1); pack(act, near, near + 1)
+            need("g", sum((c(snd, 128 * d, 128 * d + 128)[1] for d in ds), []), [])
             xs = []
-            for d, es in c:
+            for d, es in cl:
                 rid, pid = topo.addr(cores[d])[0:2]
                 xs.append(RemoteDMATransfer(dst_ids=[DstId(rid=rid, pnc=pid)], dma_engine_mask=sum(1 << e for e in es),
-                                            remote_sem=T.sem["arr%d" % (t + 1)], src=T[snd][:, 128 * d:128 * d + 128],
-                                            dst=T[lnd][:, 128 * me:128 * me + 128]))
+                                            remote_sem=T.sem["arr%d" % (t + 1)], src=c(snd, 128 * d, 128 * d + 128)[0],
+                                            dst=c("GW", lnd + 128 * me, lnd + 128 * me + 128)[0]))
             g.remote_dma_fused(xs, local_sem=T.sem.sent)
-        act(T[lnd][:, 128 * me:128 * me + 128], T[snd][:, 128 * me:128 * me + 128], " ".join(parts), lnd)
-        note(("arr%d" % (t + 1), comes, "d"), [], [lnd], True)
-        claim_rest((0, 4, 8, 9, 12, 13))
+        pack(act, me, me + 1)
+        for q in range(N):
+            if q != me:
+                note(("arr%d" % (t + 1), comes, "d"), [], c("GW", lnd + 128 * q, lnd + 128 * q + 128)[1])
+        pairs_v((0, 1, 4, 5, 8, 9, 12, 13))
+        claim_sum()
         claim_writes()
-        write([(n, b) for b in (3, 2, 1, 0) for n in ("VW", "FW")])
-        if t == 1:
-            act(T.DL[0:16, :], T.D1[0:16, :], "D1", "DL", scale=200.0)
+        write(t, [(n, b) for b in (3, 2, 1, 0) for n in ("VW", "FW", "GW")])
+        if t == 0:
+            for k, o in enumerate((1, 0, 3)):
+                act(c("J3", 16 * k, 16 * k + 16), J, scale=4.0, bias=float(o))
+        if t < RO - 2:
+            fill("inv%d" % (t + 2), 0, 256, 256)
+            lane_offsets(t + 1)
+        else:
+            act(c("ST", 112, 128), J, bias=float(N1))
 
-    g.wait_ge(T.sem.sent, (RO - 1) * sum(len(es) for c in calls for d, es in c))
+    g.wait_ge(T.sem.sent, (RO - 1) * sum(len(es) for cl in calls for d, es in cl))
     for e in "vapg":
         g.wait_ge(T.sem["s" + e], cnt[e])
     for s in ("o0", "o1", "o2", "o3", "o4"):

@@ -26,24 +26,23 @@ def _decl(dt, where, **kw):
 
 _decl(B, "sbuf", FW=4352, VW=4384, GW=LB + 3072, VG=4096, LO=4096, EQ=4096, OV=4096, V0=256, NB=256, BB=256,
       send1=1024, send2=1024, send3=1024, inv1=512, inv2=512, inv3=512, N4=1088, FL=384, FQ=1024,
-      EE=1024, OHD=256, YF=256, YV=256, ZR=48, SG=128, CAP=128,
+      EE=(12, 64), ES=256, OHD=256, YF=256, YV=256, ZR=48, SG=128, CAP=128,
       ID=128, BLK=128, BW=128, RN=128, RB=128, S1=128, S2=128, P0=128, W1=144, W16=144, WZ=144, W8=144, WE=144,
       WO=144, WK=144, TRI=2048, AB8=16, NW=32, CT=128, CK=256, NEG=128, ONE=256, JN=256, DE=256, DO=256)
 _decl(H, "sbuf", UB=256, XP=256, WR=144, BR=2048, D1=256, DK=256, O16=128, PN=256, PL16=16)
 _decl(F, "sbuf", TQ=128, QQ=144, QG=128, QK=144, TT=128, COL=48, E16=16, TAB=16, DQ=256, KS=256, KO=256, KK=256,
-      BT=256, DF2=384, SS=256, SM=256, ST=160, J3=48, PP=64, ZP=48, OO=128, LT4=64, LT2=32, JW=80, PB=128,
+      BT=256, DF=(12, 64), SS=256, SM=256, ST=160, J3=48, PP=64, ZP=48, OO=128, LT4=64, LT2=32, JW=80, PB=128,
       ZF=128, ZG=128, ZV=128)
 _decl(I, "sbuf", NI32=256, SI=128, UI=256, WI=128, H0=(16, 16), HI=(16, 16), RI=256, CI=16)
-_decl(U, "sbuf", HU=256, OU=64, PU=16, IU=64, CU=16, REP=16, DIV=16, END=16)
+_decl(U, "sbuf", HU=256, OU=64, PU=16, IU=32, CU=16, REP=16, DIV=16)
 _decl(F, "psum", PV=(64, 16), PK=(32, 16), PE=(32, 16), PO=(32, 16), Pa=512, Pb=512, Pc=512)
 
 SEMAPHORES = ["sv", "sa", "sp", "sg", "d0", "d1", "d2", "d3", "d4", "d5", "o0", "o1", "o2", "o3", "o4",
-              "arr1", "arr2", "arr3", "sent"]
+              "arr10", "arr11", "arr20", "arr21", "arr30", "arr31", "sent", "hop1", "hop2", "hop3"]
 
 
-def plan(src, cores, topo):
-    near = [d for d in range(N) if cores[d] != src and topo.chip(cores[d]) == topo.chip(src)]
-    me = cores.index(src)
+def plan(me, src, cores, topo):
+    near = [d for d in range(N) if d != me and topo.chip(cores[d]) == topo.chip(src)]
     far = [(me + k) % N for k in range(1, N) if (me + k) % N not in near]
     off = topo.engines(src, cores[far[0]])
     on = [e for e in topo.engines(src, cores[near[0]]) if e not in off]
@@ -55,11 +54,46 @@ def plan(src, cores, topo):
     return out
 
 
+def helper(me, cores, topo):
+    free = [h for h in topo.cores_of(cores[me]) if h not in cores and all(topo.may_write(h, x) for x in cores)]
+    return free[[x for x in cores if topo.chip(x) == topo.chip(cores[me])].index(cores[me])]
+
+
+def slot(me, calls):
+    ds = [d for cl in calls for d in sorted(x for x, es in cl[:4 - 2 * (len(cl) < 4)]) + [x for x, es in cl[2:] if len(cl) < 4]]
+    return {d: 64 * k for k, d in enumerate(ds)}
+
+
+def fused(g, T, topo, cores, cl, src, dst, sem):
+    xs = []
+    for d, es in cl:
+        rid, pid = topo.addr(cores[d])[0:2]
+        xs.append(RemoteDMATransfer(dst_ids=[DstId(rid=rid, pnc=pid)], remote_sem=sem, src=src(d), dst=dst,
+                                    dma_engine_mask=sum(1 << e for e in es)))
+    g.remote_dma_fused(xs, local_sem=T.sem.sent)
+
+
+def hand_on(g, core, me, T, topo):
+    cores = list(T.cores)
+    calls = plan(me, core, cores, topo)
+    at, came = slot(me, calls), len(plan(me, cores[me], cores, topo)[1][-1][1])
+    for t in range(1, RO):
+        z = LB + 1024 * (t - 1) + 64 * me
+        g.wait_ge(T.sem["hop%d" % t], came)
+        for cl in calls:
+            fused(g, T, topo, cores, cl, lambda d: T["send%d" % t][:, at[d]:at[d] + 64], T.GW[:, z:z + 64],
+                  T.sem["arr%d0" % t])
+    g.wait_ge(T.sem.sent, (RO - 1) * sum(len(es) for cl in calls for d, es in cl))
+
+
 def rank_program(g, core, T, topo):
     me = T.rank_of(core)
-    if me is None:
-        return
     cores = list(T.cores)
+    if me is None:
+        for q in range(N):
+            if helper(q, cores, topo) == core:
+                hand_on(g, core, q, T, topo)
+        return
     Q = {"v": g.vector, "a": g.scalar, "p": g.tensor, "g": g, "s": g.sync}
     cnt = {"v": 0, "a": 0, "p": 0, "g": 0}
     seen = {e: {} for e in Q}
@@ -178,7 +212,7 @@ def rank_program(g, core, T, topo):
             mm(out, c(wname, 15 - k, 143 - k), src(k), first and k == 0, last and k == 15)
 
     def base(t, o):
-        return ((X0, X0, 0, N0)[o], 1) if t == 0 else (LB + 1024 * (t - 1) + o, 4)
+        return ((X0, X0, 0, N0)[o], 1) if t == 0 else (LB + 1024 * (t - 1) + (0, 512, 1, 513)[o], 2)
 
     def lane(t, o, a=0, b=256, s=1):
         z, st = base(t, o)
@@ -202,9 +236,9 @@ def rank_program(g, core, T, topo):
 
     load("s", "d0", c("GW", X0, X0 + 256), T.wf[:])
     load("a", "d1", c("NI32"), T.nm[:])
-    load("s", "d2", c("V0"), T.wv[:])
     load("s", "d4", c("FW", 0, 4096), T.rf[:])
     load("s", "d3", c("VW", 0, 4096), T.rv[:])
+    load("s", "d2", c("V0"), T.wv[:])
     load("s", "d5", c("GW", 0, 4096), T.rg[:])
 
     iota(c("DQ", 0, 16, 1, 32), [[1, 16]], 0, -1)
@@ -218,7 +252,7 @@ def rank_program(g, core, T, topo):
     iota(c("CK"), [[0, 16], [-4096, 16]], 15 * 4096, 0)
     fill("NEG", 0, 128, -2 ** 17)
     fill("ONE", 0, 256, 4096)
-    iota(c("QK"), [[1, 36], [0, 4]], 0, 0)
+    iota(c("QK"), [[1, 72], [0, 2]], 0, 0)
     fill("ST", 0, 160, 0)
     fill("ST", 32, 48, 256)
     fill("ST", 96, 112, VT)
@@ -243,8 +277,8 @@ def rank_program(g, core, T, topo):
     ts(c("CI", 1, 2), c("CI", 0, 1), 15, OP.bitwise_and)
     ts(c("CI", 2, 3), c("CI", 0, 1), 4, OP.arith_shift_right)
     ts(c("CI", 5, 6), c("CI", 0, 1), 7, OP.bitwise_and)
-    ts(c("CI", 6, 7), c("CI", 0, 1), 3, OP.bitwise_and)
-    col("R"), col("G"), col("R8"), col("R4")
+    ts(c("CI", 6, 7), c("CI", 0, 1), 1, OP.bitwise_and)
+    col("R"), col("G"), col("R8"), col("R2")
     cp(c("COL", 0, 2), c("CI", 1, 3))
     cp(c("COL", 2, 4), c("CI", 5, 7))
     ts(c("E16"), c("QQ", 0, 16), col("R"), OP.is_equal)
@@ -304,12 +338,13 @@ def rank_program(g, core, T, topo):
         for k in range(16):
             out, src = c("BR", 128 * k, 128 * k + 128), c("O16")
             op("g", lambda: g.affine_select(out[0], src[0], [[-16, 8], [0, 16]], OP.is_equal, 0.0, -k, 1), out, src)
-        fill("EE", 0, 768, 0)
+        for s in range(3):
+            iota(vw("EE", ix[:, 4 * s:4 * s + 4, 0:16 * s + 16]), [[0, 4], [0, 16 * s + 16]], 0, 0)
         for k in range(16):
             out, src = c("TRI", 128 * k, 128 * k + 128), c("W8", 15 - k, 143 - k)
             op("g", lambda: g.affine_select(out[0], src[0], [[1, 128]], OP.is_gt, 0.0, 0, -1), out, src)
         act(J, c("QQ", 0, 16), scale=16.0, bias=col("R"))
-        act(col("g3"), col("G"), scale=4.0, bias=3.0)
+        act(col("g3"), col("G"), scale=8.0, bias=7.0)
         act(c("WZ"), c("W1"), scale=col("wz"))
         act(c("ST", 80, 96), J, bias=float(N1))
         lane_offsets(0)
@@ -320,27 +355,27 @@ def rank_program(g, core, T, topo):
         act(c("CT"), c("TQ"), scale=0.0, bias=col("rb"))
         act(col("d8"), col("R8"), scale=-1.0, bias=col("R"))
         act(c("RB"), c("BLK"), scale=col("b8"))
+        act(c("SG", 0, 128, 16), c("QQ", 0, 8), scale=0.0, bias=-float(2 ** 60))
 
     def tail_constants():
         act(col("ini"), col("R8"), scale=32.0, bias=-1.0)
         act(col("c8"), col("d8"), scale=128.0, bias=32.0)
         act(col("wr"), col("d8"), scale=255.875, bias=-1023.0)
         act(col("cap"), col("c8"), bias=col("ini"))
-        act(c("WR"), c("W1"), scale=col("wr"))
-        act(c("CAP"), c("TQ"), scale=0.0, bias=col("cap"))
-        act(DP, J, bias=256.0)
-        act(col("o4"), col("R4"), scale=272.0)
         for k in range(3):
             act(c("JW", 16 * k, 16 * k + 16), J, bias=4096.0)
+
+    def route_constants():
+        act(c("CAP"), c("TQ"), scale=0.0, bias=col("cap"))
+        act(c("WR"), c("W1"), scale=col("wr"))
+        act(DP, J, bias=256.0)
+        act(col("o2"), col("R2"), scale=272.0)
 
     def late_constants():
         ts(c("S2"), c("TQ"), col("d2"), OP.is_equal, col("R"), OP.min)
         ts(c("S1"), c("TQ"), col("d1"), OP.is_equal, col("R"), OP.min)
         ts(c("REP"), c("QQ", 0, 16), 0.0, OP.mult, col("R"), OP.add)
-        cp(c("DIV"), c("QQ", 0, 16))
-        ts(c("WK"), c("QK"), col("g3"), OP.is_equal, E(0), OP.mult)
-        ts(c("END"), c("REP"), 16.0, OP.mult, 15.0, OP.add)
-        ms(c("SG", 0, 128, 16), -float(2 ** 60))
+
 
     def lane_offsets(t):
         if t == 0:
@@ -352,8 +387,10 @@ def rank_program(g, core, T, topo):
         for a, sg in ((0, 1.0), (16, -1.0), (64, 1.0)):
             act(c("ST", a, a + 16), J, scale=sg * st, bias=sg * y)
 
-    calls = plan(core, cores, topo)
-    comes = sum(len(es) for q in range(N) if q != me for cl in plan(cores[q], cores, topo) for d, es in cl if d == me)
+    calls = plan(me, core, cores, topo)
+    at, on = slot(me, calls), calls[1][-1][1]
+    comes = [sum(len(es) for q in range(N) if q != me for cl in plan(q, via(q), cores, topo) for d, es in cl if d == me)
+             for via in (lambda q: helper(q, cores, topo), lambda q: cores[q])]
     K3, E3, O3 = rows("PK", 0, 16), rows("PE", 0, 16), rows("PO", 0, 16)
 
     def write(t, order):
@@ -389,9 +426,11 @@ def rank_program(g, core, T, topo):
         mm(E3, c("UB", 128, 256, 1, 33), c("D1", p=33), False, True)
         for k in range(16):
             mm(c("Pb", 128 + k, 512, 16, 16), lane(t, 3, k, 256, 16), c("NW", 8, 32))
-        for m in range(4):
-            for h in range(2):
-                mm(rows("PV", 32 * h + m, 32 * h + 32, 4), c("ID"), lane(t, 2, 128 * h, 128 * h + 128))
+
+        def spread_v():
+            for m in range(4):
+                for h in range(2):
+                    mm(rows("PV", 32 * h + m, 32 * h + 32, 4), c("ID"), lane(t, 2, 128 * h, 128 * h + 128))
         act(c("FL", 0, 128, 1, 16), c("Pb", 128, 256, 1, 16), bias=-16.5)
         act(c("FL", 128, 256, 1, 16), c("Pb", 256, 384, 1, 16), bias=-3.0)
         if last:
@@ -401,6 +440,8 @@ def rank_program(g, core, T, topo):
         if t == 0:
             probe_constants()
             early_constants()
+        else:
+            write(t - 1, [("GW", 1)])
         ms_ = (ix[:, :, 0:4], ix[:, :, 4:16])
         for s in ms_:
             cp(vw("H0", s), vw("PE", ix[:, 0:16, s[2]]))
@@ -452,6 +493,9 @@ def rank_program(g, core, T, topo):
             mm(c("Pb", 0, 256), c("S1"), NM)
             mm(c("Pb", 256, 512), c("S2"), NM)
 
+        def last_name():
+            act(sm(0), c("Pc", 256, 272), AF.Relu, scale=-1.0, bias=-255.0)
+
         hv = ((0, 128), (128, 256))
 
         def best(k3, miss, other):
@@ -478,39 +522,42 @@ def rank_program(g, core, T, topo):
             ts(c("PL16"), c("LT4", 48, 64), 4096.0, OP.min, 2048.0, OP.subtract)
 
         def claim_rows():
-            act(sm(12), c("PL16"))
             for k in range(16):
-                mm(c("Pc", k, 256, 16), c("BR", 128 * k, 128 * k + 128), c("PL16"))
-            act(c("PN"), c("Pc", 0, 256))
+                mm(c("Pb", k, 256, 16), c("BR", 128 * k, 128 * k + 128), c("PL16"))
 
         def pair(cc):
-            return 16 * cc + 16, 64 * (cc // 4) + 64, 256 * (cc % 4), c("SM", 192 + cc, 193 + cc)
+            a, s = 16 * cc + 16, cc % 4
+            return c("PN", a, a + 48 - 16 * s), ix[:, 4 * s + cc // 4, 16 * s + 16:64], c("SM", 192 + cc, 193 + cc)
 
-        def pairs_a(cs):
-            for i, cc in enumerate(cs):
-                a, b, s, pl = pair(cc)
-                act(c("DF2", 48 * i, 48 * i + b - a), c("PN", a, b), AF.Abs, bias=pl, scale=-1.0)
-            for i, cc in enumerate(cs):
-                a, b, s, pl = pair(cc)
-                act(c("EE", s + a, s + b), c("DF2", 48 * i, 48 * i + b - a), AF.Relu, bias=8192.0, scale=-8192.0)
+        def pairs_a(ss):
+            for s in ss:
+                for b in range(4):
+                    pn, at, pl = pair(4 * b + s)
+                    act(vw("DF", at), pn, AF.Abs, bias=pl, scale=-1.0)
+            for s in ss:
+                at = ix[:, 4 * s:4 * s + 4, 16 * s + 16:64]
+                act(vw("EE", at), vw("DF", at), AF.Relu, bias=8192.0, scale=-8192.0)
 
         def pairs_v(cs):
             for cc in cs:
-                a, b, s, pl = pair(cc)
-                ts(c("EE", s + a, s + b), c("PN", a, b), pl, OP.is_equal, 8192.0, OP.mult)
+                pn, at, pl = pair(cc)
+                ts(vw("EE", at), pn, pl, OP.is_equal, 8192.0, OP.mult)
 
         def claim_same():
-            tt(c("EE", 768, 1024), ind(sm(12), c("DIV")), c("PN"), OP.is_equal)
-            mm(c("Pb", 0, 48), c("ID"), c("ZR"), True, False)
+            tt(c("ES"), ind(sm(12), c("DIV")), c("PN"), OP.is_equal)
+            mm(c("Pb", 256, 304), c("ID"), c("ZR"), True, False)
             for k in range(16):
-                mm(c("Pb", 0, 16), c("TRI", 128 * k, 128 * k + 128), c("EE", 768 + k, 1024, 16), False, False)
+                mm(c("Pb", 256, 272), c("TRI", 128 * k, 128 * k + 128), c("ES", k, 256, 16), False, False)
 
         def claim_sum():
-            to_w(c("Pb", 0, 48), "W1", lambda r: c("EE", r, 768, 16), False, True)
+            to_w(c("Pb", 256, 304), "W1", lambda r: vw("EE", ix[:, :, r:64:16]), False, True)
 
-        def claim_writes():
-            tt(c("LT4", 0, 48), c("Pb", 0, 48), c("JW", 0, 48), OP.min)
+        def claim_lost():
+            tt(c("LT4", 0, 48), c("Pb", 256, 304), c("JW", 0, 48), OP.min)
+
+        def claim_writes(between=lambda: None):
             tt(c("LT2"), c("LT4", 0, 32), c("LT4", 32, 64), OP.max)
+            between()
             tt(sm(13), c("LT2", 0, 16), c("LT2", 16, 32), OP.max)
             cp(c("CU"), sm(13))
 
@@ -528,7 +575,7 @@ def rank_program(g, core, T, topo):
             to_w(c("Pc", 256, 272), "WZ", lambda k: lane(t, 3, k, 256, 16))
             gv(0); eq(0); hu(2); hu(3); gv(1); gv(2); gv(3)
             tt(c("BT"), rows("HI", 0, 16), c("Pa", 0, 256), OP.add)
-            eq(1); eq(2); eq(3, True)
+            eq(1); eq(2); spread_v(); eq(3, True)
             mn(0); sg(0)
             for a, b in hv:
                 tt(c("KK", a, b), rows("PE", a // 16, b // 16), c("BT", a, b), OP.min)
@@ -540,21 +587,31 @@ def rank_program(g, core, T, topo):
             ts(c("ST", 128, 144), c("OO", 16, 32), float(VZ), OP.add)
             ts(c("RI", 0, 16), c("CI"), 4095, OP.bitwise_and)
             claim_places(c("RI", 0, 16))
+            act(sm(12), c("PL16"))
             claim_rows()
+            act(c("PN"), c("Pb", 0, 256))
+            write(t - 1, [("GW", 0)])
+            pairs_a((1, 2))
             mn(1); so(0); sg(1)
             claim_same()
-            pairs_v((0, 1, 2, 4, 5, 6, 8, 9, 10, 12, 13, 14))
+            pairs_v((0, 4, 8, 12))
+            tt(ch("LO", 2), ch("VG", 2), rows("PV", 0, 64), OP.min)
             claim_sum()
-            mn(2); so(1); sg(2)
-            claim_writes()
+            sums(2, "LO", "PK", "W16")
+            sg(2); so(1)
+
+            def quarter(b):
+                a = 3072 + 256 * b
+                tt(c("LO", a, a + 256), c("VG", a, a + 256), rows("PV", 16 * b, 16 * b + 16), OP.min)
+            quarter(0); quarter(1); claim_lost(); quarter(2)
+            claim_writes(lambda: quarter(3))
+            sums(3, "LO", "PK", "W16", True)
+            sg(3)
             zf, zv, zg = c("Pc", 0, 128), rows("PV", 32, 40), rows("PV", 0, 8)
-            so(2)
-            write(t, [("FW", b) for b in (3, 2, 1, 0)])
-            zsum("FW", zf, 0, 16)
-            mn(3); sg(3)
+            so(2); so(3, True)
             act(c("KS"), K3)
-            zsum("FW", zf, 16, 32)
-            so(3, True)
+            write(t, [("FW", b) for b in (3, 2, 1, 0)])
+            zsum("FW", zf)
             zout(zf, "ZF", T.zf, "o2")
             write(t, [(n, b) for b in (3, 2, 1, 0) for n in ("GW", "VW")])
             zsum("GW", zg)
@@ -577,45 +634,57 @@ def rank_program(g, core, T, topo):
         if t == 0:
             eq(0); hu(2); hu(3); late_constants(); names_up()
             gv(0); gv(1); gv(2); gv(3)
-            eq(1); eq(2); mn(0); sg(0); eq(3, True); mn(1); ov(1); mn(2); ov(2); so(0); mn(3)
+            eq(1); spread_v(); eq(2); mn(0); sg(0); eq(3, True); mn(1); mn(2); sg(2); ov(1); so(0); mn(3)
             act(c("KS"), E3)
-            ov(3, True)
+            ov(3); so(2, True); last_name()
             first, second = "PK", "PO"
         else:
             gv(0); names_up(); eq(0); hu(2); hu(3); gv(1); gv(2); gv(3)
-            mn(0); eq(1); mn(1); sg(0); eq(2); mn(2); sg(1); so(0); mn(3); sg(2); so(1); ov(3)
-            act(c("KS"), K3)
-            so(2, True); eq(3, True)
-            first, second = "PO", "PE"
-        act(sm(0), c("Pc", 256, 272), AF.Relu, scale=-1.0, bias=-255.0)
+            eq(1); spread_v(); eq(2); mn(0); sg(0); mn(1); sg(1); mn(2); so(0); sg(2); mn(3); so(1)
+            last_name(); sg(3); so(2); eq(3, True); so(3, True)
+            cp(c("KS"), K3)
+            write(t - 1, [("GW", 0)])
+            first, second = "PE", "PO"
         act(c("GW", N1, N1 + 256), c("Pb", 0, 256))
         act(c("GW", N2, N2 + 256), c("Pb", 256, 512))
-        tt(c("KO"), rows(first, 0, 16), c("KS"), OP.min)
         tt(c("ZP"), ind(sm(0), c("REP", 0, 3)), c("ST", 0, 48), OP.mult)
+        tt(c("KO"), rows(first, 0, 16), c("KS"), OP.min)
         tt(c("PP", 16, 64), c("ZP"), c("ST", 48, 96), OP.add)
         zs = (c("Pc", 0, 128), rows(first, 0, 8))
         for h, (a, b) in enumerate(hv):
             mm(zs[h], c("ID"), c("CT"), True, False)
             mm(zs[h], c("RN"), lane(t, 3, a, b), False, False)
         if t == 0:
+            ts(c("WK"), c("QK"), col("g3"), OP.is_equal, E(0), OP.mult)
             tail_constants()
         best(second, lambda: tt(c("OO", 64, 128), ind(sm(1), c("REP", 0, 4)), c("ST", 96, 160), OP.min),
              lambda: tt(c("OO", 64, 128), c("OO", 64, 128), c("PP"), OP.max))
         act(sm(8), sm(1), AF.Abs, bias=-376832.0)
         act(sm(9), sm(8), AF.Relu, bias=-40000.0)
+        if t == 0:
+            route_constants()
         S = c("SS", 15, 256, 16)
-        for a in (16, 0, 32):
-            tt(c("OO", a, a + 16), S, c("OO", 64 + a, 80 + a), OP.max)
-        cp(c("OU", 0, 32), c("OO", 0, 32))
-        cp(c("OU", 48, 64), c("OO", 112, 128))
-        cp(c("OU", 32, 48), c("OO", 32, 48))
+        tt(sm(10), sm(9), DJ, OP.min)
+        tt(c("OO", 16, 32), S, c("OO", 80, 96), OP.max)
+        tt(c("OO", 0, 16), S, c("OO", 64, 80), OP.max)
+        tt(c("LT4", 48, 64), sm(10), S, OP.max)
+        cp(c("OU", 16, 32), c("OO", 16, 32))
+        cp(c("OU", 0, 16), c("OO", 0, 16))
         gw = c("GW", 0, LB + 1024 * t)
         for h, (a, b) in enumerate(hv):
-            cp(c("N4", 272 + a, 272 + b), ind(gw, c("OU", 16 + 8 * h, 24 + 8 * h)))
-            mm(zs[h], c("RB"), c("N4", 272 + a, 272 + b), False, True)
+            (cp, act)[h](c("N4", 544 + a, 544 + b), ind(gw, c("OU", 16 + 8 * h, 24 + 8 * h)))
+            mm(zs[h], c("RB"), c("N4", 544 + a, 544 + b), False, True)
+        ts(c("PL16"), c("LT4", 48, 64), 4096.0, OP.min, 2048.0, OP.subtract)
+        tt(c("OO", 32, 48), S, c("OO", 96, 112), OP.max)
+        cp(c("OU", 48, 64), c("OO", 112, 128))
+        cp(c("OU", 32, 48), c("OO", 32, 48))
+        claim_rows()
+        act(sm(12), c("PL16"))
         act(c("YV"), ind(c("VW"), c("OU", 0, 16)))
-        act(c("N4", 0, 256), ind(gw, c("OU", 32, 48)))
+        act(c("PN"), c("Pb", 0, 256))
         act(c("N4", 816, 1072), ind(gw, c("OU", 48, 64)))
+        act(c("N4", 0, 256), ind(gw, c("OU", 32, 48)))
+        pairs_a((1, 2))
         Y = vw(second, ix[:, 16, :])
         mm(Y, c("FL", 256, 384, 1, 16), c("DO", 0, 256, 16, 16), True, False)
         for h, (a, b) in enumerate(hv):
@@ -623,62 +692,66 @@ def rank_program(g, core, T, topo):
         for h, (a, b) in enumerate(hv):
             tt(c("OHD", a, b), zs[h], c("RI", a, b), OP.is_equal)
         scan(c("Pa", 256, 384), c("OHD", 0, 128), c("CAP"), col("ini"), OP.add, OP.min)
-        tt(sm(10), sm(9), DJ, OP.min)
         scan(c("Pa", 384, 512), c("OHD", 128, 256), c("CAP"), c("Pa", 383, 384), OP.add, OP.min)
         for a, b in hv:
             tt(c("XP", a, b), c("OHD", a, b), c("Pa", 256 + a, 256 + b), OP.mult)
         to_w(Y, "WR", lambda r: c("XP", r, 256, 16), False, True)
-        tt(c("LT4", 48, 64), sm(10), c("SS", 15, 256, 16), OP.max)
-        tt(c("N4", 544, 800), c("YV"), rows("PV", 0, 64, 4), OP.min)
-        ts(c("PL16"), c("LT4", 48, 64), 4096.0, OP.min, 2048.0, OP.subtract)
-        claim_rows()
+        if t == 0:
+            cp(c("DIV"), c("QQ", 0, 16))
+        tt(c("N4", 272, 528), c("YV"), rows("PV", 0, 64, 4), OP.min)
+        claim_same()
         inv, snd, lnd = "inv%d" % (t + 1), "send%d" % (t + 1), LB + 1024 * t
         tt(sm(2), Y, DP, OP.min)
+        pairs_v((0,))
         cp(c("PU"), sm(2))
+        pairs_v((4,))
         cp(ind(c(inv), c("PU")), c("JN"))
-        for k in range(4):
-            mm(rows("PK", 0, 4), c("WK", 12 - 4 * k, 140 - 4 * k), c(inv, k, 256, 4), k == 0, k == 3)
-        pairs_a((2, 6, 10, 14))
-        claim_same()
-        ts(c("IU"), rows("PK", 0, 4), col("o4"), OP.add)
-
-        def pack(fn, d0, d1):
-            out = c("GW", lnd + 128 * me, lnd + 128 * me + 128) if d0 == me else c(snd, 128 * d0, 128 * d1)
-            fn(out, ind(c("N4"), c("IU", 8 * d0, 8 * d1)))
-
-        for cl in calls:
-            ds = sorted(d for d, es in cl)
-            if len(ds) == 4:
-                pack(cp, ds[0], ds[0] + 2); pack(act, ds[2], ds[2] + 2)
-            else:
-                far, near = sorted(d for d, es in cl[:-1]), cl[-1][0]
-                pack(cp, far[0], far[-1] + 1); pack(act, near, near + 1)
-            need("g", sum((c(snd, 128 * d, 128 * d + 128)[1] for d in ds), []), [])
-            xs = []
-            for d, es in cl:
-                rid, pid = topo.addr(cores[d])[0:2]
-                xs.append(RemoteDMATransfer(dst_ids=[DstId(rid=rid, pnc=pid)], dma_engine_mask=sum(1 << e for e in es),
-                                            remote_sem=T.sem["arr%d" % (t + 1)], src=c(snd, 128 * d, 128 * d + 128)[0],
-                                            dst=c("GW", lnd + 128 * me, lnd + 128 * me + 128)[0]))
-            g.remote_dma_fused(xs, local_sem=T.sem.sent)
-        pack(act, me, me + 1)
-        for q in range(N):
-            if q != me:
-                note(("arr%d" % (t + 1), comes, "d"), [], c("GW", lnd + 128 * q, lnd + 128 * q + 128)[1])
-        pairs_v((0, 1, 4, 5, 8, 9, 12, 13))
+        for k in range(8):
+            mm(rows("PK", 0, 2), c("WK", 14 - 2 * k, 142 - 2 * k), c(inv, k, 256, 8), k == 0, k == 7)
+        pairs_v((8, 12))
         claim_sum()
+        ts(c("IU"), rows("PK", 0, 2), col("o2"), OP.add)
+        for part in (1, 0):
+            z, arr = 512 * part, "arr%d%d" % (t + 1, part)
+            mine = c("GW", lnd + z + 64 * me, lnd + z + 64 * me + 64)
+
+            def pack(fn, d0, d1):
+                out = mine if d0 == me else c(snd, z + at[d0], z + at[d0] + 64 * (d1 - d0))
+                fn(out, ind(c("N4", 544 * part, 544 * part + 544), c("IU", 4 * d0, 4 * d1)))
+
+            for cl in calls:
+                ds = sorted(d for d, es in cl)
+                if len(ds) == 4:
+                    pack(cp, ds[0], ds[0] + 2); pack(act, ds[2], ds[2] + 2)
+                else:
+                    far, near = sorted(d for d, es in cl[:-1]), cl[-1][0]
+                    pack(cp, far[0], far[-1] + 1); pack(act, near, near + 1)
+                if part:
+                    need("g", sum((c(snd, z + at[d], z + at[d] + 64)[1] for d in ds), []), [])
+                    fused(g, T, topo, cores, cl, lambda d: c(snd, z + at[d], z + at[d] + 64)[0], mine[0], T.sem[arr])
+            if not part:
+                rest = c(snd, 0, 64 * (N - 1))
+                need("g", rest[1], [])
+                rid, pid = topo.addr(helper(me, cores, topo))[0:2]
+                g.remote_dma(rest[0], rest[0], T.sem["hop%d" % (t + 1)], T.sem.sent, pid, rid, sum(1 << e for e in on))
+            pack(act, me, me + 1)
+            for q in range(N):
+                if q != me:
+                    note((arr, comes[part], "d"), [], c("GW", lnd + z + 64 * q, lnd + z + 64 * q + 64)[1])
+            if part:
+                claim_lost()
         claim_writes()
-        write(t, [(n, b) for b in (3, 2, 1, 0) for n in ("VW", "FW", "GW")])
+        write(t, [(n, b) for b in (3, 2, 1, 0) for n in ("VW", "FW", "GW") if (n, b // 2) != ("GW", 0)])
         if t == 0:
-            for k, o in enumerate((1, 0, 3)):
-                act(c("J3", 16 * k, 16 * k + 16), J, scale=4.0, bias=float(o))
+            for k, o in enumerate((512, 0, 513)):
+                act(c("J3", 16 * k, 16 * k + 16), J, scale=2.0, bias=float(o))
         if t < RO - 2:
             fill("inv%d" % (t + 2), 0, 256, 256)
             lane_offsets(t + 1)
         else:
             act(c("ST", 112, 128), J, bias=float(N1))
 
-    g.wait_ge(T.sem.sent, (RO - 1) * sum(len(es) for cl in calls for d, es in cl))
+    g.wait_ge(T.sem.sent, (RO - 1) * (len(on) + sum(len(es) for cl in calls for d, es in cl)))
     for e in "vapg":
         g.wait_ge(T.sem["s" + e], cnt[e])
     for s in ("o0", "o1", "o2", "o3", "o4"):

import numpy as np
from concourse.bass import DstId, RemoteDMATransfer
from concourse.mybir import AluOpType as OP, AxisListType as AX, ActivationFunctionType as AF

N = 8
RO = 4
TAU = [96, 700, 24, 2496]
WA = [7, 113, 51, 229, 87, 19, 161, 203, 35, 149, 71, 247, 93, 181, 125, 11]
WB = [1, 3, 2, 7, 5, 1, 6, 3, 7, 2, 5, 4, 1, 6, 3, 5]
KP = [3, 18, 45, 71, 102, 125, 150, 187, 208, 233, 260, 291, 318, 345, 382, 407]
TOP = 130560
T0 = -float(2 ** 36)
HG = float(2 ** 37)
N1, N2, X0, N0, LB = 4352, 4608, 4864, 5120, 5376
VZ, VT = 4352, 4368
ix = np.s_

B, F, H, I, U = "bfloat16", "float32", "float16", "int32", "uint16"
SCRATCH = {}


def _decl(dt, where, **kw):
    for k, n in kw.items():
        SCRATCH[k] = (where, [128] + (list(n) if isinstance(n, tuple) else [n]), dt)


_decl(B, "sbuf", FW=4352, VW=4384, GW=LB + 3072, VG=4096, LO=4096, EQ=4096, OV=4096, V0=256, NB=256, BB=256,
      send1=1024, send2=1024, send3=1024, inv1=512, inv2=512, inv3=512, N4=1088, FL=384, FQ=1024,
      EE=(12, 64), ES=256, OHD=256, YF=256, YV=256, ZR=48, SG=128, CAP=128,
      ID=128, BLK=128, BW=128, RN=128, RB=128, S1=128, S2=128, P0=128, W1=144, W16=144, WZ=144, W8=144, WE=144,
      WO=144, WK=144, TRI=2048, AB8=16, NW=32, CT=128, CK=256, NEG=128, ONE=256, JN=256, DE=256, DO=256)
_decl(H, "sbuf", UB=256, XP=256, WR=144, BR=2048, D1=256, DK=256, O16=128, PN=256, PL16=16)
_decl(F, "sbuf", TQ=128, QQ=144, QG=128, QK=144, TT=128, COL=48, E16=16, TAB=16, DQ=256, KS=256, KO=256, KK=256,
      BT=256, DF=(12, 64), SS=256, SM=256, ST=160, J3=48, PP=64, ZP=48, OO=128, LT4=64, LT2=32, JW=80, PB=128,
      ZF=128, ZG=128, ZV=128)
_decl(I, "sbuf", NI32=256, SI=128, UI=256, WI=128, H0=(16, 16), HI=(16, 16), RI=256, CI=16)
_decl(U, "sbuf", HU=256, OU=64, PU=16, IU=32, CU=16, REP=16, DIV=16)
_decl(F, "psum", PV=(64, 16), PK=(32, 16), PE=(32, 16), PO=(32, 16), Pa=512, Pb=512, Pc=512)

SEMAPHORES = ["sv", "sa", "sp", "sg", "d0", "d1", "d2", "d3", "d4", "d5", "o0", "o1", "o2", "o3", "o4",
              "arr10", "arr11", "arr20", "arr21", "arr30", "arr31", "sent", "hop1", "hop2", "hop3"]


def plan(me, src, cores, topo):
    near = [d for d in range(N) if d != me and topo.chip(cores[d]) == topo.chip(src)]
    far = [(me + k) % N for k in range(1, N) if (me + k) % N not in near]
    off = topo.engines(src, cores[far[0]])
    on = [e for e in topo.engines(src, cores[near[0]]) if e not in off]
    out = []
    for own in (False, True):
        ds = [d for d in far if (d // 4 == me // 4) == own]
        n = len(off) // len(ds)
        out.append([(d, off[n * k:n * k + n]) for k, d in enumerate(ds)] + ([(near[0], on)] if own else []))
    return out


def helper(me, cores, topo):
    free = [h for h in topo.cores_of(cores[me]) if h not in cores and all(topo.may_write(h, x) for x in cores)]
    return free[[x for x in cores if topo.chip(x) == topo.chip(cores[me])].index(cores[me])]


def slot(me, calls):
    ds = [d for cl in calls for d in sorted(x for x, es in cl[:4 - 2 * (len(cl) < 4)]) + [x for x, es in cl[2:] if len(cl) < 4]]
    return {d: 64 * k for k, d in enumerate(ds)}


def fused(g, T, topo, cores, cl, src, dst, sem):
    xs = []
    for d, es in cl:
        rid, pid = topo.addr(cores[d])[0:2]
        xs.append(RemoteDMATransfer(dst_ids=[DstId(rid=rid, pnc=pid)], remote_sem=sem, src=src(d), dst=dst,
                                    dma_engine_mask=sum(1 << e for e in es)))
    g.remote_dma_fused(xs, local_sem=T.sem.sent)


def hand_on(g, core, me, T, topo):
    cores = list(T.cores)
    calls = plan(me, core, cores, topo)
    at, came = slot(me, calls), len(plan(me, cores[me], cores, topo)[1][-1][1])
    for t in range(1, RO):
        z = LB + 1024 * (t - 1) + 64 * me
        g.wait_ge(T.sem["hop%d" % t], came)
        for cl in calls:
            fused(g, T, topo, cores, cl, lambda d: T["send%d" % t][:, at[d]:at[d] + 64], T.GW[:, z:z + 64],
                  T.sem["arr%d0" % t])
    g.wait_ge(T.sem.sent, (RO - 1) * sum(len(es) for cl in calls for d, es in cl))


def rank_program(g, core, T, topo):
    me = T.rank_of(core)
    cores = list(T.cores)
    if me is None:
        for q in range(N):
            if helper(q, cores, topo) == core:
                hand_on(g, core, q, T, topo)
        return
    Q = {"v": g.vector, "a": g.scalar, "p": g.tensor, "g": g, "s": g.sync}
    cnt = {"v": 0, "a": 0, "p": 0, "g": 0}
    seen = {e: {} for e in Q}
    acc, banks, knew, views = {}, {}, {}, {}

    def vw(name, s):
        key = (name, repr(s))
        if key not in views:
            where, shape, _ = SCRATCH[name]
            n = int(np.prod(shape[1:]))
            cols = np.arange(n).reshape(shape[1:])[s[1:]].ravel()
            m = np.zeros(n, bool)
            m[cols] = True
            p = range(128)[s[0]]
            bk = sorted(set((name, int(c) // 512) for c in cols)) if where == "psum" else []
            views[key] = (T[name][s], [(name, p[0], p[-1], int.from_bytes(np.packbits(m).tobytes(), "big"), bk)], [])
        return views[key]

    def c(name, a=0, b=None, s=1, p=128):
        return vw(name, ix[0:p, a:b:s])

    def ind(win, off):
        return (win[0].indirect(off[0]), win[1], off[1])

    def need(e, r, w):
        deps = []
        for cells, write in ((r, False), (w, True)):
            for name, p0, p1, m, bk in cells:
                deps += [x[4] for x in acc.get(name, []) if (write or x[0]) and x[1] <= p1 and p0 <= x[2] and x[3] & m]
                for b in bk:
                    deps += [t for e2, t in banks.get(b, {}).items() if e2 != e]
        top = {}
        for s, val, who in deps:
            if not (who == "p" and e == "p"):
                top[s] = max(top.get(s, 0), val)
        for s, val in top.items():
            if any(knew.get((s2, v2), {}).get(s, 0) >= val for s2, v2 in top.items() if s2 != s):
                continue
            if seen[e].get(s, 0) < val:
                Q[e].wait_ge(T.sem[s], val)
                seen[e][s] = val
        for tok in top.items():
            for s, val in knew.get(tok, {}).items():
                seen[e][s] = max(seen[e].get(s, 0), val)

    def note(tok, r, w, e=None):
        if e:
            knew[tok[0:2]] = dict(seen[e])
        for cells, write in ((r, False), (w, True)):
            for name, p0, p1, m, bk in cells:
                L = acc.setdefault(name, [])
                L[:] = [x for x in L if not ((write or (not x[0] and x[4][0] == tok[0]))
                                             and p0 <= x[1] and x[2] <= p1 and not x[3] & ~m)]
                L.append((write, p0, p1, m, tok))
                for b in bk:
                    banks.setdefault(b, {})[e] = tok

    def cells(out, ins):
        ins = [x for x in ins if isinstance(x, tuple)]
        return sum((x[1] + x[2] for x in ins), []) + out[2], out[1]

    def op(e, fn, out, *ins):
        r, w = cells(out, ins)
        need(e, r, w)
        cnt[e] += 1
        fn().then_inc(T.sem["s" + e], 1)
        note(("s" + e, cnt[e], e), r, w, e)

    def load(e, sem, out, src):
        need(e, [], out[1])
        Q[e].dma_start(out[0], src).then_inc(T.sem[sem], 16)
        note((sem, 16, "d"), [], out[1])

    def store(e, sem, dst, src):
        need(e, src[1], [])
        Q[e].dma_start(dst, src[0]).then_inc(T.sem[sem], 16)

    def A(x):
        return x[0] if isinstance(x, tuple) else x

    def ts(out, a, s1, o0, s2=None, o1=None):
        if o1 is None:
            op("v", lambda: g.vector.tensor_scalar(out[0], a[0], A(s1), None, o0), out, a, s1)
        else:
            op("v", lambda: g.vector.tensor_scalar(out[0], a[0], A(s1), A(s2), o0, o1), out, a, s1, s2)

    def tt(out, a, b, o):
        op("v", lambda: g.vector.tensor_tensor(out[0], a[0], b[0], o), out, a, b)

    def cp(out, a):
        op("v", lambda: g.vector.tensor_copy(out[0], a[0]), out, a)

    def ms(out, k):
        op("v", lambda: g.vector.memset(out[0], k), out)

    def scan(out, a, b, ini, o0, o1):
        op("v", lambda: g.vector.tensor_tensor_scan(out[0], a[0], b[0], A(ini), o0, o1), out, a, b, ini)

    def act(out, a, f=AF.Identity, bias=0.0, scale=1.0):
        op("a", lambda: g.scalar.activation(out[0], a[0], f, bias=A(bias), scale=A(scale)), out, a, bias, scale)

    def mm(out, l, rhs, st=True, sp=True):
        op("p", lambda: g.tensor.matmul(out[0], l[0], rhs[0], st, sp), out, l, rhs)

    def iota(out, pat, base, ch, flt=True):
        if flt:
            op("g", lambda: g.iota(out[0], pat, base, ch, allow_small_or_imprecise_dtypes=True), out)
        else:
            op("g", lambda: g.iota(out[0], pat, base, ch), out)

    def fill(name, a, b, val):
        iota(c(name, a, b), [[0, b - a]], val, 0)

    def to_w(out, wname, src, first=True, last=True):
        for k in range(16):
            mm(out, c(wname, 15 - k, 143 - k), src(k), first and k == 0, last and k == 15)

    def base(t, o):
        return ((X0, X0, 0, N0)[o], 1) if t == 0 else (LB + 1024 * (t - 1) + (0, 512, 1, 513)[o], 2)

    def lane(t, o, a=0, b=256, s=1):
        z, st = base(t, o)
        return c("V0" if (t, o) == (0, 2) else "GW", z + st * a, z + st * (b - 1) + 1, st * s)

    C = {}

    def col(n):
        if n not in C:
            C[n] = len(C)
        return c("COL", C[n], C[n] + 1)

    def E(k):
        return c("E16", k, k + 1)

    def sm(k):
        return c("SM", 16 * k, 16 * k + 16)

    def rows(name, a, b, s=1):
        return vw(name, ix[:, a:b:s, :])

    load("s", "d0", c("GW", X0, X0 + 256), T.wf[:])
    load("a", "d1", c("NI32"), T.nm[:])
    load("s", "d4", c("FW", 0, 4096), T.rf[:])
    load("s", "d3", c("VW", 0, 4096), T.rv[:])
    load("s", "d2", c("V0"), T.wv[:])
    load("s", "d5", c("GW", 0, 4096), T.rg[:])

    iota(c("DQ", 0, 16, 1, 32), [[1, 16]], 0, -1)
    ms(vw("DQ", ix[32:33, 0:16]), 0.0)
    ms(vw("KS", ix[32:33, :]), 0.0)
    iota(c("CI", 0, 1), [[0, 1]], 0, 1, False)
    iota(c("QQ"), [[1, 144]], 0, 0)
    iota(c("QG"), [[1, 8], [0, 16]], 0, 0)
    iota(c("TQ"), [[1, 128]], 0, -1)
    iota(c("KS", p=32), [[1, 16], [0, 16]], 0, -1)
    iota(c("CK"), [[0, 16], [-4096, 16]], 15 * 4096, 0)
    fill("NEG", 0, 128, -2 ** 17)
    fill("ONE", 0, 256, 4096)
    iota(c("QK"), [[1, 72], [0, 2]], 0, 0)
    fill("ST", 0, 160, 0)
    fill("ST", 32, 48, 256)
    fill("ST", 96, 112, VT)
    fill("PP", 0, 16, 0)
    fill("SG", 0, 128, 0)
    iota(c("JN"), [[1, 256]], 0, 0)
    fill("ZR", 0, 48, 0)
    fill("VW", 4096, VT, 0)
    fill("VW", VT, VT + 16, TOP)
    fill("GW", 4096, 4352, 0)
    fill("FW", 4096, 4352, 0)
    for o in range(4):
        fill("N4", 272 * o + 256, 272 * o + 272, 0)
    fill("inv1", 0, 256, 256)

    for k in range(16):
        ms(c("TAB", k, k + 1), float(8 * WA[k] + WB[k]))
        if k == 1:
            ts(c("DQ", 16, 32, 1, 33), c("DQ", 0, 16, 1, 33), 0.0, OP.is_equal)
            for m in range(8):
                act(c("DK", m, 256, 16, 33), c("DQ", 16, 32, 1, 33), scale=float(KP[m]))
    ts(c("CI", 1, 2), c("CI", 0, 1), 15, OP.bitwise_and)
    ts(c("CI", 2, 3), c("CI", 0, 1), 4, OP.arith_shift_right)
    ts(c("CI", 5, 6), c("CI", 0, 1), 7, OP.bitwise_and)
    ts(c("CI", 6, 7), c("CI", 0, 1), 1, OP.bitwise_and)
    col("R"), col("G"), col("R8"), col("R2")
    cp(c("COL", 0, 2), c("CI", 1, 3))
    cp(c("COL", 2, 4), c("CI", 5, 7))
    ts(c("E16"), c("QQ", 0, 16), col("R"), OP.is_equal)
    ts(c("BLK"), c("QG"), col("G"), OP.is_equal)
    tt(sm(0), c("TAB"), c("E16"), OP.mult)
    tt(col("e23"), E(2), E(3), OP.add)
    op("v", lambda: g.vector.tensor_reduce(col("AB")[0], sm(0)[0], AX.X, OP.add), col("AB"), sm(0))
    ts(col("lo"), col("R"), 1.0, OP.min, 3.0, OP.mult)
    cp(c("CI", 3, 4), col("AB"))
    ts(col("lt4"), col("R"), 4.0, OP.is_lt)
    ts(c("CI", 4, 5), c("CI", 3, 4), 3, OP.arith_shift_right)
    ts(c("TT"), c("TQ"), 3.0, OP.is_le)
    cp(col("A"), c("CI", 4, 5))
    ts(c("PB"), c("TQ"), col("lo"), OP.is_ge, col("lt4"), OP.mult)
    tt(c("P0"), c("TT"), c("PB"), OP.mult)
    cp(c("NB"), c("NI32"))
    blk8 = c("BLK", 0, 128, 16)
    act(col("c1"), col("e23"), scale=-254.0, bias=255.0)
    act(col("sg"), E(3), scale=-2.0, bias=1.0)
    act(c("AB8", 0, 8), blk8, scale=col("A"))
    act(col("n0"), E(0), scale=2.0, bias=col("e23"))
    act(col("ne"), E(2), scale=5.0, bias=E(3))
    act(col("no"), E(3), scale=20.0)
    act(col("bw"), E(2), scale=256.0)
    for k, w in enumerate((col("n0"), col("ne"), col("no"), E(2))):
        act(c("NW", 8 * k, 8 * k + 8), blk8, scale=w)
    act(c("BW"), c("BLK"), scale=col("bw"))
    act(c("UB", p=33), c("KS", p=33), scale=0.0, bias=2048.0)
    for m in range(8, 16):
        act(c("DK", m, 256, 16, 33), c("DQ", 16, 32, 1, 33), scale=float(KP[m]))
    mm(c("Pa", 0, 256), c("BLK"), lane(0, 1))
    mm(c("Pb", 0, 256), c("P0"), c("NB"))
    ts(c("Pa", 256, 512), c("Pa", 0, 256), 0.0, OP.is_gt, col("sg"), OP.mult)
    ts(c("BB"), c("Pb", 0, 256), col("c1"), OP.min, E(3), OP.subtract)
    ts(c("ID"), c("TQ"), 0.0, OP.is_equal)
    tt(lane(0, 3), c("Pa", 256, 512), c("BB"), OP.mult)
    ts(c("D1", p=33), c("KS", p=33), 0.0, OP.is_equal)
    ts(col("g15"), col("G"), 16.0, OP.mult, 15.0, OP.add)
    ts(c("DE", p=16), c("D1", p=16), 2 * HG, OP.mult)
    ts(c("W1"), c("QQ"), col("g15"), OP.is_equal)
    ts(c("DO", p=16), c("D1", p=16), HG, OP.mult)
    J, DJ, DP = c("JW", 48, 64), c("JW", 0, 16), c("JW", 64, 80)

    def probe_constants():
        ts(c("WE"), c("W1"), 2 * HG, OP.mult)
        ts(c("W16"), c("W1"), 65536.0, OP.mult)
        ts(c("WO"), c("W1"), HG, OP.mult)

    def early_constants():
        act(col("da"), E(4), scale=-4.0)
        act(col("d2"), E(1), scale=-1.0, bias=E(2))
        act(col("db"), E(5), scale=-1.0, bias=col("da"))
        act(col("wz"), E(2), scale=-256.0, bias=E(4))
        act(col("d1"), E(6), scale=-1.0, bias=col("db"))
        act(c("O16"), c("TQ"), scale=0.0, bias=1.0)
        act(c("W8"), c("W1"), scale=8192.0)
        for k in range(16):
            out, src = c("BR", 128 * k, 128 * k + 128), c("O16")
            op("g", lambda: g.affine_select(out[0], src[0], [[-16, 8], [0, 16]], OP.is_equal, 0.0, -k, 1), out, src)
        for s in range(3):
            iota(vw("EE", ix[:, 4 * s:4 * s + 4, 0:16 * s + 16]), [[0, 4], [0, 16 * s + 16]], 0, 0)
        for k in range(16):
            out, src = c("TRI", 128 * k, 128 * k + 128), c("W8", 15 - k, 143 - k)
            op("g", lambda: g.affine_select(out[0], src[0], [[1, 128]], OP.is_gt, 0.0, 0, -1), out, src)
        act(J, c("QQ", 0, 16), scale=16.0, bias=col("R"))
        act(col("g3"), col("G"), scale=8.0, bias=7.0)
        act(c("WZ"), c("W1"), scale=col("wz"))
        act(c("ST", 80, 96), J, bias=float(N1))
        lane_offsets(0)
        act(col("nA"), col("A"), scale=-1.0)
        act(col("rb"), col("R8"), scale=-0.125, bias=0.0625)
        act(c("RN"), c("BW"), scale=-0.0625 / 256)
        act(col("b8"), col("AB"), scale=0.125, bias=col("nA"))
        act(c("CT"), c("TQ"), scale=0.0, bias=col("rb"))
        act(col("d8"), col("R8"), scale=-1.0, bias=col("R"))
        act(c("RB"), c("BLK"), scale=col("b8"))
        act(c("SG", 0, 128, 16), c("QQ", 0, 8), scale=0.0, bias=-float(2 ** 60))

    def tail_constants():
        act(col("ini"), col("R8"), scale=32.0, bias=-1.0)
        act(col("c8"), col("d8"), scale=128.0, bias=32.0)
        act(col("wr"), col("d8"), scale=255.875, bias=-1023.0)
        act(col("cap"), col("c8"), bias=col("ini"))
        for k in range(3):
            act(c("JW", 16 * k, 16 * k + 16), J, bias=4096.0)

    def route_constants():
        act(c("CAP"), c("TQ"), scale=0.0, bias=col("cap"))
        act(c("WR"), c("W1"), scale=col("wr"))
        act(DP, J, bias=256.0)
        act(col("o2"), col("R2"), scale=272.0)

    def late_constants():
        ts(c("S2"), c("TQ"), col("d2"), OP.is_equal, col("R"), OP.min)
        ts(c("S1"), c("TQ"), col("d1"), OP.is_equal, col("R"), OP.min)
        ts(c("REP"), c("QQ", 0, 16), 0.0, OP.mult, col("R"), OP.add)


    def lane_offsets(t):
        if t == 0:
            for a, z in ((112, X0), (128, X0), (144, N0)):
                act(c("ST", a, a + 16), J, bias=float(z))
        else:
            act(c("ST", 112, 160), c("J3"), bias=float(base(t, 0)[0]))
        y, st = base(t, 0)
        for a, sg in ((0, 1.0), (16, -1.0), (64, 1.0)):
            act(c("ST", a, a + 16), J, scale=sg * st, bias=sg * y)

    calls = plan(me, core, cores, topo)
    at, on = slot(me, calls), calls[1][-1][1]
    comes = [sum(len(es) for q in range(N) if q != me for cl in plan(q, via(q), cores, topo) for d, es in cl if d == me)
             for via in (lambda q: helper(q, cores, topo), lambda q: cores[q])]
    K3, E3, O3 = rows("PK", 0, 16), rows("PE", 0, 16), rows("PO", 0, 16)

    def write(t, order):
        for n, b in order:
            o = {"FW": 1, "VW": 2, "GW": 0}[n]
            cp(ind(c(n, 0, 4352), c("CU", 4 * b, 4 * b + 4)), lane(t, o, 64 * b, 64 * b + 64))

    for t in range(RO):
        last = t == RO - 1
        NM = lane(t, 3)
        for k in range(16):
            mm(c("Pa", k, 128, 16, 16), lane(t, 1, k, 256, 16), c("AB8", 0, 8))
        for k in range(16):
            mm(c("Pb", k, 128, 16, 16), lane(t, 3, k, 256, 16), c("NW", 0, 8))
        for h, bk in enumerate(("PK", "PO")):
            for m in range(4):
                mm(rows(bk, m, 32, 4), c("ID"), lane(t, 1, 128 * h, 128 * h + 128), True, False)
                mm(rows(bk, m, 32, 4), c("BW"), lane(t, 3, 128 * h, 128 * h + 128), False, True)
            act(c("FQ", 512 * h, 512 * h + 512), rows(bk, 0, 32), AF.Relu, bias=-256.0)
        hs = ((0, 64), (64, 128))
        for a, b in hs:
            cp(c("SI", a, b, 1, 16), c("Pa", a, b, 1, 16))
        for a, b in hs:
            ts(c("UI", a, b, 1, 16), c("SI", a, b, 1, 16), 4095, OP.bitwise_and)
        for a, b in hs:
            tt(c("WI", a, b, 1, 16), c("UI", a, b, 1, 16), c("Pb", a, b, 1, 16), OP.mult)
        ts(c("UB", 0, 128, 1, 16), c("UI", 0, 128, 1, 16), 2048.0, OP.subtract)
        mm(E3, c("UB", 0, 128, 1, 33), c("DK", p=33), True, False)
        for a, b in hs:
            ts(c("UI", 128 + a, 128 + b, 1, 16), c("WI", a, b, 1, 16), 5, OP.arith_shift_right, 4095, OP.bitwise_and)
        for a, b in hs:
            ts(c("UB", 128 + a, 128 + b, 1, 16), c("UI", 128 + a, 128 + b, 1, 16), 2048.0, OP.subtract)
        mm(E3, c("UB", 128, 256, 1, 33), c("D1", p=33), False, True)
        for k in range(16):
            mm(c("Pb", 128 + k, 512, 16, 16), lane(t, 3, k, 256, 16), c("NW", 8, 32))

        def spread_v():
            for m in range(4):
                for h in range(2):
                    mm(rows("PV", 32 * h + m, 32 * h + 32, 4), c("ID"), lane(t, 2, 128 * h, 128 * h + 128))
        act(c("FL", 0, 128, 1, 16), c("Pb", 128, 256, 1, 16), bias=-16.5)
        act(c("FL", 128, 256, 1, 16), c("Pb", 256, 384, 1, 16), bias=-3.0)
        if last:
            act(c("FL", 256, 384, 1, 16), c("Pb", 256, 384, 1, 16), scale=2.0 ** -20, bias=-3.0 * 2.0 ** -20)
            for h, bk in enumerate(("PK", "PO")):
                act(c("GW", N1 + 128 * h, N1 + 128 * h + 128), rows(bk, 0, 32, 4), AF.Relu, bias=-256.0)
        if t == 0:
            probe_constants()
            early_constants()
        else:
            write(t - 1, [("GW", 1)])
        ms_ = (ix[:, :, 0:4], ix[:, :, 4:16])
        for s in ms_:
            cp(vw("H0", s), vw("PE", ix[:, 0:16, s[2]]))
        for s in ms_:
            ts(vw("HI", s), vw("H0", s), 4095, OP.bitwise_and)

        def hu(k):
            cp(c("HU", 64 * k, 64 * k + 64), vw("HI", ix[:, :, 4 * k:4 * k + 4]))
        hu(0); hu(1)
        mm(E3, c("FL", 0, 128, 1, 16), c("DE", p=16), True, False)
        mm(O3, c("FL", 128, 256, 1, 16), c("DO", p=16), True, False)
        mm(K3, c("ID"), c("CK"), True, False)
        mm(K3, c("NEG"), c("ONE"), False, False)

        def ch(name, k):
            return c(name, 1024 * k, 1024 * k + 1024)

        def hk(k):
            return c("HU", 64 * k, 64 * k + 64)

        def sums(k, name, bank, wname, close=False):
            to_w(vw(bank, ix[:, 0:16, 4 * k:4 * k + 4]), wname,
                 lambda r: c(name, 1024 * k + r, 1024 * k + 1024, 16), False, close)

        def gv(k):
            act(ch("VG", k), ind(c("VW", 0, 4096), hk(k)))

        def eq(k, close=False):
            tt(ch("EQ", k), ind(c("FW", 0, 4096), hk(k)), c("FQ"), OP.is_equal)
            sums(k, "EQ", "PE", "WE", close)

        def mn(k):
            tt(ch("LO", k), ch("VG", k), rows("PV", 0, 64), OP.min)
            sums(k, "LO", "PK", "W16", k == 3)

        def sg(k):
            act(ch("OV", k), ch("LO", k), AF.Sign, bias=-TAU[t] - 0.5)

        def so(k, close=False):
            sums(k, "OV", "PO", "WO", close)

        def ov(k, close=False):
            ts(ch("OV", k), ch("LO", k), float(TAU[t]), OP.is_gt, 0.5, OP.subtract)
            sums(k, "OV", "PO", "WE", close)

        def names_up():
            to_w(c("Pc", 256, 272), "WZ", lambda k: lane(t, 3, k, 256, 16))
            act(c("FL", 256, 384, 1, 16), c("Pb", 384, 512, 1, 16), scale=-2.0 ** -27, bias=2.0 ** -27)
            mm(c("Pb", 0, 256), c("S1"), NM)
            mm(c("Pb", 256, 512), c("S2"), NM)

        def last_name():
            act(sm(0), c("Pc", 256, 272), AF.Relu, scale=-1.0, bias=-255.0)

        hv = ((0, 128), (128, 256))

        def best(k3, miss, other):
            for a, b in hv:
                tt(c("KK", a, b), rows(k3, a // 16, b // 16), c("KO", a, b), OP.min)
            for a, b in hv:
                scan(c("Pa", a, b), c("SG"), c("KK", a, b), 0.0, OP.add, OP.max)
            for a, b in hv:
                tt(c("Pb", a, b), c("Pa", a, b), c("KK", a, b), OP.subtract)
                if a == 0:
                    ts(sm(1), c("Pa", 15, 256, 16), -1.0, OP.mult, T0 + 409600.0, OP.add)
            for a, b in hv:
                tt(c("BT", a, b), rows("HI", a // 16, b // 16), c("Pb", a, b), OP.subtract)
                if a == 0:
                    miss()
            for a, b in hv:
                scan(c("SS", a, b), c("Pb", a, b), c("BT", a, b), 0.0, OP.min, OP.max)
                if a == 0:
                    other()

        def claim_places(S):
            tt(sm(10), sm(9), DJ, OP.min)
            tt(c("LT4", 48, 64), sm(10), S, OP.max)
            ts(c("PL16"), c("LT4", 48, 64), 4096.0, OP.min, 2048.0, OP.subtract)

        def claim_rows():
            for k in range(16):
                mm(c("Pb", k, 256, 16), c("BR", 128 * k, 128 * k + 128), c("PL16"))

        def pair(cc):
            a, s = 16 * cc + 16, cc % 4
            return c("PN", a, a + 48 - 16 * s), ix[:, 4 * s + cc // 4, 16 * s + 16:64], c("SM", 192 + cc, 193 + cc)

        def pairs_a(ss):
            for s in ss:
                for b in range(4):
                    pn, at, pl = pair(4 * b + s)
                    act(vw("DF", at), pn, AF.Abs, bias=pl, scale=-1.0)
            for s in ss:
                at = ix[:, 4 * s:4 * s + 4, 16 * s + 16:64]
                act(vw("EE", at), vw("DF", at), AF.Relu, bias=8192.0, scale=-8192.0)

        def pairs_v(cs):
            for cc in cs:
                pn, at, pl = pair(cc)
                ts(vw("EE", at), pn, pl, OP.is_equal, 8192.0, OP.mult)

        def claim_same():
            tt(c("ES"), ind(sm(12), c("DIV")), c("PN"), OP.is_equal)
            mm(c("Pb", 256, 304), c("ID"), c("ZR"), True, False)
            for k in range(16):
                mm(c("Pb", 256, 272), c("TRI", 128 * k, 128 * k + 128), c("ES", k, 256, 16), False, False)

        def claim_sum():
            to_w(c("Pb", 256, 304), "W1", lambda r: vw("EE", ix[:, :, r:64:16]), False, True)

        def claim_lost():
            tt(c("LT4", 0, 48), c("Pb", 256, 304), c("JW", 0, 48), OP.min)

        def claim_writes(between=lambda: None):
            tt(c("LT2"), c("LT4", 0, 32), c("LT4", 32, 64), OP.max)
            between()
            tt(sm(13), c("LT2", 0, 16), c("LT2", 16, 32), OP.max)
            cp(c("CU"), sm(13))

        def zsum(n, out, a=0, b=32):
            for k in range(a, b):
                mm(out, c("ID"), c(n, 128 * k, 128 * k + 128), k == 0, k == 31)

        def zout(src, z, out, sem):
            act(c(z), src)
            store("s", sem, out[:], c(z))

        if last:
            mm(c("Pa", 0, 256), c("ID"), c("CK"), True, False)
            mm(c("Pa", 0, 256), c("FL", 256, 384, 1, 16), c("DO", p=16), False, True)
            to_w(c("Pc", 256, 272), "WZ", lambda k: lane(t, 3, k, 256, 16))
            gv(0); eq(0); hu(2); hu(3); gv(1); gv(2); gv(3)
            tt(c("BT"), rows("HI", 0, 16), c("Pa", 0, 256), OP.add)
            eq(1); eq(2); spread_v(); eq(3, True)
            mn(0); sg(0)
            for a, b in hv:
                tt(c("KK", a, b), rows("PE", a // 16, b // 16), c("BT", a, b), OP.min)
            for a, b in hv:
                scan(c("SS", a, b), c("SG"), c("KK", a, b), 0.0, OP.add, OP.max)
            ts(c("OO", 16, 32), c("Pc", 256, 272), 0.0, OP.is_lt, 16.0, OP.mult)
            ts(c("CI"), c("SS", 15, 256, 16), -8192.0, OP.max)
            ts(sm(9), c("SS", 15, 256, 16), -1.0, OP.mult)
            ts(c("ST", 128, 144), c("OO", 16, 32), float(VZ), OP.add)
            ts(c("RI", 0, 16), c("CI"), 4095, OP.bitwise_and)
            claim_places(c("RI", 0, 16))
            act(sm(12), c("PL16"))
            claim_rows()
            act(c("PN"), c("Pb", 0, 256))
            write(t - 1, [("GW", 0)])
            pairs_a((1, 2))
            mn(1); so(0); sg(1)
            claim_same()
            pairs_v((0, 4, 8, 12))
            tt(ch("LO", 2), ch("VG", 2), rows("PV", 0, 64), OP.min)
            claim_sum()
            sums(2, "LO", "PK", "W16")
            sg(2); so(1)

            def quarter(b):
                a = 3072 + 256 * b
                tt(c("LO", a, a + 256), c("VG", a, a + 256), rows("PV", 16 * b, 16 * b + 16), OP.min)
            quarter(0); quarter(1); claim_lost(); quarter(2)
            claim_writes(lambda: quarter(3))
            sums(3, "LO", "PK", "W16", True)
            sg(3)
            zf, zv, zg = c("Pc", 0, 128), rows("PV", 32, 40), rows("PV", 0, 8)
            so(2); so(3, True)
            act(c("KS"), K3)
            write(t, [("FW", b) for b in (3, 2, 1, 0)])
            zsum("FW", zf)
            zout(zf, "ZF", T.zf, "o2")
            write(t, [(n, b) for b in (3, 2, 1, 0) for n in ("GW", "VW")])
            zsum("GW", zg)
            zsum("VW", zv)
            tt(c("KO"), O3, c("KS"), OP.min)
            best("PE", lambda: tt(c("OO", 64, 80), sm(1), c("ST", 112, 128), OP.min),
                 lambda: tt(c("OO", 80, 96), sm(1), c("ST", 128, 144), OP.min))
            zout(zg, "ZG", T.zg, "o4")
            for a in (0, 16):
                tt(c("OO", a, a + 16), c("SS", 15, 256, 16), c("OO", 64 + a, 80 + a), OP.max)
            for a in (0, 16):
                cp(c("OU", a, a + 16), c("OO", a, a + 16))
            act(c("YF"), ind(c("GW", 0, N2), c("OU", 0, 16)))
            tt(c("YV"), ind(c("VW"), c("OU", 16, 32)), lane(t, 2), OP.min)
            store("a", "o1", T.yf[:], c("YF"))
            store("s", "o0", T.yv[:], c("YV"))
            zout(zv, "ZV", T.zv, "o3")
            break

        if t == 0:
            eq(0); hu(2); hu(3); late_constants(); names_up()
            gv(0); gv(1); gv(2); gv(3)
            eq(1); spread_v(); eq(2); mn(0); sg(0); eq(3, True); mn(1); mn(2); sg(2); ov(1); so(0); mn(3)
            act(c("KS"), E3)
            ov(3); so(2, True); last_name()
            first, second = "PK", "PO"
        else:
            gv(0); names_up(); eq(0); hu(2); hu(3); gv(1); gv(2); gv(3)
            eq(1); spread_v(); eq(2); mn(0); sg(0); mn(1); sg(1); mn(2); so(0); sg(2); mn(3); so(1)
            last_name(); sg(3); so(2); eq(3, True); so(3, True)
            cp(c("KS"), K3)
            write(t - 1, [("GW", 0)])
            first, second = "PE", "PO"
        act(c("GW", N1, N1 + 256), c("Pb", 0, 256))
        act(c("GW", N2, N2 + 256), c("Pb", 256, 512))
        tt(c("ZP"), ind(sm(0), c("REP", 0, 3)), c("ST", 0, 48), OP.mult)
        tt(c("KO"), rows(first, 0, 16), c("KS"), OP.min)
        tt(c("PP", 16, 64), c("ZP"), c("ST", 48, 96), OP.add)
        zs = (c("Pc", 0, 128), rows(first, 0, 8))
        for h, (a, b) in enumerate(hv):
            mm(zs[h], c("ID"), c("CT"), True, False)
            mm(zs[h], c("RN"), lane(t, 3, a, b), False, False)
        if t == 0:
            ts(c("WK"), c("QK"), col("g3"), OP.is_equal, E(0), OP.mult)
            tail_constants()
        best(second, lambda: tt(c("OO", 64, 128), ind(sm(1), c("REP", 0, 4)), c("ST", 96, 160), OP.min),
             lambda: tt(c("OO", 64, 128), c("OO", 64, 128), c("PP"), OP.max))
        act(sm(8), sm(1), AF.Abs, bias=-376832.0)
        act(sm(9), sm(8), AF.Relu, bias=-40000.0)
        if t == 0:
            route_constants()
        S = c("SS", 15, 256, 16)
        tt(sm(10), sm(9), DJ, OP.min)
        tt(c("OO", 16, 32), S, c("OO", 80, 96), OP.max)
        tt(c("OO", 0, 16), S, c("OO", 64, 80), OP.max)
        tt(c("LT4", 48, 64), sm(10), S, OP.max)
        cp(c("OU", 16, 32), c("OO", 16, 32))
        cp(c("OU", 0, 16), c("OO", 0, 16))
        gw = c("GW", 0, LB + 1024 * t)
        for h, (a, b) in enumerate(hv):
            (cp, act)[h](c("N4", 544 + a, 544 + b), ind(gw, c("OU", 16 + 8 * h, 24 + 8 * h)))
            mm(zs[h], c("RB"), c("N4", 544 + a, 544 + b), False, True)
        ts(c("PL16"), c("LT4", 48, 64), 4096.0, OP.min, 2048.0, OP.subtract)
        tt(c("OO", 32, 48), S, c("OO", 96, 112), OP.max)
        cp(c("OU", 48, 64), c("OO", 112, 128))
        cp(c("OU", 32, 48), c("OO", 32, 48))
        claim_rows()
        act(sm(12), c("PL16"))
        act(c("YV"), ind(c("VW"), c("OU", 0, 16)))
        act(c("PN"), c("Pb", 0, 256))
        act(c("N4", 816, 1072), ind(gw, c("OU", 48, 64)))
        act(c("N4", 0, 256), ind(gw, c("OU", 32, 48)))
        pairs_a((1, 2))
        Y = vw(second, ix[:, 16, :])
        mm(Y, c("FL", 256, 384, 1, 16), c("DO", 0, 256, 16, 16), True, False)
        for h, (a, b) in enumerate(hv):
            cp(c("RI", a, b), zs[h])
        for h, (a, b) in enumerate(hv):
            tt(c("OHD", a, b), zs[h], c("RI", a, b), OP.is_equal)
        scan(c("Pa", 256, 384), c("OHD", 0, 128), c("CAP"), col("ini"), OP.add, OP.min)
        scan(c("Pa", 384, 512), c("OHD", 128, 256), c("CAP"), c("Pa", 383, 384), OP.add, OP.min)
        for a, b in hv:
            tt(c("XP", a, b), c("OHD", a, b), c("Pa", 256 + a, 256 + b), OP.mult)
        to_w(Y, "WR", lambda r: c("XP", r, 256, 16), False, True)
        if t == 0:
            cp(c("DIV"), c("QQ", 0, 16))
        tt(c("N4", 272, 528), c("YV"), rows("PV", 0, 64, 4), OP.min)
        claim_same()
        inv, snd, lnd = "inv%d" % (t + 1), "send%d" % (t + 1), LB + 1024 * t
        tt(sm(2), Y, DP, OP.min)
        pairs_v((0,))
        cp(c("PU"), sm(2))
        pairs_v((4,))
        cp(ind(c(inv), c("PU")), c("JN"))
        for k in range(8):
            mm(rows("PK", 0, 2), c("WK", 14 - 2 * k, 142 - 2 * k), c(inv, k, 256, 8), k == 0, k == 7)
        pairs_v((8, 12))
        claim_sum()
        ts(c("IU"), rows("PK", 0, 2), col("o2"), OP.add)
        for part in (1, 0):
            z, arr = 512 * part, "arr%d%d" % (t + 1, part)
            mine = c("GW", lnd + z + 64 * me, lnd + z + 64 * me + 64)

            def pack(fn, d0, d1):
                out = mine if d0 == me else c(snd, z + at[d0], z + at[d0] + 64 * (d1 - d0))
                fn(out, ind(c("N4", 544 * part, 544 * part + 544), c("IU", 4 * d0, 4 * d1)))

            for cl in calls:
                ds = sorted(d for d, es in cl)
                if len(ds) == 4:
                    pack(cp, ds[0], ds[0] + 2); pack(act, ds[2], ds[2] + 2)
                else:
                    far, near = sorted(d for d, es in cl[:-1]), cl[-1][0]
                    pack(cp, far[0], far[-1] + 1); pack(act, near, near + 1)
                if part:
                    need("g", sum((c(snd, z + at[d], z + at[d] + 64)[1] for d in ds), []), [])
                    fused(g, T, topo, cores, cl, lambda d: c(snd, z + at[d], z + at[d] + 64)[0], mine[0], T.sem[arr])
            if not part:
                rest = c(snd, 0, 64 * (N - 1))
                need("g", rest[1], [])
                rid, pid = topo.addr(helper(me, cores, topo))[0:2]
                g.remote_dma(rest[0], rest[0], T.sem["hop%d" % (t + 1)], T.sem.sent, pid, rid, sum(1 << e for e in on))
            pack(act, me, me + 1)
            for q in range(N):
                if q != me:
                    note((arr, comes[part], "d"), [], c("GW", lnd + z + 64 * q, lnd + z + 64 * q + 64)[1])
            if part:
                claim_lost()
        claim_writes()
        write(t, [(n, b) for b in (3, 2, 1, 0) for n in ("VW", "FW", "GW") if (n, b // 2) != ("GW", 0)])
        if t == 0:
            for k, o in enumerate((512, 0, 513)):
                act(c("J3", 16 * k, 16 * k + 16), J, scale=2.0, bias=float(o))
        if t < RO - 2:
            fill("inv%d" % (t + 2), 0, 256, 256)
            lane_offsets(t + 1)
        else:
            act(c("ST", 112, 128), J, bias=float(N1))

    g.wait_ge(T.sem.sent, (RO - 1) * (len(on) + sum(len(es) for cl in calls for d, es in cl)))
    for e in "vapg":
        g.wait_ge(T.sem["s" + e], cnt[e])
    for s in ("o0", "o1", "o2", "o3", "o4"):
        g.wait_ge(T.sem[s], 16)
